import numpy as np, ml_dtypes
CORES = [16,18,20,22]
N = 4
BF = ml_dtypes.bfloat16
def gentries(a):
    return np.ascontiguousarray(a.reshape(8, 16, -1).transpose(0, 2, 1)).reshape(8, -1)
def gtable(e):
    e = np.asarray(e); return np.ascontiguousarray(e.reshape(8, -1, 16).transpose(0, 2, 1)).reshape(128, -1).astype(np.int32)
XI, M, E, L, S, RO, D = 4096, 2048, 2048, 1024, 256, 3, 5
LB = 11
def forest(rng):
    o = np.argsort(rng.random((N, 8, M)), axis=-1); k = np.arange(M)
    inner = (2 * k + 2 < M) & (rng.random((N, 8, M)) >= 0.12); sw = rng.integers(0, 2, (N, 8, M))
    k0 = np.zeros_like(o); k1 = np.zeros_like(o)
    np.put_along_axis(k0, o, np.take_along_axis(o, np.where(inner, 2 * k + 1 + sw, k), 2), 2)
    np.put_along_axis(k1, o, np.take_along_axis(o, np.where(inner, 2 * k + 2 - sw, k), 2), 2)
    return o, k0, k1
def begin(rng, o, lo, hi):
    lv = rng.integers(lo, hi, (N, 8, L))
    return np.take_along_axis(o, 2 ** lv - 1 + (rng.random((N, 8, L)) * 2 ** lv).astype(np.int64), 2)
def vals(rng, n):
    return rng.integers(0, 256, (N, 8, 16, n))
def parts(rng):
    o, k0, k1 = forest(rng)
    return dict(o=o, x=vals(rng, XI), prev=rng.integers(0, XI, (N, 8, XI)), z=vals(rng, M), rs=vals(rng, M), kid0=k0, kid1=k1, env=vals(rng, E),
                start=begin(rng, o, LB - 3 - D, LB - 1), cur=rng.integers(0, XI, (N, 8, L)), w=rng.integers(1, 128, (N, 8, 16)), th=rng.integers(1000, 1500, (N, 8, 1)))
def pack(d):
    r = {}
    for k in ("x", "prev", "z", "rs", "kid0", "kid1", "env", "start", "cur", "w", "th"):
        if k in ("x", "z", "rs", "env"): r[k] = np.ascontiguousarray(d[k].reshape(N, 128, -1)).astype(np.float32).astype(BF)
        elif k in ("start", "cur"): r[k] = np.stack([gtable(a) for a in d[k]])
        elif k == "w": r[k] = d[k].reshape(N, 128, 1).astype(np.int32)
        else: r[k] = np.ascontiguousarray(d[k]).astype(np.int32)
    return r
def setup_inputs(rng):
    return pack(parts(rng))
def setup_inputs_full(rng):
    d = parts(rng)
    d["start"][:, ::2, :S] = d["o"][:, ::2, M // 2:M // 2 + S]; d["th"][:, ::2] = 0
    d["start"][::2, :, :S] = d["o"][::2, :, M // 2:M // 2 + S]; d["th"][::2] = 0
    return pack(d)
def setup_inputs_ties(rng):
    d = parts(rng)
    for k in ("x", "z", "rs", "env"): d[k] = d[k] // 64 * 64
    d["th"] = 64 * rng.integers(18, 22, (N, 8, 1))
    return pack(d)
def setup_inputs_alike(rng):
    d = parts(rng); m = np.arange(M)
    d["start"][:, 0] = d["o"][:, 0, M - 1:M]; d["th"][:, 0] = 0
    d["start"][:, 1] = rng.choice(np.array([0, M - 1]), (N, L)); d["cur"][:, 1] = rng.choice(np.array([0, XI - 1]), (N, L))
    d["prev"][:, 1] = np.where(rng.random((N, XI)) < 0.5, np.arange(XI), rng.choice(np.array([0, XI - 1]), (N, XI)))
    d["kid0"][:, 2] = (m + 1) & (M - 1); d["kid1"][:, 2] = (m + 1 + rng.integers(0, M - 1, (N, M))) & (M - 1)
    d["kid0"][:, 3] = m; d["kid1"][:, 3] = m
    d["start"][:, 3] = np.take_along_axis(rng.integers(0, M, (N, 40)), rng.integers(0, 40, (N, L)), 1)
    d["w"][:, 4] = 0; d["th"][:, 4] = 4096
    d["z"][:, 5] = 0; d["rs"][:, 5] = rng.choice(np.array([0, 255]), (N, 16, M))
    d["kid1"][:, 6] = d["kid0"][:, 6]; d["prev"][:, 6] = np.arange(XI)
    d["x"][:, 7] = 255; d["env"][:, 7] = 255; d["w"][:, 7] = 127; d["th"][:, 7] = 0
    return pack(d)
def setup_inputs_edges(rng):
    d = parts(rng); r = np.arange(N)[:, None]
    d["start"][:, :2, :S] = d["o"][:, :2, M // 2:M // 2 + S]; d["env"][:, :2] = 0
    c = rng.integers(0, 256, (16, 1)); d["x"][:, 0] = c
    d["rs"][:, 0] = np.where(rng.random((N, 1, M)) < 0.5, c, d["rs"][:, 0]); d["th"][:, 0] = r & 1
    c = 255 * rng.integers(0, 2, (16, 1)); d["x"][:, 1] = c
    d["rs"][:, 1] = 255 - c; d["rs"][:, 1, 0] = np.abs(255 - c[0] - rng.integers(0, 3, (N, M)))
    d["th"][:, 1] = np.array([4080, 4081, 4096, 4079])[r & 3]
    d["x"][:, 2:4] = rng.integers(250, 256, (N, 2, 16, XI)); d["w"][:, 2:4] = 127; d["env"][:, 3] = 0
    d["th"][:, 3] = rng.integers(2040, 2060, (N, 1))
    d["kid1"][:, 4] = np.where(rng.random((N, M)) < 0.5, d["kid0"][:, 4], d["kid1"][:, 4])
    return pack(d)
def setup_inputs_spread(rng):
    d = parts(rng); m = np.arange(M); lf = rng.random((N, 4, M)) < 0.5
    for k in ("kid0", "kid1"): d[k][:, 1::2] = np.where(lf, m, (m + rng.integers(1, M, (N, 4, M))) & (M - 1))
    for k, n in (("x", XI), ("z", M), ("rs", M), ("env", E)):
        d[k] = np.minimum((np.exp2(8 * rng.random((N, 8, 1, n))) * rng.random((N, 8, 16, n))).astype(np.int64), 255)
    d["w"] = np.minimum(np.exp2(7 * rng.random((N, 8, 16))).astype(np.int64), 127)
    d["th"] = np.minimum(np.exp2(12 * rng.random((N, 8, 1))).astype(np.int64), 4096); d["th"][:, 0] = 1; d["th"][:, 1] = 0
    d["start"] = begin(rng, d["o"], 0, LB)
    d["cur"] = np.minimum((XI * rng.random((N, 8, L)) ** 3).astype(np.int64), XI - 1)
    d["prev"] = np.where(rng.random((N, 8, XI)) < 0.5, np.maximum(np.arange(XI) - rng.integers(0, 40, (N, 8, XI)), 0), d["prev"])
    return pack(d)
def check_inputs(d):
    bad = []
    for k, lo, hi in (("x", 0, 255), ("prev", 0, XI - 1), ("z", 0, 255), ("rs", 0, 255), ("kid0", 0, M - 1), ("kid1", 0, M - 1), ("env", 0, 255), ("start", 0, M - 1), ("cur", 0, XI - 1), ("w", 0, 127), ("th", 0, 4096)):
        a = np.asarray(d[k]).astype(np.float32)
        if not np.all((a >= lo) & (a <= hi) & (a == np.floor(a))): bad.append("range of " + k)
    m = np.arange(M)
    if np.any((np.asarray(d["kid0"]) == m) != (np.asarray(d["kid1"]) == m)): bad.append("one kid of a node is the node itself, the other isn't")
    return bad
def pick(a, ix):
    return np.take_along_axis(a, ix[:, :, None, :], 3)
def reference(x, prev, z, rs, kid0, kid1, env, start, cur, w, th):
    def cols(a, more):
        b = a.astype(np.float32).astype(np.int32).reshape(N, 8, 16, -1)
        return np.concatenate([b, np.zeros((N, 8, 16, more), np.int32)], axis=3)
    X = cols(x, RO * L); Z = cols(z, 2 * S * RO); R = cols(rs, 2 * S * RO); EN = cols(env, 0)
    P = np.concatenate([prev.astype(np.int64), np.zeros((N, 8, RO * L), np.int64)], axis=2)
    own = np.zeros((N, 8, 1), np.int64) + np.arange(M, M + 2 * S * RO)
    K0 = np.concatenate([kid0.astype(np.int64), own], axis=2); K1 = np.concatenate([kid1.astype(np.int64), own], axis=2)
    F0 = np.stack([gentries(a) for a in start]).astype(np.int64); C = np.stack([gentries(a) for a in cur]).astype(np.int64)
    W = w.reshape(N, 8, 16, 1).astype(np.int32); TH = th.reshape(N, 8, 1).astype(np.int64)
    lower = np.arange(S)[None, :] < np.arange(S)[:, None]
    for t in range(RO):
        f = F0; s = C
        for step in range(D):
            k0 = np.take_along_axis(K0, f, 2); k1 = np.take_along_axis(K1, f, 2); go = k0 != f
            b = np.sum(pick(X, s) >= pick(Z, f), axis=2) >= 9
            f = np.where(go, np.where(b, k1, k0), f); s = np.where(go, np.take_along_axis(P, s, 2), s)
        xc = pick(X, C); rf = pick(R, f); a = np.sum(rf > xc, axis=2)
        y = pick(EN, (np.sum(W * xc, axis=2) + 97 * a) & (E - 1)); v = (xc + y) & 255
        fs = f[:, :, :S]; leaf = np.take_along_axis(K0, fs, 2) == fs
        first = ~np.any((fs[:, :, :, None] == fs[:, :, None, :]) & lower, axis=3)
        far = np.sum(np.abs(rf[..., :S] - v[..., :S]), axis=2) >= TH
        q, g, i = np.nonzero(leaf & first & far); at = fs[q, g, i]; n0 = M + 2 * S * t + 2 * i; xs = pick(X, s[:, :, :S])
        Z[q, g, :, at] = xs[q, g, :, i]; K0[q, g, at] = n0; K1[q, g, at] = n0 + 1
        R[q, g, :, n0] = rf[q, g, :, i]; R[q, g, :, n0 + 1] = (rf[q, g, :, i] + v[q, g, :, i]) >> 1
        came = np.roll(v, 1, axis=0)
        h = np.sum(W * came, axis=2) & (L - 1); lo = XI + L * t
        X[..., lo:lo + L] = came; P[..., lo:lo + L] = np.take_along_axis(C, h, 2)
        C = np.zeros((N, 8, 1), np.int64) + np.arange(lo, lo + L)
    return {"yk0": K0.astype(np.float32), "yk1": K1.astype(np.float32), "yr": np.ascontiguousarray(R[..., M:].reshape(N, 128, 2 * S * RO)).astype(np.float32).astype(BF), "yp": np.ascontiguousarray(P[..., XI:]).astype(np.float32)}

@@ -1,0 +1,599 @@
+import math
+from concourse.mybir import dt, AluOpType, AxisListType, ActivationFunctionType
+
+A = AluOpType
+AF = ActivationFunctionType
+NE = 4
+NS0 = (64, 320, 320, 1024)
+NS1 = 800
+NXP = 5 * 1024 + 256
+SCRATCH = {}
+
+
+def _sb(dtype, text):
+    for w in text.split():
+        n, c = w.split(":")
+        SCRATCH[n] = ("sbuf", [128, int(c)], dtype)
+
+
+_sb("bfloat16", "xs:4096 Pt:4096 Kt:4096 Zt:4096 Rt:3584 Et:2048 Ct:1024 XA:5376 XB:5376 XC:5376 XF:1024 VV:3072 Pg:1024 Kg:1024 "
+    "bt:1024 tm:1024 mm:1024 K5:256 Rg:256 aB:256 E:4096 qB:256 flB:256 winB:256 tK:256 xf:256 depB:256 NDa:256 NDc:256 "
+    "NDe:256 NDt:768 ones:144 zer:144 Q01:144 QP:144 QW:144 Q97:144 Q48:144 QS:144 Q1k:144 QKK:144 BD:128 BDs:128 BDf2:128 "
+    "BDf1:128 idB:128 idN:128 idH:128 idS:128 idMn:128 DM:512 WK:16 dg:640 pg:512 cg:128 sfl:256 sfh:256 sfi:256")
+_sb("float32", "onesF:128 idF:128 BDF:128 bs:128 ts:128 F:128 w16:16 hsS:64 thrR:256 thx:256 laneL:16 dumpL:16 fd:16 fo:16 fp:16 "
+    "dO:16 col:16 thF:1 ypF:192 ykA:224 ykB:224 hF:64")
+_sb("int32", "prevI:256 k0I:128 k1I:128 curI:64 startI:64 wI:1 thI:1 pI:1 pmI:1 pnI:1 ownI:128 own2:128 ti:1024 tc:128 ix0:64 "
+    "iy0:64 yA:224 yB:224 yC:224 hI:64 hJ:64 hK:64 hM:64 hN:64 yI:64 yJ:64 avI:256")
+_sb("uint16", "f0:64 fl:64 sl:384 hl:64 hp:64 el:64 fru:256 offU:16 depU:16")
+for _i in range(8):
+    SCRATCH["pb%d" % _i] = ("psum", [128, 512], "float32")
+
+NDMA = 40
+SEMAPHORES = ["sV", "sS", "sP", "sG", "loc"] + ["d%d" % i for i in range(NDMA)] + ["a%d%d" % (t, c) for t in range(3) for c in range(2)]
+
+
+def rank_program(g, core, T, topo):
+    rank = T.rank_of(core)
+    if rank is None:
+        return
+    dst = T.cores[(rank + 1) % len(T.cores)]
+    src = T.cores[(rank - 1) % len(T.cores)]
+
+    def pairs(a, b):
+        return topo.engines(a, b)[::2]
+
+    QUEUE = {"V": g.vector, "S": g.scalar, "P": g.tensor, "G": g, "D": g.sync}
+    SEM = {"V": "sV", "S": "sS", "P": "sP", "G": "sG"}
+    total = {}
+    seen = {}
+    recs = {}
+    ndma = [0]
+
+    def norm(r):
+        b = r[0]
+        if b.startswith("pb"):
+            return (b, 0, 512, None)
+        if len(r) == 1:
+            return (b, 0, SCRATCH[b][1][1], None)
+        if len(r) == 3:
+            return (b, r[1], r[2], None)
+        return r
+
+    def deps(q, isdma, reads, writes):
+        need = {}
+        for rs, w in ((reads, False), (writes, True)):
+            for r in rs:
+                b, lo, hi, tag = norm(r)
+                ps = b.startswith("pb")
+                for rec in recs.get(b, []):
+                    if rec[2] <= lo or rec[1] >= hi:
+                        continue
+                    if tag is not None and rec[3] is not None and tag != rec[3]:
+                        continue
+                    if not ps and not w and not rec[0]:
+                        continue
+                    if rec[6] == q and not isdma:
+                        if ps or w:
+                            continue
+                    need[rec[4]] = max(need.get(rec[4], 0), rec[5])
+        for s in need:
+            if seen.get((q, s), 0) < need[s]:
+                QUEUE[q].wait_ge(T.sem[s], need[s])
+                seen[(q, s)] = need[s]
+
+    def note(q, reads, writes, sem, val):
+        for r in reads:
+            b, lo, hi, tag = norm(r)
+            w = b.startswith("pb")
+            if w:
+                recs[b] = []
+            lst = recs.setdefault(b, [])
+            recs[b] = [x for x in lst if not ((not x[0]) and x[4] == sem and x[1] >= lo and x[2] <= hi and x[3] == tag)]
+            recs[b].append([w, lo, hi, tag, sem, val, q])
+        for r in writes:
+            b, lo, hi, tag = norm(r)
+            lst = recs.setdefault(b, [])
+            recs[b] = [x for x in lst if not (x[1] >= lo and x[2] <= hi and (tag is None or x[3] == tag))]
+            recs[b].append([True, lo, hi, tag, sem, val, q])
+
+    def op(q, calls, reads, writes):
+        deps(q, False, reads, writes)
+        s = SEM[q]
+        if not isinstance(calls, list):
+            calls = [calls]
+        for c in calls:
+            c().then_inc(T.sem[s], 1)
+            total[s] = total.get(s, 0) + 1
+        note(q, reads, writes, s, total[s])
+
+    def dma(q, out, in_, reads, writes):
+        deps(q, True, reads, writes)
+        s = "d%d" % ndma[0]
+        ndma[0] += 1
+        QUEUE[q].dma_start(out, in_).then_inc(T.sem[s], 16)
+        total[s] = 16
+        note(q + "dma", reads, writes, s, 16)
+
+    V = g.vector
+
+    def cp(out, in_, rd, wr):
+        op("V", lambda: V.tensor_copy(out=out, in_=in_), rd, wr)
+
+    def tt(out, a, b, o, rd, wr):
+        op("V", lambda: V.tensor_tensor(out=out, in0=a, in1=b, op=o), rd, wr)
+
+    def ts(out, a, s1, o1, rd, wr, s2=None, o2=None):
+        if o2 is None:
+            op("V", lambda: V.tensor_scalar(out=out, in0=a, scalar1=s1, scalar2=None, op0=o1), rd, wr)
+        else:
+            op("V", lambda: V.tensor_scalar(out=out, in0=a, scalar1=s1, scalar2=s2, op0=o1, op1=o2), rd, wr)
+
+    def fill(name, lo, hi, v):
+        op("V", lambda: V.memset(T[name][:, lo:hi], v), [], [(name, lo, hi)])
+
+    def act(out, in_, rd, wr, func=AF.Copy, **kw):
+        op("S", lambda: g.scalar.activation(out=out, in_=in_, func=func, **kw), rd, wr)
+
+    def gather(eng, out, outr, win, winr, lst, lstr):
+        if eng == "S":
+            act(out, win.indirect(lst), [winr, lstr], [outr])
+        else:
+            cp(out, win.indirect(lst), [winr, lstr], [outr])
+
+    def mm(out, l, r, st, sp):
+        return lambda: g.tensor.matmul(out, l, r, st, sp)
+
+    def direct(bank, col, n, Q, data, base, rd):
+        b = T[bank]
+        op("P", [mm(b[:, col:col + n], Q[:, 15 - r:143 - r], data[:, base + r:base + 16 * n:16], r == 0, r == 15)
+                 for r in range(16)], rd, [(bank,)])
+
+    def block(bank, col, n, Q, data, rd):
+        b = T[bank]
+        op("P", [mm(b[:, col:col + n], Q[:, 15 - r:143 - r], data[:, n * r:n * r + n], r == 0, r == 15) for r in range(16)],
+           rd, [(bank,)])
+
+    def iota(name, lo, hi, pattern, base, cm, small):
+        ap = T[name][:, lo:hi]
+        if small:
+            op("G", lambda: g.iota(ap, pattern, base, cm, allow_small_or_imprecise_dtypes=True), [], [(name, lo, hi)])
+        else:
+            op("G", lambda: g.iota(ap, pattern, base, cm), [], [(name, lo, hi)])
+
+    def sel(name, src, pattern, cmp, base, cm, n):
+        op("G", lambda: g.affine_select(T[name][:, 0:n], T[src][:, 0:n], pattern, cmp, 0.0, base, cm), [(src, 0, n)], [(name, 0, n)])
+
+    def put(name, n, pattern, entries, lo=0):
+        for j, (base, v) in enumerate(entries):
+            ap, r = (T.zer[:, 0:n], ("zer",)) if j == 0 else (T[name][:, lo:lo + n], (name, lo, lo + n))
+            op("G", lambda ap=ap, base=base, v=v: g.affine_select(T[name][:, lo:lo + n], ap, pattern, A.not_equal, float(v), base, 1),
+               [r], [(name, lo, lo + n)])
+
+    def putQ(name, entries):
+        put(name, 144, [[-16, 9], [1000, 16]], [(-15000 - i, v) for i, v in entries])
+
+    def putB(name, entries):
+        put(name, 128, [[-16, 8], [0, 16]], [(-i, v) for i, v in entries])
+
+    def putD(name, lo, places, v=1.0):
+        put(name, 128, [[-16, 8], [999, 16]], [(-1000 * i, v) for i in places], lo)
+
+    C = {}
+
+    def column(nm):
+        i = len(C)
+        C[nm] = (T.col[:, i:i + 1], ("col", i, i + 1))
+        return C[nm]
+
+    dma("D", T.prevI[:, :], T.prev[:, :], [], [("prevI",)])
+    dma("D", T.k0I[:, :], T.kid0[:, :], [], [("k0I",)])
+    dma("S", T.curI[:, :], T.cur[:, :], [], [("curI",)])
+    dma("S", T.startI[:, :], T.start[:, :], [], [("startI",)])
+    dma("D", T.k1I[:, :], T.kid1[:, :], [], [("k1I",)])
+    dma("S", T.wI[:, :], T.w[:, :], [], [("wI",)])
+    dma("D", T.xs[:, :], T.x[:, :], [], [("xs",)])
+    dma("S", T.Zt[:, 0:2048], T.z[:, :], [], [("Zt", 0, 2048)])
+
+    iota("pI", 0, 1, [[0, 1]], 0, 1, False)
+    iota("sfl", 0, 256, [[1, 256]], 0, 0, True)
+    iota("ownI", 0, 128, [[1, 128]], 0, 128, False)
+    pm, pmr = column("pm")
+    pe, per = column("pe")
+    fill("ones", 0, 144, 1.0)
+    fill("onesF", 0, 128, 1.0)
+    ts(T.pmI[:, :], T.pI[:, :], 15, A.bitwise_and, [("pI",)], [("pmI",)])
+    ts(T.pnI[:, :], T.pI[:, :], 7, A.bitwise_and, [("pI",)], [("pnI",)])
+    fill("thI", 0, 1, 0)
+    cp(pm, T.pmI[:, :], [("pmI",)], [pmr])
+    ts(pe, T.pnI[:, :], 8.0, A.add, [("pnI",)], [per])
+    fill("Zt", 2048, 4096, 0.0)
+    fill("Kt", 0, 4096, 0.0)
+    fill("zer", 0, 144, 0.0)
+    ZU = ("Zt", 2048, 4096)
+    act(T.sfh[:, :], T.sfl[:, :], [("sfl",), pmr], [("sfh",)], func=AF.Identity, scale=0.0, bias=pm)
+    act(T.sfi[:, :], T.sfl[:, :], [("sfl",), per], [("sfi",)], func=AF.Identity, scale=0.0, bias=pe)
+    act(T.Pt[:, 0:2048], T.Zt[:, 2048:4096], [ZU], [("Pt", 0, 2048)])
+    act(T.Pt[:, 2048:4096], T.Zt[:, 2048:4096], [ZU], [("Pt", 2048, 4096)])
+
+    sel("Q01", "ones", [[0, 9], [1, 16]], A.is_equal, -15, 0, 144)
+    sel("Q01", "Q01", [[-16, 9], [0, 16]], A.is_ge, 0, 1, 144)
+    sel("Q01", "Q01", [[16, 9], [0, 16]], A.is_ge, 15, -1, 144)
+    putQ("QP", [(0, 1), (1, 256)])
+    put("WK", 8, [[-16, 8]], [(0, 1), (-1, 256)], 0)
+    put("WK", 8, [[-16, 8]], [(0, -1), (-1, -256), (-2, 1), (-3, 256)], 8)
+    putB("BDf1", [(6, 1)])
+    sel("idF", "onesF", [[-1, 128]], A.is_equal, 0, 1, 128)
+    sel("BD", "ones", [[-16, 8], [0, 16]], A.is_ge, 0, 1, 128)
+    sel("BD", "BD", [[16, 8], [0, 16]], A.is_ge, 15, -1, 128)
+    iota("laneL", 0, 16, [[16, 16]], 0, 0, True)
+    for nm, v in (("idB", 1.0), ("idN", -1.0), ("idH", 0.5), ("idS", -128.0)):
+        put(nm, 128, [[-1, 128]], [(0, v)])
+    putB("BDs", [(4, 1), (5, 256)])
+    putB("BDf2", [(6, 2)])
+    putQ("Q1k", [(0, 1024)])
+    putQ("QS", [(0, 1)])
+    iota("NDa", 0, 256, [[0, 2], [2, 128]], 0, 0, True)
+    iota("NDc", 0, 256, [[0, 2], [2, 128]], 1, 0, True)
+    iota("NDe", 0, 256, [[0, 256]], 1, 0, True)
+    for t in range(3):
+        iota("NDt", 256 * t, 256 * t + 256, [[1, 2], [0, 128]], 8 + 2 * t, 0, True)
+    putD("DM", 0, (0,))
+    putD("DM", 128, (2,))
+    putD("DM", 256, (1, 3))
+    putD("DM", 384, (6,))
+    putD("idMn", 0, (0, 1, 2, 3, 6), -1.0)
+    putQ("QKK", [(0, 1), (1, 256), (2, 4096), (3, 1048576)])
+
+    def digits(name, n, tmp, to, out, oo):
+        for j, (o, v) in enumerate(((A.bitwise_and, 255), (A.arith_shift_right, 8))):
+            a, b = to + j * n, oo + j * n
+            ts(T[tmp][:, a:a + n], T[name][:, :], v, o, [(name,)], [(tmp, a, a + n)])
+            cp(T[out][:, b:b + n], T[tmp][:, a:a + n], [(tmp, a, a + n)], [(out, b, b + n)])
+
+    cp(T.f0[:, :], T.startI[:, :], [("startI",)], [("f0",)])
+    cp(T.sl[:, 0:64], T.curI[:, :], [("curI",)], [("sl", 0, 64)])
+    digits("prevI", 256, "ti", 512, "pg", 0)
+    dma("D", T.Pt[0:128:16, :], T.pg[:, 0:256], [("pg", 0, 256)], [("Pt", 0, 4096, "r0")])
+    dma("D", T.Pt[1:128:16, :], T.pg[:, 256:512], [("pg", 256, 512)], [("Pt", 0, 4096, "r1")])
+    ts(T.own2[:, :], T.ownI[:, :], 2047, A.bitwise_and, [("ownI",)], [("own2",)])
+    digits("k0I", 128, "ti", 0, "dg", 0)
+    digits("k1I", 128, "ti", 256, "dg", 256)
+    tt(T.dg[:, 512:640], T.k0I[:, :], T.own2[:, :], A.not_equal, [("k0I",), ("own2",)], [("dg", 512, 640)])
+    dma("D", T.Kt[4:128:16, :], T.sfl[:, :], [("sfl",)], [("Kt", 0, 4096, "r4")])
+    dma("D", T.Kt[5:128:16, :], T.sfh[:, :], [("sfh",)], [("Kt", 0, 4096, "r5")])
+    for i in range(4):
+        nm = ("sfl", "sfi")[i % 2]
+        dma("D", T.Kt[i:128:16, 2048:4096], T[nm][0:64, :], [(nm,)], [("Kt", 2048, 4096, "r%d" % i)])
+    for i, j in ((0, 0), (1, 1), (2, 2), (3, 3), (6, 4)):
+        dma("D", T.Kt[i:128:16, 0:2048], T.dg[:, 128 * j:128 * j + 128], [("dg", 128 * j, 128 * j + 128)], [("Kt", 0, 2048, "r%d" % i)])
+    dma("D", T.thI[0:128:16, :], T.th[:, :], [], [("thI",)])
+    dma("D", T.Rt[:, 0:2048], T.rs[:, :], [], [("Rt", 0, 2048)])
+    dma("D", T.Et[:, :], T.env[:, :], [], [("Et",)])
+    wc, wcr = column("w")
+    cp(wc, T.wI[:, :], [("wI",)], [wcr])
+    W1 = T.Q01[:, 15:128:16]
+
+    def scaled(name, c, rd):
+        ts(T[name][:, :], T.Q01[:, :], c, A.mult, [("Q01",)] + rd, [(name,)])
+
+    LN = math.log(1.85)
+
+    def late1():
+        fill("Rt", 2048, 3584, 0.0)
+        fill("Ct", 0, 1024, 0.0)
+        scaled("QW", wc, [wcr])
+
+    def late1b():
+        ts(T.laneL[:, :], T.laneL[:, :], pm, A.add, [("laneL",), pmr], [("laneL",)])
+        scaled("Q97", 97.0, [])
+        scaled("Q48", 48.5, [])
+        ts(T.dumpL[:, :], T.laneL[:, :], 3584.0, A.add, [("laneL",)], [("dumpL",)])
+
+    def late2():
+        act(T.w16[:, :], T.laneL[:, :], [("laneL",)], [("w16",)], func=AF.Exp, scale=-LN, bias=128 * LN)
+        act(T.thrR[:, :], T.sfl[:, :], [("sfl",)], [("thrR",)], func=AF.Exp, scale=-LN, bias=128 * LN + math.log(2.5))
+
+    def late3():
+        cp(T.BDF[:, :], T.BD[:, :], [("BD",)], [("BDF",)])
+        cp(T.thF[:, :], T.thI[:, :], [("thI",)], [("thF",)])
+        op("P", mm(T.pb4[:, 100:101], T.BDF[:, :], T.thF[:, :], True, True), [("BDF",), ("thF",)], [("pb4",)])
+        c, r = column("thm")
+        ts(c, T.pb4[:, 100:101], -1048576.0, A.add, [("pb4",)], [r])
+
+    def late4():
+        digits("curI", 64, "tc", 0, "cg", 0)
+        dma("D", T.Ct[0:128:16, :], T.cg[:, 0:64], [("cg", 0, 64)], [("Ct", 0, 1024, "r0")])
+        dma("D", T.Ct[1:128:16, :], T.cg[:, 64:128], [("cg", 64, 128)], [("Ct", 0, 1024, "r1")])
+
+    XP = ["XA", "XB", "XC", "XF"]
+
+    def nodes(h, k):
+        nm = "f0" if k == 0 else "fl"
+        return T[nm][:, 32 * h:32 * h + 32], (nm, 32 * h, 32 * h + 32)
+
+    def kid(h, k):
+        l, r = nodes(h, k)
+        act(T.Kg[:, 512 * h:512 * h + 512], T.Kt[:, :].indirect(l), [("Kt",), r], [("Kg", 512 * h, 512 * h + 512)])
+
+    def cmpz(t, h, k):
+        l, r = nodes(h, k)
+        a = 1024 * k + 512 * h
+        tt(T.bt[:, 512 * h:512 * h + 512], T.Zt[:, :].indirect(l), T[XP[t]][:, a:a + 512], A.is_le,
+           [("Zt",), r, (XP[t], a, a + 512)], [("bt", 512 * h, 512 * h + 512)])
+
+    def pekids(h):
+        op("P", [mm(T.pb0[32 * h:32 * h + 32, r:256:16], T.Kg[:, 512 * h + r:512 * h + 512:16], T.WK[:, :], True, True) for r in range(16)],
+           [("Kg", 512 * h, 512 * h + 512), ("WK",)], [("pb0",)])
+
+    def pecnt(h):
+        op("P", [mm(T.pb6[32 * h:32 * h + 32, r:128:16], T.bt[:, 512 * h + r:512 * h + 512:16], W1, True, True) for r in range(16)],
+           [("bt", 512 * h, 512 * h + 512), ("Q01",)], [("pb6",)])
+
+    def xg(eng, t, k, a, b):
+        o = 1024 * k
+        out, outr = T[XP[t]][:, o + a:o + b], (XP[t], o + a, o + b)
+        if t == 0:
+            lo, hi = 64 * k + a // 16, 64 * k + b // 16
+            gather(eng, out, outr, T.xs[:, :], ("xs",), T.sl[:, lo:hi], ("sl", lo, hi))
+        else:
+            w = 1024 * (k - 1)
+            gather(eng, out, outr, T[XP[t - 1]][:, w:w + 1024], (XP[t - 1], w, w + 1024), T.hl[:, a // 16:b // 16], ("hl", a // 16, b // 16))
+
+    def pgat(k, n):
+        gather("S", T.Pg[:, 0:n], ("Pg",), T.Pt[:, :], ("Pt",), T.sl[:, 64 * k:64 * k + n // 16], ("sl", 64 * k, 64 * k + n // 16))
+
+    def psum(n):
+        direct("pb2", 0, n // 16, T.QP, T.Pg, 0, [("Pg",), ("QP",)])
+
+    def plist(k, n):
+        cp(T.sl[:, 64 * k:64 * k + n // 16], T.pb2[:, 0:n // 16], [("pb2",)], [("sl", 64 * k, 64 * k + n // 16)])
+
+    def hsum(t, h):
+        direct("pb2", 64 + 32 * h, 32, T.QW, T[XP[t]], 512 * h, [(XP[t], 512 * h, 512 * h + 512), ("QW",)])
+
+    def hlow():
+        ts(T.hsS[:, 0:16], T.pb2[:, 64:80], 776.0, A.add, [("pb2",)], [("hsS", 0, 16)])
+
+    def hhigh():
+        cp(T.hsS[:, 16:64], T.pb2[:, 80:128], [("pb2",)], [("hsS", 16, 64)])
+
+    def hlist():
+        cp(T.hI[:, :], T.pb2[:, 64:128], [("pb2",)], [("hI",)])
+        hlow()
+        ts(T.hJ[:, :], T.hI[:, :], 1023, A.bitwise_and, [("hI",)], [("hJ",)])
+        hhigh()
+        cp(T.hl[:, :], T.hJ[:, :], [("hJ",)], [("hl",)])
+
+    def arrived(t, h):
+        s = "a%d%d" % (t, h)
+        total[s] = len(pairs(src, core))
+        recs.setdefault(XP[t + 1], []).append([True, 512 * h, 512 * h + 512, None, s, total[s], "remote"])
+
+    def send(t, h):
+        a, b = 1024 * t + 512 * h, 1024 * t + 512 * h + 512
+        deps("G", True, [("VV", a, b)], [])
+        en = pairs(core, dst)
+        mask = sum(1 << x for x in en)
+        rid, pid, _ = topo.addr(dst)
+        g.remote_dma(out_ap=T[XP[t + 1]][:, 512 * h:512 * h + 512], in_ap=T.VV[:, a:b], remote_sem=T.sem["a%d%d" % (t, h)],
+                     local_sem=T.sem.loc, pid=pid, routing_id=rid, dma_engine_mask=mask)
+        total["loc"] = total.get("loc", 0) + len(en)
+
+    def out0(t):
+        tt(T.tm[:, 0:512], T.Et[:, :].indirect(T.el[:, 0:32]), T[XP[t]][:, 0:512], A.add,
+           [("Et",), ("el",), (XP[t], 0, 512)], [("tm", 0, 512)])
+        ts(T.mm[:, 0:512], T.tm[:, 0:512], 0.0, A.is_lt, [("tm", 0, 512)], [("mm", 0, 512)], 256.0, A.mult)
+        op("P", [mm(T.pb7[:, :], T.idB[:, :], T.tm[:, 0:512], True, False), mm(T.pb7[:, :], T.idB[:, :], T.mm[:, 0:512], False, True)],
+           [("tm", 0, 512), ("mm", 0, 512), ("idB",)], [("pb7",)])
+
+    def out0c(t):
+        act(T.VV[:, 1024 * t:1024 * t + 512], T.pb7[:, :], [("pb7",)], [("VV", 1024 * t, 1024 * t + 512)])
+        send(t, 0)
+
+    def sums1(t, bank, stop):
+        op("P", [mm(T[bank][:, :], T.idB[:, :], T.tm[:, 512:1024], True, False),
+                 mm(T[bank][:, :], T.idB[:, :], T[XP[t]][:, 512:1024], False, stop)],
+           [("tm", 512, 1024), (XP[t], 512, 1024), ("idB",)], [(bank,)])
+
+    def out1a(t):
+        gather("S", T.tm[:, 512:1024], ("tm", 512, 1024), T.Et[:, :], ("Et",), T.el[:, 32:64], ("el",))
+        sums1(t, "pb3", True)
+
+    def out1b():
+        act(T.mm[:, 512:1024], T.pb3[:, :], [("pb3",)], [("mm", 512, 1024)], func=AF.Sign, bias=0.5)
+
+    def out1c(t):
+        op("P", mm(T.pb0[:, :], T.idS[:, :], T.mm[:, 512:1024], False, True), [("mm", 512, 1024), ("idS",)], [("pb0",)])
+        act(T.VV[:, 1024 * t + 512:1024 * t + 1024], T.pb0[:, :], [("pb0",)], [("VV", 1024 * t + 512, 1024 * t + 1024)], bias=128.0)
+        send(t, 1)
+
+    def eqs(c0, c1):
+        ms = []
+        for c in range(c0, c1):
+            n = 256 - 16 * c
+            ts(T.E[:, 256 * c:256 * c + n], T.fru[:, 16 * c:256], T.pb1[:, c:c + 1], A.is_equal, [("fru",), ("pb1",), ("w16",)],
+               [("E", 256 * c, 256 * c + n)], T.w16[:, c:c + 1], A.mult)
+            ms.append(mm(T.pb5[:, 16 * c:256], T.BD[:, :], T.E[:, 256 * c:256 * c + n], c == 0, c == 15))
+        op("P", ms, [("E", 256 * c0, 256 * c1), ("BD",)], [("pb5",)])
+
+    def rwrites1(t):
+        a = 1024 * t
+        op("P", [mm(T.pb7[:, 0:256], T.idH[:, :], T.Rg[:, :], True, False), mm(T.pb7[:, 0:256], T.idH[:, :], T.VV[:, a:a + 256], False, True)],
+           [("Rg",), ("VV", a, a + 256), ("idH",)], [("pb7",)])
+        n = 2048 + 512 * t
+        tt(T.Rt[:, n:n + 512:2], T.Rg[:, :], T.winB[:, :], A.mult, [("Rg",), ("winB",)], [("Rt", n, n + 512, "even")])
+
+    def rwrites2(t):
+        n = 2048 + 512 * t
+        ts(T.avI[:, :], T.pb7[:, 0:256], -0.25, A.add, [("pb7",)], [("avI",)])
+        tt(T.Rt[:, n + 1:n + 512:2], T.avI[:, :], T.winB[:, :], A.mult, [("avI",), ("winB",)], [("Rt", n, n + 512, "odd")])
+
+    def ypn(t, xn):
+        block("pb2", 128, 64, T.QW, T[xn], [(xn, 0, 1024), ("QW",)])
+        cp(T.yI[:, :], T.pb2[:, 128:192], [("pb2",)], [("yI",)])
+        ts(T.yJ[:, :], T.yI[:, :], 1023, A.bitwise_and, [("yI",)], [("yJ",)])
+        ts(T.ypF[:, 64 * t:64 * t + 64], T.yJ[:, :], float(4096 + 1024 * (t - 1)), A.add, [("yJ",)], [("ypF", 64 * t, 64 * t + 64)])
+        dma("D", T.yp[:, 1024 * t:1024 * t + 1024], T.ypF[:, 64 * t:64 * t + 64], [("ypF", 64 * t, 64 * t + 64)], [])
+
+    def yp0a():
+        ts(T.hK[:, :], T.hJ[:, :], 15, A.bitwise_and, [("hJ",)], [("hK",)])
+        ts(T.hM[:, :], T.hJ[:, :], 4, A.arith_shift_right, [("hJ",)], [("hM",)])
+        ts(T.hN[:, :], T.hK[:, :], 64.0, A.mult, [("hK",)], [("hN",)])
+        tt(T.hF[:, :], T.hN[:, :], T.hM[:, :], A.add, [("hN",), ("hM",)], [("hF",)])
+        cp(T.hp[:, :], T.hF[:, :], [("hF",)], [("hp",)])
+
+    def yp0b(h):
+        gather("S", T.Pg[:, 512 * h:512 * h + 512], ("Pg", 512 * h, 512 * h + 512), T.Ct[:, :], ("Ct",), T.hp[:, 32 * h:32 * h + 32], ("hp",))
+        if h == 1:
+            block("pb2", 192, 64, T.QP, T.Pg, [("Pg",), ("QP",)])
+
+    def yp0c():
+        cp(T.ypF[:, 0:64], T.pb2[:, 192:256], [("pb2",)], [("ypF", 0, 64)])
+        dma("D", T.yp[:, 0:1024], T.ypF[:, 0:64], [("ypF", 0, 64)], [])
+
+    for t in range(3):
+        XT = XP[t]
+        if t == 0:
+            xg("S", 0, 0, 0, 512)
+            pgat(0, 1024)
+            psum(1024)
+            xg("V", 0, 0, 512, 1024)
+        for k in range(5):
+            kid(0, k)
+            cmpz(t, 0, k)
+            pekids(0)
+            op("P", mm(T.pb3[:, 0:256], T.BDf1[:, :], T.Kg[:, 0:256], k == 0, k == 4), [("Kg", 0, 256), ("BDf1",)], [("pb3",)])
+            if t > 0 and k == 0:
+                hsum(t, 0)
+            pecnt(0)
+            if t == 0 and k > 0:
+                plist(k + 1, 1024 if k < 4 else 256)
+            kid(1, k)
+            cmpz(t, 1, k)
+            if t > 0 and k == 0:
+                hsum(t, 1)
+            pecnt(1)
+            pekids(1)
+            if k == 0:
+                if t == 0:
+                    late1()
+                    plist(1, 1024)
+                else:
+                    hlist()
+            if t == 0 and k < 4:
+                pgat(k + 1, 1024 if k < 3 else 256)
+                if NS0[k] < 1024:
+                    xg("V", 0, k + 1, NS0[k], 1024)
+                xg("S", 0, k + 1, 0, NS0[k])
+                if k == 0:
+                    late1b()
+                if k == 1:
+                    late3()
+                if k == 3:
+                    ts(T.Et[:, :], T.Et[:, :], -256.0, A.add, [("Et",)], [("Et",)])
+            elif k < 4:
+                xg("V", t, k + 1, NS1, 1024)
+                xg("S", t, k + 1, 0, NS1)
+            elif t < 2:
+                xg("S", t, 5, 0, 256)
+            if t == 2 and k == 4:
+                yp0b(0)
+            if t == 0 and k == 4:
+                late2()
+            ts(T.bs[0:64, :], T.pb6[0:64, 0:128], 8.5, A.is_ge, [("pb6",)], [("bs",)])
+            tt(T.ts[0:64, :], T.pb0[0:64, 128:256], T.bs[0:64, :], A.mult, [("pb0",), ("bs",)], [("ts",)])
+            tt(T.F[0:64, :], T.pb0[0:64, 0:128], T.ts[0:64, :], A.add, [("pb0",), ("ts",)], [("F",)])
+            op("P", lambda: g.tensor.transpose(T.pb1[:, 0:64], T.F[0:64, :], T.idF[0:64, 0:64]), [("F",), ("idF",)], [("pb1",)])
+            if t == 0 and k < 4:
+                psum(1024 if k < 3 else 256)
+            if t > 0:
+                if t == 1 and k == 4:
+                    late4()
+                if k == 1:
+                    rwrites1(t - 1)
+                if k == 2:
+                    rwrites2(t - 1)
+                if t == 1 and k == 1:
+                    yp0a()
+                if t == 2 and k == 3:
+                    ypn(1, "XC")
+            elif k == 4:
+                hsum(0, 0)
+                hsum(0, 1)
+                hlow()
+                hhigh()
+            cp(T.fl[:, :], T.pb1[:, 0:64], [("pb1",)], [("fl",)])
+        l0, l1 = ("fl", 0, 16), ("fl", 16, 64)
+        gather("S", T.Rg[:, :], ("Rg",), T.Rt[:, :], ("Rt",), T.fl[:, 0:16], l0)
+        tt(T.bt[:, 256:1024], T.Rt[:, :].indirect(T.fl[:, 16:64]), T[XT][:, 256:1024], A.is_gt, [("Rt",), l1, (XT, 256, 1024)], [("bt", 256, 1024)])
+        gather("S", T.K5[:, :], ("K5",), T.Kt[:, :], ("Kt",), T.fl[:, 0:16], l0)
+        op("P", [mm(T.pb7[:, 0:256], T.idB[:, :], T.Rg[:, :], True, False), mm(T.pb7[:, 0:256], T.idN[:, :], T[XT][:, 0:256], False, True)],
+           [("Rg",), (XT, 0, 256), ("idB",), ("idN",)], [("pb7",)])
+        op("P", [mm(T.pb4[:, 0:256], T.BDs[:, :], T.K5[:, :], True, True), mm(T.pb4[:, 256:512], T.BDf2[:, :], T.K5[:, :], True, True)],
+           [("K5",), ("BDs",), ("BDf2",)], [("pb4",)])
+        act(T.bt[:, 0:256], T.pb7[:, 0:256], [("pb7",)], [("bt", 0, 256)], func=AF.Sign, bias=-0.5)
+        direct("pb6", 16, 48, T.Q97, T.bt, 256, [("bt", 256, 1024), ("Q97",)])
+        direct("pb6", 0, 16, T.Q48, T.bt, 0, [("bt", 0, 256), ("Q48",)])
+        if t < 2:
+            act(T.depB[:, :], T.pb3[:, 0:256], [("pb3",)], [("depB",)])
+        cp(T.fru[:, :], T.pb4[:, 0:256], [("pb4",)], [("fru",)])
+        eqs(0, NE)
+        if t < 2:
+            direct("pb2", 0, 16, T.Q1k, T.depB, 0, [("depB",), ("Q1k",)])
+        ms = [mm(T.pb4[:, 0:256], T.DM[:, 0:128], T.NDa[:, :], True, False), mm(T.pb4[:, 0:256], T.DM[:, 128:256], T.NDc[:, :], False, False),
+              mm(T.pb4[:, 0:256], T.DM[:, 256:384], T.NDt[:, 256 * t:256 * t + 256], False, False),
+              mm(T.pb4[:, 0:256], T.DM[:, 384:512], T.NDe[:, :], False, False), mm(T.pb4[:, 0:256], T.idMn[:, :], T.K5[:, :], False, True)]
+        op("P", ms, [("DM",), ("idMn",), ("NDa",), ("NDc",), ("NDe",), ("NDt",), ("K5",)], [("pb4",)])
+        tt(T.ix0[:, :], T.pb6[:, 0:64], T.hsS[:, :], A.add, [("pb6",), ("hsS",)], [("ix0",)])
+        ts(T.iy0[:, :], T.ix0[:, :], 2047, A.bitwise_and, [("ix0",)], [("iy0",)])
+        cp(T.el[:, :], T.iy0[:, :], [("iy0",)], [("el",)])
+        out1a(t)
+        out0(t)
+        eqs(NE, 10)
+        eqs(10, 16)
+        out1b()
+        out0c(t)
+        v0 = ("VV", 1024 * t, 1024 * t + 256)
+        op("P", [mm(T.pb7[:, 0:256], T.idB[:, :], T.Rg[:, :], True, False), mm(T.pb7[:, 0:256], T.idN[:, :], T.VV[:, 1024 * t:1024 * t + 256], False, True)],
+           [("Rg",), v0, ("idB",), ("idN",)], [("pb7",)])
+        act(T.aB[:, :], T.pb7[:, 0:256], [("pb7",)], [("aB",)], func=AF.Abs)
+        sums1(t, "pb0", False)
+        out1c(t)
+        if t < 2:
+            tt(T.dO[:, :], T.pb2[:, 0:16], T.laneL[:, :], A.add, [("pb2",), ("laneL",)], [("dO",)])
+        tt(T.fd[:, :], T.pb1[:, 0:16], T.dumpL[:, :], A.subtract, [("pb1",), ("dumpL",)], [("fd",)])
+        if t < 2:
+            cp(T.depU[:, :], T.dO[:, :], [("dO",)], [("depU",)])
+            gather("S", T.xf[:, :], ("xf",), T[XT][:, 0:NXP], (XT, 0, NXP), T.depU[:, :], ("depU",))
+        tt(T.qB[:, :], T.pb5[:, 0:256], T.thrR[:, :], A.is_ge, [("pb5",), ("thrR",)], [("qB",)])
+        op("P", mm(T.pb5[:, 256:512], T.BD[:, :], T.aB[:, :], True, True), [("aB",), ("BD",)], [("pb5",)])
+        tt(T.flB[:, :], T.pb4[:, 256:512], T.qB[:, :], A.is_equal, [("pb4",), ("qB",)], [("flB",)])
+        direct("pb6", 64, 16, T.QS, T.flB, 0, [("flB",), ("QS",)])
+        ts(T.thx[:, :], T.flB[:, :], C["thm"][0], A.mult, [("flB",), C["thm"][1]], [("thx",)], 1048576.0, A.add)
+        tt(T.winB[:, :], T.pb5[:, 256:512], T.thx[:, :], A.is_ge, [("pb5",), ("thx",)], [("winB",)])
+        tt(T.fo[:, :], T.pb6[:, 64:80], T.fd[:, :], A.mult, [("pb6",), ("fd",)], [("fo",)])
+        tt(T.tK[:, :], T.pb4[:, 0:256], T.winB[:, :], A.mult, [("pb4",), ("winB",)], [("tK",)])
+        tt(T.fp[:, :], T.fo[:, :], T.dumpL[:, :], A.add, [("fo",), ("dumpL",)], [("fp",)])
+        cp(T.offU[:, :], T.fp[:, :], [("fp",)], [("offU",)])
+        tt(T.Kt[:, :].indirect(T.offU[:, :]), T.K5[:, :], T.tK[:, :], A.add, [("K5",), ("tK",), ("offU",)], [("Kt",)])
+        if t < 2:
+            cp(T.Zt[:, :].indirect(T.offU[:, :]), T.xf[:, :], [("xf",), ("offU",)], [("Zt",)])
+        arrived(t, 0)
+        arrived(t, 1)
+    rwrites1(2)
+    rwrites2(2)
+    dma("D", T.yr[:, :], T.Rt[:, 2048:3584], [("Rt", 2048, 3584)], [])
+    ypn(2, "XF")
+    block("pb3", 0, 224, T.QKK, T.Kt, [("Kt",), ("QKK",)])
+    cp(T.yA[:, :], T.pb3[:, 0:224], [("pb3",)], [("yA",)])
+    ts(T.yB[:, :], T.yA[:, :], 4095, A.bitwise_and, [("yA",)], [("yB",)])
+    ts(T.yC[:, :], T.yA[:, :], 12, A.arith_shift_right, [("yA",)], [("yC",)])
+    cp(T.ykA[:, :], T.yB[:, :], [("yB",)], [("ykA",)])
+    cp(T.ykB[:, :], T.yC[:, :], [("yC",)], [("ykB",)])
+    dma("D", T.yk0[:, :], T.ykA[:, :], [("ykA",)], [])
+    dma("D", T.yk1[:, :], T.ykB[:, :], [("ykB",)], [])
+    yp0b(1)
+    yp0c()
+    for s in total:
+        if seen.get(("G", s), 0) < total[s]:
+            g.wait_ge(T.sem[s], total[s])

@@ -1,12 +1,16 @@
 import math
+from concourse.bass import DstId, RemoteDMATransfer
 from concourse.mybir import dt, AluOpType, AxisListType, ActivationFunctionType
 
 A = AluOpType
 AF = ActivationFunctionType
-NE = 4
-NS0 = (64, 320, 320, 1024)
-NS1 = 800
+XS = ((256, 256), (416, 416), (416, 416))
+PS = 1024
+RB_ON_S = (True, True, True)
+EB_ON_S = (True, True, True)
 NXP = 5 * 1024 + 256
+OFF = 1792
+EW = 3600
 SCRATCH = {}
 
 
@@ -16,20 +20,25 @@ def _sb(dtype, text):
         SCRATCH[n] = ("sbuf", [128, int(c)], dtype)
 
 
-_sb("bfloat16", "xs:4096 Pt:4096 Kt:4096 Zt:4096 Rt:3584 Et:2048 Ct:1024 XA:5376 XB:5376 XC:5376 XF:1024 VV:3072 Pg:1024 Kg:1024 "
-    "bt:1024 tm:1024 mm:1024 K5:256 Rg:256 aB:256 E:4096 qB:256 flB:256 winB:256 tK:256 xf:256 depB:256 NDa:256 NDc:256 "
-    "NDe:256 NDt:768 ones:144 zer:144 Q01:144 QP:144 QW:144 Q97:144 Q48:144 QS:144 Q1k:144 QKK:144 BD:128 BDs:128 BDf2:128 "
-    "BDf1:128 idB:128 idN:128 idH:128 idS:128 idMn:128 DM:512 WK:16 dg:640 pg:512 cg:128 sfl:256 sfh:256 sfi:256")
-_sb("float32", "onesF:128 idF:128 BDF:128 bs:128 ts:128 F:128 w16:16 hsS:64 thrR:256 thx:256 laneL:16 dumpL:16 fd:16 fo:16 fp:16 "
-    "dO:16 col:16 thF:1 ypF:192 ykA:224 ykB:224 hF:64")
-_sb("int32", "prevI:256 k0I:128 k1I:128 curI:64 startI:64 wI:1 thI:1 pI:1 pmI:1 pnI:1 ownI:128 own2:128 ti:1024 tc:128 ix0:64 "
-    "iy0:64 yA:224 yB:224 yC:224 hI:64 hJ:64 hK:64 hM:64 hN:64 yI:64 yJ:64 avI:256")
-_sb("uint16", "f0:64 fl:64 sl:384 hl:64 hp:64 el:64 fru:256 offU:16 depU:16")
+_sb("bfloat16", "xs:4096 Kt:4096 Zt:3840 Rt:3584 Et:3600 XA:5376 XB:5376 XC:5376 XF:1024 TM:3072 MM:3072 VV:1536 Pg:1024 Kg:1024 "
+    "bt:1024 Rb:512 K5:256 Rg:768 aB:256 E:4096 qB:256 winB:768 tK:256 xf:256 depB:256 NDlo:128 NEW:768 bs:64 "
+    "ones:256 zer:144 Qa:144 Qb:144 Q01:144 QP:144 QW:144 Q97:144 Q48:144 Q64:144 Q512:144 W1:8 WK:16 RQb:128 BD:128 BDs:128 BDi:128 "
+    "BDf:128 idB:128 idN:128 idH:128 idS:128 idM:128 idW:128 idMn:128 Mb:128 MbN:128 dg:640 pg:512 sfl:256 sfi:256 laneB:16")
+_sb("float16", "RQ:128 id16:128 hs:64 fru:256")
+_sb("float32", "onesF:128 BDF:128 ts:64 w16:16 thrR:256 laneL:16 dumpL:16 fo:16 col:32 thF:1 ypF:64 curF:64 curT:64 hF:64 hT:64 "
+    "Ct:1024 Cg:1024 Ko:3840 old32:256 tK32:256")
+_sb("int32", "prevI:256 kI:256 kH:256 curI:64 startI:64 wI:1 thI:1 pI:1 pmI:1 pnI:1 ownI:128 own2:128 hI:64 hJ:128 hK:64 yI:64 yJ:64 avI:256")
+_sb("uint16", "f0:64 fl:64 sl:384 hl:128 el:64 offU:16 depU:16")
+for _h in range(2):
+    SCRATCH["Fz%d" % _h] = ("sbuf", [128, 36, 4], "float16")
 for _i in range(8):
     SCRATCH["pb%d" % _i] = ("psum", [128, 512], "float32")
 
-NDMA = 40
+NDMA = 64
 SEMAPHORES = ["sV", "sS", "sP", "sG", "loc"] + ["d%d" % i for i in range(NDMA)] + ["a%d%d" % (t, c) for t in range(3) for c in range(2)]
+
+CYC, PEC, GAT, SCA, HAND, DMA0, DMAB, REMOTE = 0.00083, 0.00042, 1.4, 3.0, 0.14, 1.2, 1 / 350e3, 2.6
+WIDTH = {"bfloat16": 2, "float16": 2, "uint16": 2, "float32": 4, "int32": 4}
 
 
 def rank_program(g, core, T, topo):
@@ -44,139 +53,183 @@ def rank_program(g, core, T, topo):
 
     QUEUE = {"V": g.vector, "S": g.scalar, "P": g.tensor, "G": g, "D": g.sync}
     SEM = {"V": "sV", "S": "sS", "P": "sP", "G": "sG"}
-    total = {}
-    seen = {}
+    ops = []
     recs = {}
-    ndma = [0]
 
     def norm(r):
         b = r[0]
-        if b.startswith("pb"):
-            return (b, 0, 512, None)
-        if len(r) == 1:
-            return (b, 0, SCRATCH[b][1][1], None)
+        if len(r) == 1 or b.startswith("pb"):
+            return (b, 0, 1 << 20, None)
         if len(r) == 3:
             return (b, r[1], r[2], None)
         return r
 
-    def deps(q, isdma, reads, writes):
-        need = {}
+    def record(q, kind, calls, busy, done, reads, writes, sem=None, after=()):
+        me = len(ops)
+        pred = {}
+        for p in after:
+            pred[p] = False
         for rs, w in ((reads, False), (writes, True)):
             for r in rs:
                 b, lo, hi, tag = norm(r)
                 ps = b.startswith("pb")
                 for rec in recs.get(b, []):
-                    if rec[2] <= lo or rec[1] >= hi:
-                        continue
-                    if tag is not None and rec[3] is not None and tag != rec[3]:
+                    if rec[2] <= lo or rec[1] >= hi or (tag is not None and rec[3] is not None and tag != rec[3]):
                         continue
                     if not ps and not w and not rec[0]:
                         continue
-                    if rec[6] == q and not isdma:
-                        if ps or w:
-                            continue
-                    need[rec[4]] = max(need.get(rec[4], 0), rec[5])
-        for s in need:
-            if seen.get((q, s), 0) < need[s]:
-                QUEUE[q].wait_ge(T.sem[s], need[s])
-                seen[(q, s)] = need[s]
+                    o = ops[rec[4]]
+                    same = o[0] == q and o[1] == "op" and kind == "op"
+                    pred[rec[4]] = pred.get(rec[4], False) or not (same and (ps or w))
+        ops.append([q, kind, calls, busy, done, pred, sem])
+        for rs, w in ((reads, False), (writes, True)):
+            for r in rs:
+                b, lo, hi, tag = norm(r)
+                lst = recs.setdefault(b, [])
+                if b.startswith("pb"):
+                    recs[b] = [[True, lo, hi, tag, me]]
+                    continue
+                if w:
+                    recs[b] = [x for x in lst if not (x[1] >= lo and x[2] <= hi and (tag is None or x[3] == tag))]
+                recs[b].append([w, lo, hi, tag, me])
+        return me
 
-    def note(q, reads, writes, sem, val):
-        for r in reads:
-            b, lo, hi, tag = norm(r)
-            w = b.startswith("pb")
-            if w:
-                recs[b] = []
-            lst = recs.setdefault(b, [])
-            recs[b] = [x for x in lst if not ((not x[0]) and x[4] == sem and x[1] >= lo and x[2] <= hi and x[3] == tag)]
-            recs[b].append([w, lo, hi, tag, sem, val, q])
-        for r in writes:
-            b, lo, hi, tag = norm(r)
-            lst = recs.setdefault(b, [])
-            recs[b] = [x for x in lst if not (x[1] >= lo and x[2] <= hi and (tag is None or x[3] == tag))]
-            recs[b].append([True, lo, hi, tag, sem, val, q])
-
-    def op(q, calls, reads, writes):
-        deps(q, False, reads, writes)
-        s = SEM[q]
+    def op(q, calls, cost, reads, writes):
         if not isinstance(calls, list):
             calls = [calls]
-        for c in calls:
-            c().then_inc(T.sem[s], 1)
-            total[s] = total.get(s, 0) + 1
-        note(q, reads, writes, s, total[s])
+        return record(q, "op", calls, cost, cost + (0.06 if q == "P" else 0), reads, writes)
 
-    def dma(q, out, in_, reads, writes):
-        deps(q, True, reads, writes)
+    ndma = [0]
+
+    def dma(q, out, in_, nbytes, reads, writes, after=(), **kw):
         s = "d%d" % ndma[0]
         ndma[0] += 1
-        QUEUE[q].dma_start(out, in_).then_inc(T.sem[s], 16)
-        total[s] = 16
-        note(q + "dma", reads, writes, s, 16)
+        return record(q, "dma", lambda: QUEUE[q].dma_start(out, in_, **kw), 0.06 if q != "G" else 1.0, DMA0 + 0.2 + nbytes * DMAB, reads, writes, s, after)
+
+    def emit():
+        n = len(ops)
+        succ = [[] for _ in ops]
+        for i, o in enumerate(ops):
+            for p in o[5]:
+                succ[p].append(i)
+
+        def gap(p, i):
+            return ops[p][4] + HAND if ops[i][5][p] else ops[p][3]
+        level = [0.0] * n
+        for i in range(n - 1, -1, -1):
+            level[i] = max([gap(i, j) + level[j] for j in succ[i]] + [ops[i][4]])
+        start = [0.0] * n
+        taken = {}
+        for i in sorted(range(n), key=lambda i: (-level[i], i)):
+            t = max([start[p] + gap(p, i) for p in ops[i][5]] + [0.0])
+            uses = [(ops[i][0], 0.0, ops[i][3])]
+            if ops[i][1] == "dma":
+                uses.append(("engines", DMA0, ops[i][4]))
+            moved = True
+            while moved:
+                moved = False
+                for q, lo, hi in uses:
+                    for a, b in taken.setdefault(q, []):
+                        if t + lo < b - 1e-9 and t + hi > a + 1e-9:
+                            t, moved = b - lo, True
+            for q, lo, hi in uses:
+                taken[q].append((t + lo, t + hi))
+                taken[q].sort()
+            start[i] = t
+        total, seen, mark = {}, {}, {}
+        for i in sorted(range(n), key=lambda i: (start[i], i)):
+            q, kind, calls, _, _, pred, sem = ops[i]
+            if kind == "arrival":
+                mark[i] = (sem, calls)
+                total[sem] = calls
+                continue
+            need = {}
+            for p in pred:
+                if pred[p]:
+                    s, v = mark[p]
+                    need[s] = max(need.get(s, 0), v)
+            for s in need:
+                if seen.get((q, s), 0) < need[s]:
+                    QUEUE[q].wait_ge(T.sem[s], need[s])
+                    seen[(q, s)] = need[s]
+            if kind == "dma":
+                calls().then_inc(T.sem[sem], 16)
+                total[sem] = 16
+                mark[i] = (sem, 16)
+            elif kind == "send":
+                total["loc"] = total.get("loc", 0) + calls()
+            else:
+                s = SEM[q]
+                for c in calls:
+                    c().then_inc(T.sem[s], 1)
+                total[s] = total.get(s, 0) + len(calls)
+                mark[i] = (s, total[s])
+        for s in total:
+            if seen.get(("G", s), 0) < total[s]:
+                g.wait_ge(T.sem[s], total[s])
 
     V = g.vector
 
-    def cp(out, in_, rd, wr):
-        op("V", lambda: V.tensor_copy(out=out, in_=in_), rd, wr)
+    def count(ap):
+        return math.prod(ap.shape[1:])
 
-    def tt(out, a, b, o, rd, wr):
-        op("V", lambda: V.tensor_tensor(out=out, in0=a, in1=b, op=o), rd, wr)
+    def vcost(n, rd, wr, two=False, ind=0.0):
+        if ind:
+            return 0.05 + n * ind * CYC
+        psum = any(r[0].startswith("pb") for r in rd + wr)
+        narrow = WIDTH[SCRATCH[rd[0][0]][2]] == 2 and WIDTH[SCRATCH[wr[0][0]][2]] == 2
+        return 0.05 + n * CYC * ((1 if psum else 2) if two else (0.5 if narrow else 1))
+
+    def cp(out, in_, rd, wr, n=None, ind=0.0):
+        return op("V", lambda: V.tensor_copy(out=out, in_=in_), vcost(n or count(out), rd, wr, False, ind), rd, wr)
+
+    def tt(out, a, b, o, rd, wr, ind=0.0):
+        return op("V", lambda: V.tensor_tensor(out=out, in0=a, in1=b, op=o), vcost(count(b), rd, wr, True, ind), rd, wr)
 
     def ts(out, a, s1, o1, rd, wr, s2=None, o2=None):
+        c = vcost(count(out), rd, wr)
         if o2 is None:
-            op("V", lambda: V.tensor_scalar(out=out, in0=a, scalar1=s1, scalar2=None, op0=o1), rd, wr)
-        else:
-            op("V", lambda: V.tensor_scalar(out=out, in0=a, scalar1=s1, scalar2=s2, op0=o1, op1=o2), rd, wr)
+            return op("V", lambda: V.tensor_scalar(out=out, in0=a, scalar1=s1, scalar2=None, op0=o1), c, rd, wr)
+        return op("V", lambda: V.tensor_scalar(out=out, in0=a, scalar1=s1, scalar2=s2, op0=o1, op1=o2), c, rd, wr)
 
     def fill(name, lo, hi, v):
-        op("V", lambda: V.memset(T[name][:, lo:hi], v), [], [(name, lo, hi)])
+        r = (name, lo, hi)
+        op("V", lambda: V.memset(T[name][:, lo:hi], v), vcost(hi - lo, [r], [r]), [], [r])
 
-    def act(out, in_, rd, wr, func=AF.Copy, **kw):
-        op("S", lambda: g.scalar.activation(out=out, in_=in_, func=func, **kw), rd, wr)
+    def act(out, in_, rd, wr, func=AF.Copy, ind=1.0, more=0.0, **kw):
+        op("S", lambda: g.scalar.activation(out=out, in_=in_, func=func, **kw), 0.065 + more + count(out) * ind * CYC, rd, wr)
 
     def gather(eng, out, outr, win, winr, lst, lstr):
         if eng == "S":
-            act(out, win.indirect(lst), [winr, lstr], [outr])
+            act(out, win.indirect(lst), [winr, lstr], [outr], ind=GAT)
         else:
-            cp(out, win.indirect(lst), [winr, lstr], [outr])
+            cp(out, win.indirect(lst), [winr, lstr], [outr], ind=GAT)
 
-    def mm(out, l, r, st, sp):
-        return lambda: g.tensor.matmul(out, l, r, st, sp)
+    def pe(bank, terms, rd, first=True, last=True, wide=1, alone=False):
+        n = len(terms)
+        for a in range(0, n, 4):
+            calls, cost = [], 0.0
+            for i in range(a, min(a + 4, n)):
+                o, l, r = terms[i]
+                st, sp = alone or (first and i == 0), alone or (last and i == n - 1)
+                calls.append(lambda o=o, l=l, r=r, st=st, sp=sp: g.tensor.matmul(o, l, r, st, sp))
+                cost += wide * max(64, count(r)) * PEC
+            op("P", calls, cost, rd, [(bank,)])
 
-    def direct(bank, col, n, Q, data, base, rd):
-        b = T[bank]
-        op("P", [mm(b[:, col:col + n], Q[:, 15 - r:143 - r], data[:, base + r:base + 16 * n:16], r == 0, r == 15)
-                 for r in range(16)], rd, [(bank,)])
+    def direct(out, n, Q, data, base):
+        return [(out, Q[:, 15 - r:143 - r], data[:, base + r:base + 16 * n:16]) for r in range(16)]
 
-    def block(bank, col, n, Q, data, rd):
-        b = T[bank]
-        op("P", [mm(b[:, col:col + n], Q[:, 15 - r:143 - r], data[:, n * r:n * r + n], r == 0, r == 15) for r in range(16)],
-           rd, [(bank,)])
+    def block(out, n, Q, data):
+        return [(out, Q[:, 15 - r:143 - r], data[:, n * r:n * r + n]) for r in range(16)]
 
-    def iota(name, lo, hi, pattern, base, cm, small):
+    def iota(name, lo, hi, pattern, base, cm):
         ap = T[name][:, lo:hi]
-        if small:
-            op("G", lambda: g.iota(ap, pattern, base, cm, allow_small_or_imprecise_dtypes=True), [], [(name, lo, hi)])
-        else:
-            op("G", lambda: g.iota(ap, pattern, base, cm), [], [(name, lo, hi)])
+        kw = {} if SCRATCH[name][2] == "int32" else {"allow_small_or_imprecise_dtypes": True}
+        op("G", lambda: g.iota(ap, pattern, base, cm, **kw), 0.13 + 2 * (hi - lo) * CYC, [], [(name, lo, hi)])
 
-    def sel(name, src, pattern, cmp, base, cm, n):
-        op("G", lambda: g.affine_select(T[name][:, 0:n], T[src][:, 0:n], pattern, cmp, 0.0, base, cm), [(src, 0, n)], [(name, 0, n)])
-
-    def put(name, n, pattern, entries, lo=0):
-        for j, (base, v) in enumerate(entries):
-            ap, r = (T.zer[:, 0:n], ("zer",)) if j == 0 else (T[name][:, lo:lo + n], (name, lo, lo + n))
-            op("G", lambda ap=ap, base=base, v=v: g.affine_select(T[name][:, lo:lo + n], ap, pattern, A.not_equal, float(v), base, 1),
-               [r], [(name, lo, lo + n)])
-
-    def putQ(name, entries):
-        put(name, 144, [[-16, 9], [1000, 16]], [(-15000 - i, v) for i, v in entries])
-
-    def putB(name, entries):
-        put(name, 128, [[-16, 8], [0, 16]], [(-i, v) for i, v in entries])
-
-    def putD(name, lo, places, v=1.0):
-        put(name, 128, [[-16, 8], [999, 16]], [(-1000 * i, v) for i in places], lo)
+    def sel(name, src_, n, pattern, cmp, v, base, cm):
+        op("G", lambda: g.affine_select(T[name][:, 0:n], T[src_][:, 0:n], pattern, cmp, float(v), base, cm), 0.17 + 2 * n * CYC,
+           [(src_, 0, n)], [(name, 0, n)])
 
     C = {}
 
@@ -185,415 +238,377 @@ def rank_program(g, core, T, topo):
         C[nm] = (T.col[:, i:i + 1], ("col", i, i + 1))
         return C[nm]
 
-    dma("D", T.prevI[:, :], T.prev[:, :], [], [("prevI",)])
-    dma("D", T.k0I[:, :], T.kid0[:, :], [], [("k0I",)])
-    dma("S", T.curI[:, :], T.cur[:, :], [], [("curI",)])
-    dma("S", T.startI[:, :], T.start[:, :], [], [("startI",)])
-    dma("D", T.k1I[:, :], T.kid1[:, :], [], [("k1I",)])
-    dma("S", T.wI[:, :], T.w[:, :], [], [("wI",)])
-    dma("D", T.xs[:, :], T.x[:, :], [], [("xs",)])
-    dma("S", T.Zt[:, 0:2048], T.z[:, :], [], [("Zt", 0, 2048)])
+    MB = 128 * 2
+    small = [dma("D", T.prevI[:, :], T.prev[:, :], 131072, [], [("prevI",)]),
+             dma("S", T.kI[:, 0:128], T.kid0[:, :], 65536, [], [("kI", 0, 128)]),
+             dma("D", T.kI[:, 128:256], T.kid1[:, :], 65536, [], [("kI", 128, 256)]),
+             dma("S", T.curI[:, :], T.cur[:, :], 32768, [], [("curI",)]),
+             dma("D", T.startI[:, :], T.start[:, :], 32768, [], [("startI",)])]
+    big = dma("S", T.xs[:, :], T.x[:, :], 4096 * MB, [], [("xs",)], small)
+    dma("D", T.Zt[:, 0:2048], T.z[:, :], 2048 * MB, [], [("Zt", 0, 2048)], small + [big])
+    dma("S", T.wI[:, :], T.w[:, :], 512, [], [("wI",)], [big])
 
-    iota("pI", 0, 1, [[0, 1]], 0, 1, False)
-    iota("sfl", 0, 256, [[1, 256]], 0, 0, True)
-    iota("ownI", 0, 128, [[1, 128]], 0, 128, False)
-    pm, pmr = column("pm")
-    pe, per = column("pe")
-    fill("ones", 0, 144, 1.0)
-    fill("onesF", 0, 128, 1.0)
-    ts(T.pmI[:, :], T.pI[:, :], 15, A.bitwise_and, [("pI",)], [("pmI",)])
-    ts(T.pnI[:, :], T.pI[:, :], 7, A.bitwise_and, [("pI",)], [("pnI",)])
-    fill("thI", 0, 1, 0)
-    cp(pm, T.pmI[:, :], [("pmI",)], [pmr])
-    ts(pe, T.pnI[:, :], 8.0, A.add, [("pnI",)], [per])
-    fill("Zt", 2048, 4096, 0.0)
-    fill("Kt", 0, 4096, 0.0)
+    fill("ones", 0, 256, 1.0)
     fill("zer", 0, 144, 0.0)
-    ZU = ("Zt", 2048, 4096)
-    act(T.sfh[:, :], T.sfl[:, :], [("sfl",), pmr], [("sfh",)], func=AF.Identity, scale=0.0, bias=pm)
-    act(T.sfi[:, :], T.sfl[:, :], [("sfl",), per], [("sfi",)], func=AF.Identity, scale=0.0, bias=pe)
-    act(T.Pt[:, 0:2048], T.Zt[:, 2048:4096], [ZU], [("Pt", 0, 2048)])
-    act(T.Pt[:, 2048:4096], T.Zt[:, 2048:4096], [ZU], [("Pt", 2048, 4096)])
-
-    sel("Q01", "ones", [[0, 9], [1, 16]], A.is_equal, -15, 0, 144)
-    sel("Q01", "Q01", [[-16, 9], [0, 16]], A.is_ge, 0, 1, 144)
-    sel("Q01", "Q01", [[16, 9], [0, 16]], A.is_ge, 15, -1, 144)
-    putQ("QP", [(0, 1), (1, 256)])
-    put("WK", 8, [[-16, 8]], [(0, 1), (-1, 256)], 0)
-    put("WK", 8, [[-16, 8]], [(0, -1), (-1, -256), (-2, 1), (-3, 256)], 8)
-    putB("BDf1", [(6, 1)])
-    sel("idF", "onesF", [[-1, 128]], A.is_equal, 0, 1, 128)
-    sel("BD", "ones", [[-16, 8], [0, 16]], A.is_ge, 0, 1, 128)
-    sel("BD", "BD", [[16, 8], [0, 16]], A.is_ge, 15, -1, 128)
-    iota("laneL", 0, 16, [[16, 16]], 0, 0, True)
-    for nm, v in (("idB", 1.0), ("idN", -1.0), ("idH", 0.5), ("idS", -128.0)):
-        put(nm, 128, [[-1, 128]], [(0, v)])
-    putB("BDs", [(4, 1), (5, 256)])
-    putB("BDf2", [(6, 2)])
-    putQ("Q1k", [(0, 1024)])
-    putQ("QS", [(0, 1)])
-    iota("NDa", 0, 256, [[0, 2], [2, 128]], 0, 0, True)
-    iota("NDc", 0, 256, [[0, 2], [2, 128]], 1, 0, True)
-    iota("NDe", 0, 256, [[0, 256]], 1, 0, True)
-    for t in range(3):
-        iota("NDt", 256 * t, 256 * t + 256, [[1, 2], [0, 128]], 8 + 2 * t, 0, True)
-    putD("DM", 0, (0,))
-    putD("DM", 128, (2,))
-    putD("DM", 256, (1, 3))
-    putD("DM", 384, (6,))
-    putD("idMn", 0, (0, 1, 2, 3, 6), -1.0)
-    putQ("QKK", [(0, 1), (1, 256), (2, 4096), (3, 1048576)])
-
-    def digits(name, n, tmp, to, out, oo):
-        for j, (o, v) in enumerate(((A.bitwise_and, 255), (A.arith_shift_right, 8))):
-            a, b = to + j * n, oo + j * n
-            ts(T[tmp][:, a:a + n], T[name][:, :], v, o, [(name,)], [(tmp, a, a + n)])
-            cp(T[out][:, b:b + n], T[tmp][:, a:a + n], [(tmp, a, a + n)], [(out, b, b + n)])
+    for a in range(0, 4096, 1024):
+        fill("Kt", a, a + 1024, 1.0)
+    for h in range(2):
+        cp(T["Fz%d" % h][:, :, :], T.zer[:, :], [("zer",)], [("Fz%d" % h,)])
+    GR = [-16, 8]
+    sel("W1", "ones", 8, [GR], A.is_ge, 0, 0, 1)
+    sel("W1", "W1", 8, [[16, 8]], A.is_ge, 0, 15, -1)
+    sel("WK", "zer", 16, [[2, 2], GR], A.is_ge, 1, -4, 1)
+    sel("WK", "WK", 16, [[2, 2], GR], A.is_ge, -1, -2, 1)
+    sel("WK", "WK", 16, [[0, 2], GR], A.is_ge, 0, 0, 1)
+    sel("WK", "WK", 16, [[1000, 2], GR], A.not_equal, -OFF, -1013, 1)
+    sel("Qa", "ones", 144, [[0, 9], [1, 16]], A.is_equal, 0, -15, 0)
+    sel("Qb", "Qa", 144, [[16, 9], [0, 16]], A.is_ge, 0, 15, -1)
+    sel("QP", "Qb", 144, [[-16, 9], [0, 16]], A.is_ge, 0, -14, 1)
+    sel("Q01", "Qb", 144, [[-16, 9], [0, 16]], A.is_ge, 0, 0, 1)
+    sel("RQb", "ones", 128, [[-1, 4], [-4, 32]], A.is_equal, 0, 0, 1)
+    cp(T.RQ[:, :], T.RQb[:, :], [("RQb",)], [("RQ",)])
+    iota("ownI", 0, 128, [[1, 128]], 0, 128)
+    iota("pI", 0, 1, [[0, 1]], 0, 1)
+    iota("sfl", 0, 256, [[1, 256]], 0, 0)
+    iota("laneL", 0, 16, [[16, 16]], 0, 0)
+    iota("NDlo", 0, 128, [[2, 128]], 0, 0)
+    for nm, v in (("idB", 1), ("idN", -1), ("idH", 0.5), ("idS", -128), ("idM", -8192), ("idW", 512)):
+        sel(nm, "zer", 128, [[-1, 128]], A.not_equal, v, 0, 1)
+    cp(T.id16[:, :], T.idB[:, :], [("idB",)], [("id16",)])
+    sel("Mb", "idB", 128, [[-1, 128]], A.not_equal, 1, -1, 1)
+    sel("MbN", "idN", 128, [[-1, 128]], A.not_equal, -1, -1, 1)
+    PL = [GR, [0, 16]]
+    sel("BD", "ones", 128, PL, A.is_ge, 0, 0, 1)
+    sel("BD", "BD", 128, [[16, 8], [0, 16]], A.is_ge, 0, 15, -1)
+    sel("BDf", "zer", 128, PL, A.not_equal, 1, -4, 1)
+    sel("BDs", "zer", 128, PL, A.not_equal, 1, 0, 1)
+    sel("BDs", "BDs", 128, PL, A.not_equal, 1, -1, 1)
+    sel("BDs", "BDs", 128, PL, A.not_equal, -OFF, -13, 1)
+    fill("onesF", 0, 128, 1.0)
+    sel("BDF", "onesF", 128, PL, A.is_ge, 0, 0, 1)
+    sel("BDF", "BDF", 128, [[16, 8], [0, 16]], A.is_ge, 0, 15, -1)
 
     cp(T.f0[:, :], T.startI[:, :], [("startI",)], [("f0",)])
     cp(T.sl[:, 0:64], T.curI[:, :], [("curI",)], [("sl", 0, 64)])
-    digits("prevI", 256, "ti", 512, "pg", 0)
-    dma("D", T.Pt[0:128:16, :], T.pg[:, 0:256], [("pg", 0, 256)], [("Pt", 0, 4096, "r0")])
-    dma("D", T.Pt[1:128:16, :], T.pg[:, 256:512], [("pg", 256, 512)], [("Pt", 0, 4096, "r1")])
+    cp(T.pg[:, 0:256], T.prevI[:, :], [("prevI",)], [("pg", 0, 256)])
+    tt(T.pg[:, 256:512], T.prevI[:, :], T.pg[:, 0:256], A.subtract, [("prevI",), ("pg", 0, 256)], [("pg", 256, 512)])
+    for j in range(2):
+        dma("D", T.Kt[14 + j:128:16, :], T.pg[:, 256 * j:256 * j + 256], 65536, [("pg", 256 * j, 256 * j + 256)], [("Kt", 0, 4096, "r%d" % (14 + j))])
+    ts(T.kH[:, :], T.kI[:, :], 0xF00, A.bitwise_and, [("kI",)], [("kH",)])
+    cp(T.dg[:, 0:256], T.kH[:, :], [("kH",)], [("dg", 0, 256)])
+    tt(T.dg[:, 256:512], T.kI[:, :], T.kH[:, :], A.subtract, [("kI",), ("kH",)], [("dg", 256, 512)])
     ts(T.own2[:, :], T.ownI[:, :], 2047, A.bitwise_and, [("ownI",)], [("own2",)])
-    digits("k0I", 128, "ti", 0, "dg", 0)
-    digits("k1I", 128, "ti", 256, "dg", 256)
-    tt(T.dg[:, 512:640], T.k0I[:, :], T.own2[:, :], A.not_equal, [("k0I",), ("own2",)], [("dg", 512, 640)])
-    dma("D", T.Kt[4:128:16, :], T.sfl[:, :], [("sfl",)], [("Kt", 0, 4096, "r4")])
-    dma("D", T.Kt[5:128:16, :], T.sfh[:, :], [("sfh",)], [("Kt", 0, 4096, "r5")])
-    for i in range(4):
-        nm = ("sfl", "sfi")[i % 2]
-        dma("D", T.Kt[i:128:16, 2048:4096], T[nm][0:64, :], [(nm,)], [("Kt", 2048, 4096, "r%d" % i)])
-    for i, j in ((0, 0), (1, 1), (2, 2), (3, 3), (6, 4)):
-        dma("D", T.Kt[i:128:16, 0:2048], T.dg[:, 128 * j:128 * j + 128], [("dg", 128 * j, 128 * j + 128)], [("Kt", 0, 2048, "r%d" % i)])
-    dma("D", T.thI[0:128:16, :], T.th[:, :], [], [("thI",)])
-    dma("D", T.Rt[:, 0:2048], T.rs[:, :], [], [("Rt", 0, 2048)])
-    dma("D", T.Et[:, :], T.env[:, :], [], [("Et",)])
+    tt(T.dg[:, 512:640], T.kI[:, 0:128], T.own2[:, :], A.not_equal, [("kI", 0, 128), ("own2",)], [("dg", 512, 640)])
+    for i, j in ((0, 0), (1, 2), (2, 1), (3, 3), (4, 4)):
+        dma("DS"[i % 2], T.Kt[i:128:16, 0:2048], T.dg[:, 128 * j:128 * j + 128], 32768, [("dg", 128 * j, 128 * j + 128)], [("Kt", 0, 2048, "r%d" % i)])
+
+    pm, pmr = column("pm")
+    ts(T.pmI[:, :], T.pI[:, :], 15, A.bitwise_and, [("pI",)], [("pmI",)])
+    cp(pm, T.pmI[:, :], [("pmI",)], [pmr])
     wc, wcr = column("w")
     cp(wc, T.wI[:, :], [("wI",)], [wcr])
-    W1 = T.Q01[:, 15:128:16]
-
-    def scaled(name, c, rd):
-        ts(T[name][:, :], T.Q01[:, :], c, A.mult, [("Q01",)] + rd, [(name,)])
-
+    ts(T.QW[:, :], T.Q01[:, :], wc, A.mult, [("Q01",), wcr], [("QW",)])
+    for nm, v in (("Q97", 97.0), ("Q48", 48.5), ("Q64", 64.0), ("Q512", 512.0)):
+        act(T[nm][:, :], T.Q01[:, :], [("Q01",)], [(nm,)], scale=v)
+    ts(T.BDi[:, :], T.BDf[:, :], 1e18, A.mult, [("BDf",)], [("BDi",)], 1e18, A.mult)
+    ts(T.laneL[:, :], T.laneL[:, :], pm, A.add, [("laneL",), pmr], [("laneL",)])
+    cp(T.laneB[:, :], T.laneL[:, :], [("laneL",)], [("laneB",)])
+    ts(T.dumpL[:, :], T.laneL[:, :], 3584.0 - OFF, A.add, [("laneL",)], [("dumpL",)])
     LN = math.log(1.85)
+    act(T.w16[:, :], T.laneL[:, :], [("laneL",)], [("w16",)], func=AF.Exp, more=1.3, scale=-LN, bias=128 * LN)
+    act(T.thrR[:, :], T.sfl[:, :], [("sfl",), ("w16",)], [("thrR",)], func=AF.Exp, scale=-LN, bias=128 * LN + math.log(2.5))
+    for nm, o, v in (("lt5", A.is_lt, 5.0), ("e0", A.is_equal, 0.0), ("e1", A.is_equal, 1.0), ("e2", A.is_equal, 2.0), ("e3", A.is_equal, 3.0),
+                     ("e4", A.is_equal, 4.0)):
+        c, r = column(nm)
+        ts(c, pm, v, o, [pmr], [r])
+    for nm, a, b in (("hi", "e0", "e2"), ("lo", "e1", "e3"), ("one", "e3", "e4")):
+        c, r = column(nm)
+        tt(c, C[a][0], C[b][0], A.add, [C[a][1], C[b][1]], [r])
+    ts(T.idMn[:, :], T.idN[:, :], C["lt5"][0], A.mult, [("idN",), C["lt5"][1]], [("idMn",)])
+    for j in range(6):
+        c, r = column("n%d" % j)
+        ts(c, C["hi"][0], 2048.0 + 256 * j, A.mult, [C["hi"][1], C["one"][1]], [r], C["one"][0], A.add)
+        act(T.NEW[:, 128 * j:128 * j + 128], T.NDlo[:, :], [("NDlo",), C["lo"][1], r], [("NEW", 128 * j, 128 * j + 128)], func=AF.Identity,
+            scale=C["lo"][0], bias=c)
+    fill("thI", 0, 1, 0)
+    dma("D", T.thI[0:128:16, :], T.th[:, :], 32, [], [("thI",)])
+    cp(T.thF[:, :], T.thI[:, :], [("thI",)], [("thF",)])
+    pe("pb5", [(T.pb5[:, 0:1], T.BDF[:, :], T.thF[:, :])], [("BDF",), ("thF",)], wide=4)
+    thc, thr = column("th")
+    cp(thc, T.pb5[:, 0:1], [("pb5",)], [thr])
+    gate = [("XA", 1024, 1040)]
+    iota("Et", 0, 900, [[0, 900]], -256, 0)
+    iota("Ct", 0, 1024, [[0, 1024]], 0, 0)
+    pe_, per = column("pe")
+    ts(T.pnI[:, :], T.pI[:, :], 7, A.bitwise_and, [("pI",)], [("pnI",)])
+    ts(pe_, T.pnI[:, :], 256.0, A.mult, [("pnI",)], [per], 2048.0, A.add)
+    act(T.sfi[:, :], T.sfl[:, :], [("sfl",), per], [("sfi",)], func=AF.Identity, scale=0.0, bias=pe_)
 
-    def late1():
-        fill("Rt", 2048, 3584, 0.0)
-        fill("Ct", 0, 1024, 0.0)
-        scaled("QW", wc, [wcr])
+    def env_table():
+        dma("D", T.Rt[:, 0:2048], T.rs[:, :], 2048 * MB, gate, [("Rt", 0, 2048)])
+        dma("D", T.Zt[:, 2048:3840], T.z[:, 0:1792], 1792 * MB, gate, [("Zt", 2048, 3840)])
+        for a in (900, 1800, 2700):
+            dma("D", T.Et[:, a:a + 900], T.Et[:, 0:900], 900 * MB, [("Et", 0, 900)] + gate, [("Et", a - 4, a + 904)])
+        dma("G", T.Et[:, 0:2048], T.env[:, :], 2048 * MB * 2, [], [("Et", 0, 2048)], accum_op=A.add)
+        dma("G", T.Et[:, 2048:EW], T.env[:, 0:EW - 2048], 1552 * MB * 2, [], [("Et", 2048, EW)], accum_op=A.add)
 
-    def late1b():
-        ts(T.laneL[:, :], T.laneL[:, :], pm, A.add, [("laneL",), pmr], [("laneL",)])
-        scaled("Q97", 97.0, [])
-        scaled("Q48", 48.5, [])
-        ts(T.dumpL[:, :], T.laneL[:, :], 3584.0, A.add, [("laneL",)], [("dumpL",)])
+    def new_nodes():
+        for i in range(5):
+            if i < 4:
+                nm = ("sfi", "sfl")[i % 2]
+                dma("D", T.Kt[i:128:16, 2048:4096], T[nm][0:64, :], 32768, [(nm,)], [("Kt", 2048, 4096, "r%d" % i)])
+            else:
+                dma("D", T.Kt[i:128:16, 2048:4096], T.zer[:, 0:128], 32768, [("zer",)], [("Kt", 2048, 4096, "r%d" % i)])
 
-    def late2():
-        act(T.w16[:, :], T.laneL[:, :], [("laneL",)], [("w16",)], func=AF.Exp, scale=-LN, bias=128 * LN)
-        act(T.thrR[:, :], T.sfl[:, :], [("sfl",)], [("thrR",)], func=AF.Exp, scale=-LN, bias=128 * LN + math.log(2.5))
+    def turn(lst, lstr, buf, to, tor, col):
+        op("V", lambda: V.transpose(T[buf][:, :], lst), 0.05 + 64 * CYC, [lstr], [(buf,)])
+        for e in range(2):
+            for b in range(2):
+                a = col + 512 * b
+                dma("D", to(e, a), T[buf][:, 32 * b + 16 * e:32 * b + 16 * e + 16], 8192, [(buf,)],
+                    [tor + ("e%d%d" % (e, b),)] if tor else [])
 
-    def late3():
-        cp(T.BDF[:, :], T.BD[:, :], [("BD",)], [("BDF",)])
-        cp(T.thF[:, :], T.thI[:, :], [("thI",)], [("thF",)])
-        op("P", mm(T.pb4[:, 100:101], T.BDF[:, :], T.thF[:, :], True, True), [("BDF",), ("thF",)], [("pb4",)])
-        c, r = column("thm")
-        ts(c, T.pb4[:, 100:101], -1048576.0, A.add, [("pb4",)], [r])
-
-    def late4():
-        digits("curI", 64, "tc", 0, "cg", 0)
-        dma("D", T.Ct[0:128:16, :], T.cg[:, 0:64], [("cg", 0, 64)], [("Ct", 0, 1024, "r0")])
-        dma("D", T.Ct[1:128:16, :], T.cg[:, 64:128], [("cg", 64, 128)], [("Ct", 0, 1024, "r1")])
+    cp(T.curF[:, :], T.curI[:, :], [("curI",)], [("curF",)])
+    turn(T.curF[:, :], ("curF",), "curT", lambda e, a: T.Ct[16 * e:128:32, a:a + 512], ("Ct", 0, 1024), 0)
 
     XP = ["XA", "XB", "XC", "XF"]
+    IB = ["pb2", "pb3"]
 
     def nodes(h, k):
         nm = "f0" if k == 0 else "fl"
         return T[nm][:, 32 * h:32 * h + 32], (nm, 32 * h, 32 * h + 32)
 
-    def kid(h, k):
+    def to_list(h, out, n):
+        return [(out, T["Fz%d" % h][:, 3 - q:35 - q, :], T.RQ[:, 32 * q:32 * q + n]) for q in range(4)]
+
+    def step(t, h, k):
         l, r = nodes(h, k)
-        act(T.Kg[:, 512 * h:512 * h + 512], T.Kt[:, :].indirect(l), [("Kt",), r], [("Kg", 512 * h, 512 * h + 512)])
-
-    def cmpz(t, h, k):
-        l, r = nodes(h, k)
-        a = 1024 * k + 512 * h
-        tt(T.bt[:, 512 * h:512 * h + 512], T.Zt[:, :].indirect(l), T[XP[t]][:, a:a + 512], A.is_le,
-           [("Zt",), r, (XP[t], a, a + 512)], [("bt", 512 * h, 512 * h + 512)])
-
-    def pekids(h):
-        op("P", [mm(T.pb0[32 * h:32 * h + 32, r:256:16], T.Kg[:, 512 * h + r:512 * h + 512:16], T.WK[:, :], True, True) for r in range(16)],
-           [("Kg", 512 * h, 512 * h + 512), ("WK",)], [("pb0",)])
-
-    def pecnt(h):
-        op("P", [mm(T.pb6[32 * h:32 * h + 32, r:128:16], T.bt[:, 512 * h + r:512 * h + 512:16], W1, True, True) for r in range(16)],
-           [("bt", 512 * h, 512 * h + 512), ("Q01",)], [("pb6",)])
+        a, top, bank = 512 * h, 2048 + 512 * t, "pb%d" % h
+        pb, F = T[bank], "Fz%d" % h
+        kg, b_ = ("Kg", a, a + 512), ("bt", a, a + 512)
+        act(T.Kg[:, a:a + 512], T.Kt[:, 0:top].indirect(l), [("Kt", 0, top), r], [kg], ind=GAT)
+        x = 1024 * k + a
+        tt(T.bt[:, a:a + 512], T.Zt[:, 0:top].indirect(l), T[XP[t]][:, x:x + 512], A.is_le, [("Zt", 0, top), r, (XP[t], x, x + 512)], [b_], ind=GAT)
+        pe(bank, [(pb[:, 32 + j:96:4], T.Kg[:, a + j:a + 512:4], T.WK[:, :]) for j in range(4)], [kg, ("WK",)], alone=True)
+        pe(bank, [(pb[:, j:32:4], T.bt[:, a + j:a + 512:4], T.W1[:, :]) for j in range(4)], [b_, ("W1",)], alone=True)
+        if h == 0 and t < 2:
+            pe("pb4", [(T.pb4[:, 0:256], T.BDf[:, :], T.Kg[:, 0:256])], [("Kg", 0, 256), ("BDf",)], k == 0, k == 4)
+        c = 32 * h
+        ts(T.bs[:, c:c + 32], pb[:, 0:32], 8.5, A.is_ge, [(bank,)], [("bs", c, c + 32)])
+        tt(T.ts[:, c:c + 32], pb[:, 32:64], T.bs[:, c:c + 32], A.mult, [(bank,), ("bs", c, c + 32)], [("ts", c, c + 32)])
+        tt(T[F][:, 3:35:4, :], pb[:, 64:96], T.ts[:, c:c + 32], A.add, [(bank,), ("ts", c, c + 32)], [(F,)])
+        pe(bank, to_list(h, pb[:, 128:160], 32), [(F,), ("RQ",)])
+        ts(T.fl[:, c:c + 32], pb[:, 128:160], float(OFF), A.add, [(bank,)], [("fl", c, c + 32)])
 
     def xg(eng, t, k, a, b):
+        if a >= b:
+            return
         o = 1024 * k
         out, outr = T[XP[t]][:, o + a:o + b], (XP[t], o + a, o + b)
         if t == 0:
             lo, hi = 64 * k + a // 16, 64 * k + b // 16
             gather(eng, out, outr, T.xs[:, :], ("xs",), T.sl[:, lo:hi], ("sl", lo, hi))
         else:
-            w = 1024 * (k - 1)
-            gather(eng, out, outr, T[XP[t - 1]][:, w:w + 1024], (XP[t - 1], w, w + 1024), T.hl[:, a // 16:b // 16], ("hl", a // 16, b // 16))
+            w, lo, hi = 1024 * (k - 1), 64 * (t - 1) + a // 16, 64 * (t - 1) + b // 16
+            gather(eng, out, outr, T[XP[t - 1]][:, w:w + 1024], (XP[t - 1], w, w + 1024), T.hl[:, lo:hi], ("hl", lo, hi))
 
-    def pgat(k, n):
-        gather("S", T.Pg[:, 0:n], ("Pg",), T.Pt[:, :], ("Pt",), T.sl[:, 64 * k:64 * k + n // 16], ("sl", 64 * k, 64 * k + n // 16))
+    def paths(t, h, k):
+        a = 512 * h
+        xg("S", t, k, a, a + XS[t][h])
+        xg("V", t, k, a + XS[t][h], a + 512)
 
-    def psum(n):
-        direct("pb2", 0, n // 16, T.QP, T.Pg, 0, [("Pg",), ("QP",)])
-
-    def plist(k, n):
-        cp(T.sl[:, 64 * k:64 * k + n // 16], T.pb2[:, 0:n // 16], [("pb2",)], [("sl", 64 * k, 64 * k + n // 16)])
+    def pred(k, n):
+        for eng, a, b in (("S", 0, min(n, 512, PS)), ("S", 512, min(n, PS)), ("V", PS, n)):
+            if a < b:
+                lo, hi = 64 * k + a // 16, 64 * k + b // 16
+                gather(eng, T.Pg[:, a:b], ("Pg", a, b), T.Kt[:, :], ("Kt",), T.sl[:, lo:hi], ("sl", lo, hi))
+        m = n // 16
+        pe("pb7", direct(T.pb7[:, 0:m], m, T.QP, T.Pg, 0), [("Pg", 0, n), ("QP",)])
+        cp(T.sl[:, 64 * k + 64:64 * k + 64 + m], T.pb7[:, 0:m], [("pb7",)], [("sl", 64 * k + 64, 64 * k + 64 + m)])
 
     def hsum(t, h):
-        direct("pb2", 64 + 32 * h, 32, T.QW, T[XP[t]], 512 * h, [(XP[t], 512 * h, 512 * h + 512), ("QW",)])
+        c, bank = 32 * h, IB[h]
+        pe(bank, direct(T[bank][:, 0:32], 32, T.QW, T[XP[t]], 512 * h), [(XP[t], 512 * h, 512 * h + 512), ("QW",)])
+        cp(T.hI[:, c:c + 32], T[bank][:, 0:32], [(bank,)], [("hI", c, c + 32)])
+        if t > 0:
+            d = 64 * (t - 1) + c
+            ts(T.hJ[:, d:d + 32], T.hI[:, c:c + 32], 1023, A.bitwise_and, [("hI", c, c + 32)], [("hJ", d, d + 32)])
+            cp(T.hl[:, d:d + 32], T.hJ[:, d:d + 32], [("hJ", d, d + 32)], [("hl", d, d + 32)])
+        ts(T.hK[:, c:c + 32], T.hI[:, c:c + 32], 2047, A.bitwise_and, [("hI", c, c + 32)], [("hK", c, c + 32)])
+        cp(T.hs[:, c:c + 32], T.hK[:, c:c + 32], [("hK", c, c + 32)], [("hs", c, c + 32)])
 
-    def hlow():
-        ts(T.hsS[:, 0:16], T.pb2[:, 64:80], 776.0, A.add, [("pb2",)], [("hsS", 0, 16)])
-
-    def hhigh():
-        cp(T.hsS[:, 16:64], T.pb2[:, 80:128], [("pb2",)], [("hsS", 16, 64)])
-
-    def hlist():
-        cp(T.hI[:, :], T.pb2[:, 64:128], [("pb2",)], [("hI",)])
-        hlow()
-        ts(T.hJ[:, :], T.hI[:, :], 1023, A.bitwise_and, [("hI",)], [("hJ",)])
-        hhigh()
-        cp(T.hl[:, :], T.hJ[:, :], [("hJ",)], [("hl",)])
-
-    def arrived(t, h):
-        s = "a%d%d" % (t, h)
-        total[s] = len(pairs(src, core))
-        recs.setdefault(XP[t + 1], []).append([True, 512 * h, 512 * h + 512, None, s, total[s], "remote"])
-
-    def send(t, h):
-        a, b = 1024 * t + 512 * h, 1024 * t + 512 * h + 512
-        deps("G", True, [("VV", a, b)], [])
+    def send(t, h, names):
         en = pairs(core, dst)
         mask = sum(1 << x for x in en)
         rid, pid, _ = topo.addr(dst)
-        g.remote_dma(out_ap=T[XP[t + 1]][:, 512 * h:512 * h + 512], in_ap=T.VV[:, a:b], remote_sem=T.sem["a%d%d" % (t, h)],
-                     local_sem=T.sem.loc, pid=pid, routing_id=rid, dma_engine_mask=mask)
-        total["loc"] = total.get("loc", 0) + len(en)
+        to = T[XP[t + 1]][:, 512 * h:512 * h + 512]
+        s = "a%d%d" % (t, h)
+        srcs = [T[nm][:, a:a + 512] for nm, a in names]
 
-    def out0(t):
-        tt(T.tm[:, 0:512], T.Et[:, :].indirect(T.el[:, 0:32]), T[XP[t]][:, 0:512], A.add,
-           [("Et",), ("el",), (XP[t], 0, 512)], [("tm", 0, 512)])
-        ts(T.mm[:, 0:512], T.tm[:, 0:512], 0.0, A.is_lt, [("tm", 0, 512)], [("mm", 0, 512)], 256.0, A.mult)
-        op("P", [mm(T.pb7[:, :], T.idB[:, :], T.tm[:, 0:512], True, False), mm(T.pb7[:, :], T.idB[:, :], T.mm[:, 0:512], False, True)],
-           [("tm", 0, 512), ("mm", 0, 512), ("idB",)], [("pb7",)])
+        def call():
+            if len(srcs) == 1:
+                g.remote_dma(out_ap=to, in_ap=srcs[0], remote_sem=T.sem[s], local_sem=T.sem.loc, pid=pid, routing_id=rid, dma_engine_mask=mask)
+            else:
+                g.remote_dma_fused([RemoteDMATransfer(dst_ids=[DstId(rid=rid, pnc=pid)], dma_engine_mask=mask, remote_sem=T.sem[s],
+                                                      srcs=srcs, dsts=[to], alu_op=1)], local_sem=T.sem.loc)
+            return len(en)
+        me = record("G", "send", call, 0.3, 0.3, [(nm, a, a + 512) for nm, a in names], [])
+        record("R", "arrival", len(pairs(src, core)), 0.001, REMOTE, [], [(XP[t + 1], 512 * h, 512 * h + 512)], s, [me])
 
-    def out0c(t):
-        act(T.VV[:, 1024 * t:1024 * t + 512], T.pb7[:, :], [("pb7",)], [("VV", 1024 * t, 1024 * t + 512)])
-        send(t, 0)
+    def outcome(t, h):
+        a, c, bank, X = 512 * h, 32 * h, IB[h], T[XP[t]]
+        top, xr = 2048 + 512 * t, (XP[t], a, a + 512)
+        l, r = nodes(h, 5)
+        b_ = ("bt", a, a + 512)
+        on_s = h == 1 and RB_ON_S[t]
+        if on_s:
+            gather("S", T.Rb[:, :], ("Rb",), T.Rt[:, 0:top], ("Rt", 0, top), l, r)
+            pe("pb6", [(T.pb6[:, :], T.idB[:, :], T.Rb[:, :]), (T.pb6[:, :], T.idN[:, :], X[:, a:a + 512])], [("Rb",), xr, ("idB",), ("idN",)])
+            act(T.bt[:, a:a + 512], T.pb6[:, :], [("pb6",)], [b_], func=AF.Sign, bias=-0.5)
+        else:
+            tt(T.bt[:, a:a + 512], T.Rt[:, 0:top].indirect(l), X[:, a:a + 512], A.is_gt, [("Rt", 0, top), r, xr], [b_], ind=GAT)
+        o = T[bank][:, 32:64]
+        pe(bank, [(o, T.id16[:, :], T.hs[:, c:c + 32])], [("id16",), ("hs", c, c + 32)], last=False)
+        Q = "Q48" if on_s else "Q97"
+        pe(bank, direct(o, 32, T[Q], T.bt, a), [b_, (Q,)], first=False)
+        ts(T.el[:, c:c + 32], o, 776.0 if on_s else 0.0, A.add, [(bank,)], [("el", c, c + 32)])
+        e, er = T.el[:, c:c + 32], ("el", c, c + 32)
+        m = 1024 * t + a
+        tm, tmr, mk, mkr = T.TM[:, m:m + 512], ("TM", m, m + 512), T.MM[:, m:m + 512], ("MM", m, m + 512)
+        if h == 1 and EB_ON_S[t]:
+            gather("S", tm, tmr, T.Et[:, :], ("Et",), e, er)
+            for bk, last in (("pb6", True), ("pb7", False)):
+                pe(bk, [(T[bk][:, :], T.idB[:, :], tm), (T[bk][:, :], T.idB[:, :], X[:, a:a + 512])], [tmr, xr, ("idB",)], last=last)
+            act(mk, T.pb6[:, :], [("pb6",)], [mkr], func=AF.Sign, bias=0.5)
+            pe("pb7", [(T.pb7[:, :], T.idS[:, :], mk)], [mkr, ("idS",)], first=False)
+            act(T.VV[:, 512 * t:512 * t + 512], T.pb7[:, :], [("pb7",)], [("VV", 512 * t, 512 * t + 512)], bias=128.0)
+            send(t, h, [("VV", 512 * t)])
+        else:
+            for u in (0, 256):
+                tt(T.TM[:, m + u:m + u + 256], T.Et[:, :].indirect(T.el[:, c + u // 16:c + u // 16 + 16]), X[:, a + u:a + u + 256], A.add,
+                   [("Et",), er, xr], [("TM", m + u, m + u + 256)], ind=GAT)
+                ts(T.MM[:, m + u:m + u + 256], T.TM[:, m + u:m + u + 256], 0.0, A.is_lt, [("TM", m + u, m + u + 256)], [("MM", m + u, m + u + 256)],
+                   256.0, A.mult)
+            send(t, h, [("TM", m), ("MM", m)])
 
-    def sums1(t, bank, stop):
-        op("P", [mm(T[bank][:, :], T.idB[:, :], T.tm[:, 512:1024], True, False),
-                 mm(T[bank][:, :], T.idB[:, :], T[XP[t]][:, 512:1024], False, stop)],
-           [("tm", 512, 1024), (XP[t], 512, 1024), ("idB",)], [(bank,)])
-
-    def out1a(t):
-        gather("S", T.tm[:, 512:1024], ("tm", 512, 1024), T.Et[:, :], ("Et",), T.el[:, 32:64], ("el",))
-        sums1(t, "pb3", True)
-
-    def out1b():
-        act(T.mm[:, 512:1024], T.pb3[:, :], [("pb3",)], [("mm", 512, 1024)], func=AF.Sign, bias=0.5)
-
-    def out1c(t):
-        op("P", mm(T.pb0[:, :], T.idS[:, :], T.mm[:, 512:1024], False, True), [("mm", 512, 1024), ("idS",)], [("pb0",)])
-        act(T.VV[:, 1024 * t + 512:1024 * t + 1024], T.pb0[:, :], [("pb0",)], [("VV", 1024 * t + 512, 1024 * t + 1024)], bias=128.0)
-        send(t, 1)
-
-    def eqs(c0, c1):
-        ms = []
-        for c in range(c0, c1):
+    def firsts(t):
+        top = 2048 + 512 * t
+        l0 = ("fl", 0, 16)
+        if t < 2:
+            act(T.depB[:, :], T.pb4[:, 0:256], [("pb4",)], [("depB",)])
+        gather("S", T.K5[:, :], ("K5",), T.Kt[:, 0:top], ("Kt", 0, top), T.fl[:, 0:16], l0)
+        u = 256 * t
+        gather("S", T.Rg[:, u:u + 256], ("Rg", u, u + 256), T.Rt[:, 0:top], ("Rt", 0, top), T.fl[:, 0:16], l0)
+        pe("pb4", [(T.pb4[:, 0:256], T.BDs[:, :], T.K5[:, :])], [("K5",), ("BDs",)])
+        cp(T.fru[:, :], T.pb4[:, 0:256], [("pb4",)], [("fru",)])
+        pe("pb5", [(T.pb5[:, 0:256], T.BDi[:, :], T.K5[:, :])], [("K5",), ("BDi",)], last=False)
+        for c in range(16):
             n = 256 - 16 * c
-            ts(T.E[:, 256 * c:256 * c + n], T.fru[:, 16 * c:256], T.pb1[:, c:c + 1], A.is_equal, [("fru",), ("pb1",), ("w16",)],
-               [("E", 256 * c, 256 * c + n)], T.w16[:, c:c + 1], A.mult)
-            ms.append(mm(T.pb5[:, 16 * c:256], T.BD[:, :], T.E[:, 256 * c:256 * c + n], c == 0, c == 15))
-        op("P", ms, [("E", 256 * c0, 256 * c1), ("BD",)], [("pb5",)])
+            e = ("E", 256 * c, 256 * c + n)
+            ts(T.E[:, 256 * c:256 * c + n], T.fru[:, 16 * c:256], T.pb0[:, 128 + c:129 + c], A.is_equal, [("fru",), ("pb0",), ("w16",)],
+               [e], T.w16[:, c:c + 1], A.mult)
+            pe("pb5", [(T.pb5[:, 16 * c:256], T.BD[:, :], T.E[:, 256 * c:256 * c + n])], [e, ("BD",)], False, c == 15)
+        tt(T.qB[:, :], T.pb5[:, 0:256], T.thrR[:, :], A.is_ge, [("pb5",), ("thrR",)], [("qB",)])
 
-    def rwrites1(t):
-        a = 1024 * t
-        op("P", [mm(T.pb7[:, 0:256], T.idH[:, :], T.Rg[:, :], True, False), mm(T.pb7[:, 0:256], T.idH[:, :], T.VV[:, a:a + 256], False, True)],
-           [("Rg",), ("VV", a, a + 256), ("idH",)], [("pb7",)])
-        n = 2048 + 512 * t
-        tt(T.Rt[:, n:n + 512:2], T.Rg[:, :], T.winB[:, :], A.mult, [("Rg",), ("winB",)], [("Rt", n, n + 512, "even")])
+    def lists(t):
+        if t < 2:
+            o = T.pb2[:, 80:96]
+            pe("pb2", [(o, T.idB[:, :], T.laneB[:, :])] + direct(o, 16, T.Q64, T.depB, 0), [("depB",), ("Q64",), ("idB",), ("laneB",)])
+            cp(T.depU[:, :], o, [("pb2",)], [("depU",)])
+            gather("S", T.xf[:, :], ("xf",), T[XP[t]][:, 0:NXP], (XP[t], 0, NXP), T.depU[:, :], ("depU",))
+        o = T.pb2[:, 64:80]
+        pe("pb2", to_list(0, o, 16), [("Fz0",), ("RQ",)], last=False)
+        pe("pb2", direct(o, 16, T.Q512, T.qB, 0), [("qB",), ("Q512",)], first=False)
+        tt(T.fo[:, :], o, T.dumpL[:, :], A.min, [("pb2",), ("dumpL",)], [("fo",)])
+        ts(T.offU[:, :], T.fo[:, :], float(OFF), A.add, [("fo",)], [("offU",)])
 
-    def rwrites2(t):
-        n = 2048 + 512 * t
-        ts(T.avI[:, :], T.pb7[:, 0:256], -0.25, A.add, [("pb7",)], [("avI",)])
-        tt(T.Rt[:, n + 1:n + 512:2], T.avI[:, :], T.winB[:, :], A.mult, [("avI",), ("winB",)], [("Rt", n, n + 512, "odd")])
+    def vterms(o, ident, t):
+        m = 1024 * t
+        return [(o, T[ident][:, :], T.TM[:, m:m + 256]), (o, T[ident][:, :], T.MM[:, m:m + 256])], [("TM", m, m + 256), ("MM", m, m + 256), (ident,)]
 
-    def ypn(t, xn):
-        block("pb2", 128, 64, T.QW, T[xn], [(xn, 0, 1024), ("QW",)])
-        cp(T.yI[:, :], T.pb2[:, 128:192], [("pb2",)], [("yI",)])
-        ts(T.yJ[:, :], T.yI[:, :], 1023, A.bitwise_and, [("yI",)], [("yJ",)])
-        ts(T.ypF[:, 64 * t:64 * t + 64], T.yJ[:, :], float(4096 + 1024 * (t - 1)), A.add, [("yJ",)], [("ypF", 64 * t, 64 * t + 64)])
-        dma("D", T.yp[:, 1024 * t:1024 * t + 1024], T.ypF[:, 64 * t:64 * t + 64], [("ypF", 64 * t, 64 * t + 64)], [])
+    def splits(t):
+        u = 256 * t
+        rg, rgr, win, winr = T.Rg[:, u:u + 256], ("Rg", u, u + 256), T.winB[:, u:u + 256], ("winB", u, u + 256)
+        new, newr = T.NEW[:, u:u + 256], ("NEW", u, u + 256)
+        d = T.pb4[:, 256:512]
+        if t < 2:
+            pe("pb4", [(d, T.idB[:, :], new), (d, T.idMn[:, :], T.K5[:, :])], [newr, ("K5",), ("idB",), ("idMn",)])
+            cp(T.Zt[:, :].indirect(T.offU[:, :]), T.xf[:, :], [("xf",), ("offU",)], [("Zt",)], n=256, ind=SCA)
+        else:
+            pe("pb4", [(T.pb4[:, 0:256], T.Mb[:, :], T.K5[:, :])], [("K5",), ("Mb",)])
+            act(T.old32[:, :], T.pb4[:, 0:256], [("pb4",)], [("old32",)])
+            pe("pb4", [(d, T.Mb[:, :], new), (d, T.MbN[:, :], T.K5[:, :])], [newr, ("K5",), ("Mb",), ("MbN",)])
+        o = T.pb1[:, 256:512]
+        terms, rd = vterms(o, "idN", t)
+        pe("pb1", [(o, T.idB[:, :], rg)] + terms, rd + [rgr, ("idB",)])
+        act(T.aB[:, :], o, [("pb1",)], [("aB",)], func=AF.Abs)
+        o = T.pb5[:, 256:512]
+        pe("pb5", [(o, T.idM[:, :], T.qB[:, :])], [("qB",), ("idM",)], last=False)
+        pe("pb5", [(o, T.BD[:, :], T.aB[:, :])], [("aB",), ("BD",)], first=False)
+        ts(win, o, thc, A.is_ge, [("pb5",), thr], [winr])
+        if t < 2:
+            tt(T.tK[:, :], d, win, A.mult, [("pb4",), winr], [("tK",)])
+            tt(T.Kt[:, :].indirect(T.offU[:, :]), T.K5[:, :], T.tK[:, :], A.add, [("K5",), ("tK",), ("offU",)], [("Kt",)], ind=SCA)
+        else:
+            tt(T.tK32[:, :], d, win, A.mult, [("pb4",), winr], [("tK32",)])
+            tt(T.Ko[:, :].indirect(T.offU[:, :]), T.old32[:, :], T.tK32[:, :], A.add, [("old32",), ("tK32",), ("offU",)], [("Ko",)], ind=SCA)
 
-    def yp0a():
-        ts(T.hK[:, :], T.hJ[:, :], 15, A.bitwise_and, [("hJ",)], [("hK",)])
-        ts(T.hM[:, :], T.hJ[:, :], 4, A.arith_shift_right, [("hJ",)], [("hM",)])
-        ts(T.hN[:, :], T.hK[:, :], 64.0, A.mult, [("hK",)], [("hN",)])
-        tt(T.hF[:, :], T.hN[:, :], T.hM[:, :], A.add, [("hN",), ("hM",)], [("hF",)])
-        cp(T.hp[:, :], T.hF[:, :], [("hF",)], [("hp",)])
-
-    def yp0b(h):
-        gather("S", T.Pg[:, 512 * h:512 * h + 512], ("Pg", 512 * h, 512 * h + 512), T.Ct[:, :], ("Ct",), T.hp[:, 32 * h:32 * h + 32], ("hp",))
-        if h == 1:
-            block("pb2", 192, 64, T.QP, T.Pg, [("Pg",), ("QP",)])
-
-    def yp0c():
-        cp(T.ypF[:, 0:64], T.pb2[:, 192:256], [("pb2",)], [("ypF", 0, 64)])
-        dma("D", T.yp[:, 0:1024], T.ypF[:, 0:64], [("ypF", 0, 64)], [])
+    def new_r(t):
+        u, n = 256 * t, 2048 + 512 * t
+        rg, rgr, win, winr = T.Rg[:, u:u + 256], ("Rg", u, u + 256), T.winB[:, u:u + 256], ("winB", u, u + 256)
+        o = T.pb7[:, 0:256]
+        pe("pb7", [(o, T.idB[:, :], rg), (o, T.idW[:, :], win)], [rgr, winr, ("idB",), ("idW",)])
+        act(T.Rt[:, n:n + 512:2], o, [("pb7",)], [("Rt", n, n + 512, "even")], func=AF.Relu, bias=-512.0)
+        o = T.pb6[:, 0:256]
+        terms, rd = vterms(o, "idH", t)
+        pe("pb6", [(o, T.idH[:, :], rg)] + terms + [(o, T.idW[:, :], win)], rd + [rgr, winr, ("idW",)])
+        ts(T.avI[:, :], o, -512.25, A.add, [("pb6",)], [("avI",)], 0.0, A.max)
+        cp(T.Rt[:, n + 1:n + 512:2], T.avI[:, :], [("avI",)], [("Rt", n, n + 512, "odd")])
+        dma("D", T.yr[:, 512 * t:512 * t + 512], T.Rt[:, n:n + 512], 512 * MB, [("Rt", n, n + 512)], [])
 
     for t in range(3):
-        XT = XP[t]
         if t == 0:
-            xg("S", 0, 0, 0, 512)
-            pgat(0, 1024)
-            psum(1024)
-            xg("V", 0, 0, 512, 1024)
+            for k in range(5):
+                for h in range(2):
+                    paths(0, h, k)
+                pred(k, 1024 if k < 4 else 256)
+            env_table()
+        for h in range(2):
+            hsum(t, h)
+        if t > 0:
+            for k in range(1, 5):
+                for h in range(2):
+                    paths(t, h, k)
+        if t < 2:
+            xg("S", t, 5, 0, 256)
         for k in range(5):
-            kid(0, k)
-            cmpz(t, 0, k)
-            pekids(0)
-            op("P", mm(T.pb3[:, 0:256], T.BDf1[:, :], T.Kg[:, 0:256], k == 0, k == 4), [("Kg", 0, 256), ("BDf1",)], [("pb3",)])
-            if t > 0 and k == 0:
-                hsum(t, 0)
-            pecnt(0)
-            if t == 0 and k > 0:
-                plist(k + 1, 1024 if k < 4 else 256)
-            kid(1, k)
-            cmpz(t, 1, k)
-            if t > 0 and k == 0:
-                hsum(t, 1)
-            pecnt(1)
-            pekids(1)
-            if k == 0:
-                if t == 0:
-                    late1()
-                    plist(1, 1024)
-                else:
-                    hlist()
-            if t == 0 and k < 4:
-                pgat(k + 1, 1024 if k < 3 else 256)
-                if NS0[k] < 1024:
-                    xg("V", 0, k + 1, NS0[k], 1024)
-                xg("S", 0, k + 1, 0, NS0[k])
-                if k == 0:
-                    late1b()
-                if k == 1:
-                    late3()
-                if k == 3:
-                    ts(T.Et[:, :], T.Et[:, :], -256.0, A.add, [("Et",)], [("Et",)])
-            elif k < 4:
-                xg("V", t, k + 1, NS1, 1024)
-                xg("S", t, k + 1, 0, NS1)
-            elif t < 2:
-                xg("S", t, 5, 0, 256)
-            if t == 2 and k == 4:
-                yp0b(0)
-            if t == 0 and k == 4:
-                late2()
-            ts(T.bs[0:64, :], T.pb6[0:64, 0:128], 8.5, A.is_ge, [("pb6",)], [("bs",)])
-            tt(T.ts[0:64, :], T.pb0[0:64, 128:256], T.bs[0:64, :], A.mult, [("pb0",), ("bs",)], [("ts",)])
-            tt(T.F[0:64, :], T.pb0[0:64, 0:128], T.ts[0:64, :], A.add, [("pb0",), ("ts",)], [("F",)])
-            op("P", lambda: g.tensor.transpose(T.pb1[:, 0:64], T.F[0:64, :], T.idF[0:64, 0:64]), [("F",), ("idF",)], [("pb1",)])
-            if t == 0 and k < 4:
-                psum(1024 if k < 3 else 256)
-            if t > 0:
-                if t == 1 and k == 4:
-                    late4()
-                if k == 1:
-                    rwrites1(t - 1)
-                if k == 2:
-                    rwrites2(t - 1)
-                if t == 1 and k == 1:
-                    yp0a()
-                if t == 2 and k == 3:
-                    ypn(1, "XC")
-            elif k == 4:
-                hsum(0, 0)
-                hsum(0, 1)
-                hlow()
-                hhigh()
-            cp(T.fl[:, :], T.pb1[:, 0:64], [("pb1",)], [("fl",)])
-        l0, l1 = ("fl", 0, 16), ("fl", 16, 64)
-        gather("S", T.Rg[:, :], ("Rg",), T.Rt[:, :], ("Rt",), T.fl[:, 0:16], l0)
-        tt(T.bt[:, 256:1024], T.Rt[:, :].indirect(T.fl[:, 16:64]), T[XT][:, 256:1024], A.is_gt, [("Rt",), l1, (XT, 256, 1024)], [("bt", 256, 1024)])
-        gather("S", T.K5[:, :], ("K5",), T.Kt[:, :], ("Kt",), T.fl[:, 0:16], l0)
-        op("P", [mm(T.pb7[:, 0:256], T.idB[:, :], T.Rg[:, :], True, False), mm(T.pb7[:, 0:256], T.idN[:, :], T[XT][:, 0:256], False, True)],
-           [("Rg",), (XT, 0, 256), ("idB",), ("idN",)], [("pb7",)])
-        op("P", [mm(T.pb4[:, 0:256], T.BDs[:, :], T.K5[:, :], True, True), mm(T.pb4[:, 256:512], T.BDf2[:, :], T.K5[:, :], True, True)],
-           [("K5",), ("BDs",), ("BDf2",)], [("pb4",)])
-        act(T.bt[:, 0:256], T.pb7[:, 0:256], [("pb7",)], [("bt", 0, 256)], func=AF.Sign, bias=-0.5)
-        direct("pb6", 16, 48, T.Q97, T.bt, 256, [("bt", 256, 1024), ("Q97",)])
-        direct("pb6", 0, 16, T.Q48, T.bt, 0, [("bt", 0, 256), ("Q48",)])
-        if t < 2:
-            act(T.depB[:, :], T.pb3[:, 0:256], [("pb3",)], [("depB",)])
-        cp(T.fru[:, :], T.pb4[:, 0:256], [("pb4",)], [("fru",)])
-        eqs(0, NE)
-        if t < 2:
-            direct("pb2", 0, 16, T.Q1k, T.depB, 0, [("depB",), ("Q1k",)])
-        ms = [mm(T.pb4[:, 0:256], T.DM[:, 0:128], T.NDa[:, :], True, False), mm(T.pb4[:, 0:256], T.DM[:, 128:256], T.NDc[:, :], False, False),
-              mm(T.pb4[:, 0:256], T.DM[:, 256:384], T.NDt[:, 256 * t:256 * t + 256], False, False),
-              mm(T.pb4[:, 0:256], T.DM[:, 384:512], T.NDe[:, :], False, False), mm(T.pb4[:, 0:256], T.idMn[:, :], T.K5[:, :], False, True)]
-        op("P", ms, [("DM",), ("idMn",), ("NDa",), ("NDc",), ("NDe",), ("NDt",), ("K5",)], [("pb4",)])
-        tt(T.ix0[:, :], T.pb6[:, 0:64], T.hsS[:, :], A.add, [("pb6",), ("hsS",)], [("ix0",)])
-        ts(T.iy0[:, :], T.ix0[:, :], 2047, A.bitwise_and, [("ix0",)], [("iy0",)])
-        cp(T.el[:, :], T.iy0[:, :], [("iy0",)], [("el",)])
-        out1a(t)
-        out0(t)
-        eqs(NE, 10)
-        eqs(10, 16)
-        out1b()
-        out0c(t)
-        v0 = ("VV", 1024 * t, 1024 * t + 256)
-        op("P", [mm(T.pb7[:, 0:256], T.idB[:, :], T.Rg[:, :], True, False), mm(T.pb7[:, 0:256], T.idN[:, :], T.VV[:, 1024 * t:1024 * t + 256], False, True)],
-           [("Rg",), v0, ("idB",), ("idN",)], [("pb7",)])
-        act(T.aB[:, :], T.pb7[:, 0:256], [("pb7",)], [("aB",)], func=AF.Abs)
-        sums1(t, "pb0", False)
-        out1c(t)
-        if t < 2:
-            tt(T.dO[:, :], T.pb2[:, 0:16], T.laneL[:, :], A.add, [("pb2",), ("laneL",)], [("dO",)])
-        tt(T.fd[:, :], T.pb1[:, 0:16], T.dumpL[:, :], A.subtract, [("pb1",), ("dumpL",)], [("fd",)])
-        if t < 2:
-            cp(T.depU[:, :], T.dO[:, :], [("dO",)], [("depU",)])
-            gather("S", T.xf[:, :], ("xf",), T[XT][:, 0:NXP], (XT, 0, NXP), T.depU[:, :], ("depU",))
-        tt(T.qB[:, :], T.pb5[:, 0:256], T.thrR[:, :], A.is_ge, [("pb5",), ("thrR",)], [("qB",)])
-        op("P", mm(T.pb5[:, 256:512], T.BD[:, :], T.aB[:, :], True, True), [("aB",), ("BD",)], [("pb5",)])
-        tt(T.flB[:, :], T.pb4[:, 256:512], T.qB[:, :], A.is_equal, [("pb4",), ("qB",)], [("flB",)])
-        direct("pb6", 64, 16, T.QS, T.flB, 0, [("flB",), ("QS",)])
-        ts(T.thx[:, :], T.flB[:, :], C["thm"][0], A.mult, [("flB",), C["thm"][1]], [("thx",)], 1048576.0, A.add)
-        tt(T.winB[:, :], T.pb5[:, 256:512], T.thx[:, :], A.is_ge, [("pb5",), ("thx",)], [("winB",)])
-        tt(T.fo[:, :], T.pb6[:, 64:80], T.fd[:, :], A.mult, [("pb6",), ("fd",)], [("fo",)])
-        tt(T.tK[:, :], T.pb4[:, 0:256], T.winB[:, :], A.mult, [("pb4",), ("winB",)], [("tK",)])
-        tt(T.fp[:, :], T.fo[:, :], T.dumpL[:, :], A.add, [("fo",), ("dumpL",)], [("fp",)])
-        cp(T.offU[:, :], T.fp[:, :], [("fp",)], [("offU",)])
-        tt(T.Kt[:, :].indirect(T.offU[:, :]), T.K5[:, :], T.tK[:, :], A.add, [("K5",), ("tK",), ("offU",)], [("Kt",)])
-        if t < 2:
-            cp(T.Zt[:, :].indirect(T.offU[:, :]), T.xf[:, :], [("xf",), ("offU",)], [("Zt",)])
-        arrived(t, 0)
-        arrived(t, 1)
-    rwrites1(2)
-    rwrites2(2)
-    dma("D", T.yr[:, :], T.Rt[:, 2048:3584], [("Rt", 2048, 3584)], [])
-    ypn(2, "XF")
-    block("pb3", 0, 224, T.QKK, T.Kt, [("Kt",), ("QKK",)])
-    cp(T.yA[:, :], T.pb3[:, 0:224], [("pb3",)], [("yA",)])
-    ts(T.yB[:, :], T.yA[:, :], 4095, A.bitwise_and, [("yA",)], [("yB",)])
-    ts(T.yC[:, :], T.yA[:, :], 12, A.arith_shift_right, [("yA",)], [("yC",)])
-    cp(T.ykA[:, :], T.yB[:, :], [("yB",)], [("ykA",)])
-    cp(T.ykB[:, :], T.yC[:, :], [("yC",)], [("ykB",)])
-    dma("D", T.yk0[:, :], T.ykA[:, :], [("ykA",)], [])
-    dma("D", T.yk1[:, :], T.ykB[:, :], [("ykB",)], [])
-    yp0b(1)
-    yp0c()
-    for s in total:
-        if seen.get(("G", s), 0) < total[s]:
-            g.wait_ge(T.sem[s], total[s])
+            for h in range(2):
+                step(t, h, k)
+        if t == 0:
+            new_nodes()
+        if t == 1:
+            for h in range(2):
+                gather("S", T.Cg[:, 512 * h:512 * h + 512], ("Cg", 512 * h, 512 * h + 512), T.Ct[:, :], ("Ct",), T.hl[:, 32 * h:32 * h + 32],
+                       ("hl", 32 * h, 32 * h + 32))
+            dma("D", T.yp[:, 0:1024], T.Cg[0:128:16, :], 32768, [("Cg",)], [])
+        if t == 2:
+            ts(T.hF[:, :], T.hJ[:, 64:128], 4096.0, A.add, [("hJ", 64, 128)], [("hF",)])
+            turn(T.hF[:, :], ("hF",), "hT", lambda e, a: T.yp[e:8:2, a:a + 512], None, 1024)
+            dma("G", T.Ko[:, :], T.Kt[:, 0:3840], 3840 * 512, [("Kt",)], [("Ko",)])
+            for i in (0, 2):
+                dma("G", T.Ko[i:128:16, 0:3584], T.Kt[i + 1:128:16, 0:3584], 3584 * 64, [("Kt",)], [("Ko", 0, 3840, "r%d" % i)],
+                    accum_op=A.add, max_dma_last_dim=4096)
+        firsts(t)
+        outcome(t, 0)
+        lists(t)
+        outcome(t, 1)
+        splits(t)
+        new_r(t)
+    dma("D", T.yk0[:, :], T.Ko[0:128:16, 0:3584], 114688, [("Ko",)], [])
+    dma("S", T.yk1[:, :], T.Ko[2:128:16, 0:3584], 114688, [("Ko",)], [])
+    pe("pb3", block(T.pb3[:, 128:192], 64, T.QW, T.XF), [("XF",), ("QW",)])
+    cp(T.yI[:, :], T.pb3[:, 128:192], [("pb3",)], [("yI",)])
+    ts(T.yJ[:, :], T.yI[:, :], 1023, A.bitwise_and, [("yI",)], [("yJ",)])
+    ts(T.ypF[:, :], T.yJ[:, :], 5120.0, A.add, [("yJ",)], [("ypF",)])
+    dma("D", T.yp[:, 2048:3072], T.ypF[:, :], 32768, [("ypF",)], [])
+    emit()

@@ -4,10 +4,20 @@ from concourse.mybir import dt, AluOpType, AxisListType, ActivationFunctionType
 
 A = AluOpType
 AF = ActivationFunctionType
-XS = ((256, 256), (416, 416), (416, 416))
-PS = 1024
-RB_ON_S = (True, True, True)
-EB_ON_S = (True, True, True)
+PARTS = ((0, 512), (512, 512))
+IB = ("pb2", "pb3")
+LB = "pb2"
+XS = ((384, 384), (448, 448), (448, 448))
+BOTH, ALONE = ((("S", 0, 512), ("V", 512, 1024)),), ((("S", 0, 512), ("S", 512, 1024)),)
+PRED = (BOTH, BOTH, BOTH, BOTH, BOTH)
+R_ON_S = ((), (), ())
+E_ON_S = ((), (), ())
+LEAD = 0.0
+XFIRST = 2048
+PASSES = 4
+NOISE, FIN, SLACK = 0.0, 1.0, 0.5
+PLAN = []
+BIG = 65536.0
 NXP = 5 * 1024 + 256
 OFF = 1792
 EW = 3600
@@ -20,22 +30,22 @@ def _sb(dtype, text):
         SCRATCH[n] = ("sbuf", [128, int(c)], dtype)
 
 
-_sb("bfloat16", "xs:4096 Kt:4096 Zt:3840 Rt:3584 Et:3600 XA:5376 XB:5376 XC:5376 XF:1024 TM:3072 MM:3072 VV:1536 Pg:1024 Kg:1024 "
-    "bt:1024 Rb:512 K5:256 Rg:768 aB:256 E:4096 qB:256 winB:768 tK:256 xf:256 depB:256 NDlo:128 NEW:768 bs:64 "
+_sb("bfloat16", "xs:4096 Pt:4096 Kt:4096 Zt:3840 Rt:3584 Et:3600 XA:5376 XB:5376 XC:5376 XF:1024 TM:3072 MM:3072 VV:3072 Pg:1024 Kg:1024 "
+    "bt:1024 Rb:1024 K5:256 Rg:768 aB:256 E:4096 qB:256 winB:768 tK:256 xf:256 depB:256 NDlo:128 NEW:768 SC:96 "
     "ones:256 zer:144 Qa:144 Qb:144 Q01:144 QP:144 QW:144 Q97:144 Q48:144 Q64:144 Q512:144 W1:8 WK:16 RQb:128 BD:128 BDs:128 BDi:128 "
     "BDf:128 idB:128 idN:128 idH:128 idS:128 idM:128 idW:128 idMn:128 Mb:128 MbN:128 dg:640 pg:512 sfl:256 sfi:256 laneB:16")
 _sb("float16", "RQ:128 id16:128 hs:64 fru:256")
-_sb("float32", "onesF:128 BDF:128 ts:64 w16:16 thrR:256 laneL:16 dumpL:16 fo:16 col:32 thF:1 ypF:64 curF:64 curT:64 hF:64 hT:64 "
+_sb("float32", "onesF:128 BDF:128 sc:288 fL:16 w16:16 thrR:256 laneL:16 dumpL:16 fo:16 col:32 thF:1 ypF:64 curF:64 curT:64 hF:64 hT:64 "
     "Ct:1024 Cg:1024 Ko:3840 old32:256 tK32:256")
 _sb("int32", "prevI:256 kI:256 kH:256 curI:64 startI:64 wI:1 thI:1 pI:1 pmI:1 pnI:1 ownI:128 own2:128 hI:64 hJ:128 hK:64 yI:64 yJ:64 avI:256")
 _sb("uint16", "f0:64 fl:64 sl:384 hl:128 el:64 offU:16 depU:16")
-for _h in range(2):
+for _h in range(3):
     SCRATCH["Fz%d" % _h] = ("sbuf", [128, 36, 4], "float16")
 for _i in range(8):
     SCRATCH["pb%d" % _i] = ("psum", [128, 512], "float32")
 
 NDMA = 64
-SEMAPHORES = ["sV", "sS", "sP", "sG", "loc"] + ["d%d" % i for i in range(NDMA)] + ["a%d%d" % (t, c) for t in range(3) for c in range(2)]
+SEMAPHORES = ["sV", "sS", "sP", "sG", "loc"] + ["d%d" % i for i in range(NDMA)] + ["a%d%d" % (t, c) for t in range(3) for c in range(3)]
 
 CYC, PEC, GAT, SCA, HAND, DMA0, DMAB, REMOTE = 0.00083, 0.00042, 1.4, 3.0, 0.14, 1.2, 1 / 350e3, 2.6
 WIDTH = {"bfloat16": 2, "float16": 2, "uint16": 2, "float32": 4, "int32": 4}
@@ -100,6 +110,7 @@ def rank_program(g, core, T, topo):
         return record(q, "op", calls, cost, cost + (0.06 if q == "P" else 0), reads, writes)
 
     ndma = [0]
+    lead = []
 
     def dma(q, out, in_, nbytes, reads, writes, after=(), **kw):
         s = "d%d" % ndma[0]
@@ -117,25 +128,59 @@ def rank_program(g, core, T, topo):
             return ops[p][4] + HAND if ops[i][5][p] else ops[p][3]
         level = [0.0] * n
         for i in range(n - 1, -1, -1):
-            level[i] = max([gap(i, j) + level[j] for j in succ[i]] + [ops[i][4]])
-        start = [0.0] * n
-        taken = {}
-        for i in sorted(range(n), key=lambda i: (-level[i], i)):
-            t = max([start[p] + gap(p, i) for p in ops[i][5]] + [0.0])
-            uses = [(ops[i][0], 0.0, ops[i][3])]
-            if ops[i][1] == "dma":
-                uses.append(("engines", DMA0, ops[i][4]))
-            moved = True
-            while moved:
-                moved = False
+            level[i] = max([gap(i, j) + level[j] for j in succ[i]] + [ops[i][4] + (LEAD if i in lead else 0)])
+
+        def place(order, back):
+            at, taken = [0.0] * n, {}
+            for i in order:
+                if back:
+                    t = max([at[j] + gap(i, j) for j in succ[i]] + [ops[i][4]])
+                else:
+                    t = max([at[p] + gap(p, i) for p in ops[i][5]] + [0.0])
+                uses = [(ops[i][0], 0.0, ops[i][3])]
+                if ops[i][1] == "dma":
+                    uses.append(("engines", DMA0, ops[i][4]))
+                if back:
+                    uses = [(q, -hi, -lo) for q, lo, hi in uses]
+                moved = True
+                while moved:
+                    moved = False
+                    for q, lo, hi in uses:
+                        for a, b in taken.setdefault(q, []):
+                            if a >= t + hi:
+                                break
+                            if t + lo < b - 1e-9 and t + hi > a + 1e-9:
+                                t, moved = b - lo, True
                 for q, lo, hi in uses:
-                    for a, b in taken.setdefault(q, []):
-                        if t + lo < b - 1e-9 and t + hi > a + 1e-9:
-                            t, moved = b - lo, True
-            for q, lo, hi in uses:
-                taken[q].append((t + lo, t + hi))
-                taken[q].sort()
-            start[i] = t
+                    taken[q].append((t + lo, t + hi))
+                    taken[q].sort()
+                at[i] = t
+            return at
+
+        def length(at):
+            return max(at[i] + ops[i][4] for i in range(n))
+
+        def ranked(key, back):
+            key = list(key)
+            for i in (range(n) if back else range(n - 1, -1, -1)):
+                for j in (ops[i][5] if back else succ[i]):
+                    key[i] = max(key[i], key[j] + 1e-6)
+            return sorted(range(n), key=lambda i: -key[i])
+        start = best = place(ranked(level, False), False)
+        seed = [1]
+
+        def noise():
+            seed[0] = (seed[0] * 1103515245 + 12345) % 2147483648
+            return (seed[0] / 2147483648 - 0.5) * NOISE
+        for _ in range(PASSES):
+            late = place(ranked([start[i] + FIN * ops[i][4] + noise() for i in range(n)], True), True)
+            start = place(ranked([late[i] + noise() for i in range(n)], False), False)
+            if length(start) < length(best):
+                best = start
+            elif length(start) > length(best) + SLACK:
+                start = best
+        start = best
+        PLAN[:] = [(length(best), max(level), ops, level, start)]
         total, seen, mark = {}, {}, {}
         for i in sorted(range(n), key=lambda i: (start[i], i)):
             q, kind, calls, _, _, pred, sem = ops[i]
@@ -244,21 +289,24 @@ def rank_program(g, core, T, topo):
              dma("D", T.kI[:, 128:256], T.kid1[:, :], 65536, [], [("kI", 128, 256)]),
              dma("S", T.curI[:, :], T.cur[:, :], 32768, [], [("curI",)]),
              dma("D", T.startI[:, :], T.start[:, :], 32768, [], [("startI",)])]
-    big = dma("S", T.xs[:, :], T.x[:, :], 4096 * MB, [], [("xs",)], small)
-    dma("D", T.Zt[:, 0:2048], T.z[:, :], 2048 * MB, [], [("Zt", 0, 2048)], small + [big])
-    dma("S", T.wI[:, :], T.w[:, :], 512, [], [("wI",)], [big])
+    big = dma("D", T.xs[:, 0:XFIRST], T.x[:, 0:XFIRST], XFIRST * MB, [], [("xs", 0, XFIRST)], small)
+    dma("S", T.wI[:, :], T.w[:, :], 512, [], [("wI",)], small)
 
     fill("ones", 0, 256, 1.0)
     fill("zer", 0, 144, 0.0)
     for a in range(0, 4096, 1024):
-        fill("Kt", a, a + 1024, 1.0)
-    for h in range(2):
+        fill("Pt", a, a + 1024, 1.0)
+    for a in (0, 1024):
+        act(T.Kt[:, a:a + 1024], T.Pt[:, a:a + 1024], [("Pt", a, a + 1024)], [("Kt", a, a + 1024)])
+    for h in range(len(PARTS)):
         cp(T["Fz%d" % h][:, :, :], T.zer[:, :], [("zer",)], [("Fz%d" % h,)])
+    for j, v in enumerate((1, 8, -9)):
+        op("V", lambda j=j, v=v: V.memset(T.SC[:, j:96:3], v * BIG), 0.07, [], [("SC", 0, 96, "c%d" % j)])
     GR = [-16, 8]
     sel("W1", "ones", 8, [GR], A.is_ge, 0, 0, 1)
     sel("W1", "W1", 8, [[16, 8]], A.is_ge, 0, 15, -1)
-    sel("WK", "zer", 16, [[2, 2], GR], A.is_ge, 1, -4, 1)
-    sel("WK", "WK", 16, [[2, 2], GR], A.is_ge, -1, -2, 1)
+    for j, (half, below, v) in enumerate(((0, 4, -1 / BIG), (1, 4, -8), (0, 2, 1 / BIG), (1, 2, 9))):
+        sel("WK", "WK" if j else "zer", 16, [[1000 - 2000 * half, 2], GR], A.is_ge, v, 1000 * half - below, 1)
     sel("WK", "WK", 16, [[0, 2], GR], A.is_ge, 0, 0, 1)
     sel("WK", "WK", 16, [[1000, 2], GR], A.not_equal, -OFF, -1013, 1)
     sel("Qa", "ones", 144, [[0, 9], [1, 16]], A.is_equal, 0, -15, 0)
@@ -275,6 +323,8 @@ def rank_program(g, core, T, topo):
     for nm, v in (("idB", 1), ("idN", -1), ("idH", 0.5), ("idS", -128), ("idM", -8192), ("idW", 512)):
         sel(nm, "zer", 128, [[-1, 128]], A.not_equal, v, 0, 1)
     cp(T.id16[:, :], T.idB[:, :], [("idB",)], [("id16",)])
+    for h in range(len(PARTS)):
+        pe("pb%d" % h, [(T["pb%d" % h][:, 1:96:3], T.idN[:, :], T.ones[:, 0:32])], [("idN",), ("ones",)])
     sel("Mb", "idB", 128, [[-1, 128]], A.not_equal, 1, -1, 1)
     sel("MbN", "idN", 128, [[-1, 128]], A.not_equal, -1, -1, 1)
     PL = [GR, [0, 16]]
@@ -292,15 +342,19 @@ def rank_program(g, core, T, topo):
     cp(T.sl[:, 0:64], T.curI[:, :], [("curI",)], [("sl", 0, 64)])
     cp(T.pg[:, 0:256], T.prevI[:, :], [("prevI",)], [("pg", 0, 256)])
     tt(T.pg[:, 256:512], T.prevI[:, :], T.pg[:, 0:256], A.subtract, [("prevI",), ("pg", 0, 256)], [("pg", 256, 512)])
-    for j in range(2):
-        dma("D", T.Kt[14 + j:128:16, :], T.pg[:, 256 * j:256 * j + 256], 65536, [("pg", 256 * j, 256 * j + 256)], [("Kt", 0, 4096, "r%d" % (14 + j))])
+    rows = [dma("D", T.Pt[14 + j:128:16, :], T.pg[:, 256 * j:256 * j + 256], 65536, [("pg", 256 * j, 256 * j + 256)],
+                [("Pt", 0, 4096, "r%d" % (14 + j))], [big]) for j in range(2)]
     ts(T.kH[:, :], T.kI[:, :], 0xF00, A.bitwise_and, [("kI",)], [("kH",)])
     cp(T.dg[:, 0:256], T.kH[:, :], [("kH",)], [("dg", 0, 256)])
     tt(T.dg[:, 256:512], T.kI[:, :], T.kH[:, :], A.subtract, [("kI",), ("kH",)], [("dg", 256, 512)])
     ts(T.own2[:, :], T.ownI[:, :], 2047, A.bitwise_and, [("ownI",)], [("own2",)])
     tt(T.dg[:, 512:640], T.kI[:, 0:128], T.own2[:, :], A.not_equal, [("kI", 0, 128), ("own2",)], [("dg", 512, 640)])
     for i, j in ((0, 0), (1, 2), (2, 1), (3, 3), (4, 4)):
-        dma("DS"[i % 2], T.Kt[i:128:16, 0:2048], T.dg[:, 128 * j:128 * j + 128], 32768, [("dg", 128 * j, 128 * j + 128)], [("Kt", 0, 2048, "r%d" % i)])
+        rows.append(dma("D", T.Kt[i:128:16, 0:2048], T.dg[:, 128 * j:128 * j + 128], 32768, [("dg", 128 * j, 128 * j + 128)],
+                        [("Kt", 0, 2048, "r%d" % i)], [big]))
+    if XFIRST < 4096:
+        rows.append(dma("D", T.xs[:, XFIRST:4096], T.x[:, XFIRST:4096], (4096 - XFIRST) * MB, [], [("xs", XFIRST, 4096)], rows))
+    dma("D", T.Zt[:, 0:2048], T.z[:, :], 2048 * MB, [], [("Zt", 0, 2048)], rows)
 
     pm, pmr = column("pm")
     ts(T.pmI[:, :], T.pI[:, :], 15, A.bitwise_and, [("pI",)], [("pmI",)])
@@ -347,6 +401,7 @@ def rank_program(g, core, T, topo):
     def env_table():
         dma("D", T.Rt[:, 0:2048], T.rs[:, :], 2048 * MB, gate, [("Rt", 0, 2048)])
         dma("D", T.Zt[:, 2048:3840], T.z[:, 0:1792], 1792 * MB, gate, [("Zt", 2048, 3840)])
+        dma("D", T.Kt[:, 2048:4096], T.Pt[:, 0:2048], 2048 * MB, gate + [("Pt", 0, 2048)], [("Kt", 2048, 4096)])
         for a in (900, 1800, 2700):
             dma("D", T.Et[:, a:a + 900], T.Et[:, 0:900], 900 * MB, [("Et", 0, 900)] + gate, [("Et", a - 4, a + 904)])
         dma("G", T.Et[:, 0:2048], T.env[:, :], 2048 * MB * 2, [], [("Et", 0, 2048)], accum_op=A.add)
@@ -372,33 +427,39 @@ def rank_program(g, core, T, topo):
     turn(T.curF[:, :], ("curF",), "curT", lambda e, a: T.Ct[16 * e:128:32, a:a + 512], ("Ct", 0, 1024), 0)
 
     XP = ["XA", "XB", "XC", "XF"]
-    IB = ["pb2", "pb3"]
 
-    def nodes(h, k):
-        nm = "f0" if k == 0 else "fl"
-        return T[nm][:, 32 * h:32 * h + 32], (nm, 32 * h, 32 * h + 32)
+    def cols(name, h, base=0):
+        a, n = PARTS[h]
+        lo, hi = base + a // 16, base + (a + n) // 16
+        return T[name][:, lo:hi], (name, lo, hi)
+
+    def lanes(name, h, base=0):
+        a, n = PARTS[h]
+        return T[name][:, base + a:base + a + n], (name, base + a, base + a + n)
 
     def to_list(h, out, n):
-        return [(out, T["Fz%d" % h][:, 3 - q:35 - q, :], T.RQ[:, 32 * q:32 * q + n]) for q in range(4)]
+        m = PARTS[h][1] // 4
+        return [(out, T["Fz%d" % h][0:m, 3 - q:35 - q, :], T.RQ[0:m, 32 * q:32 * q + n]) for q in range(4)]
 
     def step(t, h, k):
-        l, r = nodes(h, k)
-        a, top, bank = 512 * h, 2048 + 512 * t, "pb%d" % h
-        pb, F = T[bank], "Fz%d" % h
-        kg, b_ = ("Kg", a, a + 512), ("bt", a, a + 512)
-        act(T.Kg[:, a:a + 512], T.Kt[:, 0:top].indirect(l), [("Kt", 0, top), r], [kg], ind=GAT)
-        x = 1024 * k + a
-        tt(T.bt[:, a:a + 512], T.Zt[:, 0:top].indirect(l), T[XP[t]][:, x:x + 512], A.is_le, [("Zt", 0, top), r, (XP[t], x, x + 512)], [b_], ind=GAT)
-        pe(bank, [(pb[:, 32 + j:96:4], T.Kg[:, a + j:a + 512:4], T.WK[:, :]) for j in range(4)], [kg, ("WK",)], alone=True)
-        pe(bank, [(pb[:, j:32:4], T.bt[:, a + j:a + 512:4], T.W1[:, :]) for j in range(4)], [b_, ("W1",)], alone=True)
+        l, r = cols("fl" if k else "f0", h)
+        (a, n), top, bank = PARTS[h], 2048 + 512 * t, "pb%d" % h
+        pb, F, m = T[bank], "Fz%d" % h, n // 4
+        (kg, kgr), (bt, btr), (x, xr) = lanes("Kg", h), lanes("bt", h), lanes(XP[t], h, 1024 * k)
+        act(kg, T.Kt[:, 0:top].indirect(l), [("Kt", 0, top), r], [kgr], ind=GAT)
+        tt(bt, T.Zt[:, 0:top].indirect(l), x, A.is_le, [("Zt", 0, top), r, xr], [btr], ind=GAT)
+        pe(bank, [(pb[0:m, 3 * j + 2:192:12], T.Kg[:, a + j:a + n:4], T.WK[:, :]) for j in range(4)], [kgr, ("WK",)], alone=True)
+        pe(bank, [(pb[0:m, 3 * j:96:12], T.bt[:, a + j:a + n:4], T.W1[:, :]) for j in range(4)], [btr, ("W1",)], alone=True)
         if h == 0 and t < 2:
             pe("pb4", [(T.pb4[:, 0:256], T.BDf[:, :], T.Kg[:, 0:256])], [("Kg", 0, 256), ("BDf",)], k == 0, k == 4)
-        c = 32 * h
-        ts(T.bs[:, c:c + 32], pb[:, 0:32], 8.5, A.is_ge, [(bank,)], [("bs", c, c + 32)])
-        tt(T.ts[:, c:c + 32], pb[:, 32:64], T.bs[:, c:c + 32], A.mult, [(bank,), ("bs", c, c + 32)], [("ts", c, c + 32)])
-        tt(T[F][:, 3:35:4, :], pb[:, 64:96], T.ts[:, c:c + 32], A.add, [(bank,), ("ts", c, c + 32)], [(F,)])
-        pe(bank, to_list(h, pb[:, 128:160], 32), [(F,), ("RQ",)])
-        ts(T.fl[:, c:c + 32], pb[:, 128:160], float(OFF), A.add, [(bank,)], [("fl", c, c + 32)])
+        c, scr = 96 * h, ("sc", 96 * h, 96 * h + 96)
+        op("V", lambda: V.tensor_tensor_scan(T.sc[0:m, c:c + 96], T.SC[0:m, :], pb[0:m, 0:96], 0.0, A.max, A.mult), 0.05 + 96 * CYC,
+           [("SC",), (bank,)], [scr])
+        tt(T[F][0:m, 3:35:4, :], pb[0:m, 98:192:3], T.sc[0:m, c + 2:c + 96:3], A.add, [(bank,), scr], [(F,)])
+        o = pb[:, 192:192 + n // 16]
+        pe(bank, to_list(h, o, n // 16), [(F,), ("RQ",)])
+        l, r = cols("fl", h)
+        ts(l, o, float(OFF), A.add, [(bank,)], [r])
 
     def xg(eng, t, k, a, b):
         if a >= b:
@@ -413,37 +474,42 @@ def rank_program(g, core, T, topo):
             gather(eng, out, outr, T[XP[t - 1]][:, w:w + 1024], (XP[t - 1], w, w + 1024), T.hl[:, lo:hi], ("hl", lo, hi))
 
     def paths(t, h, k):
-        a = 512 * h
+        a, n = PARTS[h]
         xg("S", t, k, a, a + XS[t][h])
-        xg("V", t, k, a + XS[t][h], a + 512)
+        xg("V", t, k, a + XS[t][h], a + n)
 
     def pred(k, n):
-        for eng, a, b in (("S", 0, min(n, 512, PS)), ("S", 512, min(n, PS)), ("V", PS, n)):
+        for j, who in enumerate(PRED[k]):
+            for eng, a, b in who:
+                if a < min(b, n):
+                    b = min(b, n)
+                    lo, hi = 64 * k + a // 16, 64 * k + b // 16
+                    gather(eng, T.Pg[:, a:b], ("Pg", a, b), T.Pt[:, :], ("Pt",), T.sl[:, lo:hi], ("sl", lo, hi))
+            a, b, bank = who[0][1], min(who[-1][2], n), "pb%d" % (7 - j)
             if a < b:
-                lo, hi = 64 * k + a // 16, 64 * k + b // 16
-                gather(eng, T.Pg[:, a:b], ("Pg", a, b), T.Kt[:, :], ("Kt",), T.sl[:, lo:hi], ("sl", lo, hi))
-        m = n // 16
-        pe("pb7", direct(T.pb7[:, 0:m], m, T.QP, T.Pg, 0), [("Pg", 0, n), ("QP",)])
-        cp(T.sl[:, 64 * k + 64:64 * k + 64 + m], T.pb7[:, 0:m], [("pb7",)], [("sl", 64 * k + 64, 64 * k + 64 + m)])
+                m, lo = (b - a) // 16, 64 * k + 64 + a // 16
+                pe(bank, direct(T[bank][:, 0:m], m, T.QP, T.Pg, a), [("Pg", a, b), ("QP",)])
+                cp(T.sl[:, lo:lo + m], T[bank][:, 0:m], [(bank,)], [("sl", lo, lo + m)])
 
     def hsum(t, h):
-        c, bank = 32 * h, IB[h]
-        pe(bank, direct(T[bank][:, 0:32], 32, T.QW, T[XP[t]], 512 * h), [(XP[t], 512 * h, 512 * h + 512), ("QW",)])
-        cp(T.hI[:, c:c + 32], T[bank][:, 0:32], [(bank,)], [("hI", c, c + 32)])
-        if t > 0:
-            d = 64 * (t - 1) + c
-            ts(T.hJ[:, d:d + 32], T.hI[:, c:c + 32], 1023, A.bitwise_and, [("hI", c, c + 32)], [("hJ", d, d + 32)])
-            cp(T.hl[:, d:d + 32], T.hJ[:, d:d + 32], [("hJ", d, d + 32)], [("hl", d, d + 32)])
-        ts(T.hK[:, c:c + 32], T.hI[:, c:c + 32], 2047, A.bitwise_and, [("hI", c, c + 32)], [("hK", c, c + 32)])
-        cp(T.hs[:, c:c + 32], T.hK[:, c:c + 32], [("hK", c, c + 32)], [("hs", c, c + 32)])
+        (a, n), bank = PARTS[h], IB[h]
+        o = T[bank][:, 224:224 + n // 16]
+        pe(bank, direct(o, n // 16, T.QW, T[XP[t]], a), [lanes(XP[t], h)[1], ("QW",)])
+        hi, hir = cols("hI", h)
+        cp(hi, o, [(bank,)], [hir])
+        for want, bits, mid, out, base in ((t > 0, 1023, "hJ", "hl", 64 * t - 64), (True, 2047, "hK", "hs", 0)):
+            if want:
+                (u, ur), (w, wr) = cols(mid, h, base), cols(out, h, base)
+                ts(u, hi, bits, A.bitwise_and, [hir], [ur])
+                cp(w, u, [ur], [wr])
 
     def send(t, h, names):
         en = pairs(core, dst)
         mask = sum(1 << x for x in en)
         rid, pid, _ = topo.addr(dst)
-        to = T[XP[t + 1]][:, 512 * h:512 * h + 512]
+        to, tor = lanes(XP[t + 1], h)
         s = "a%d%d" % (t, h)
-        srcs = [T[nm][:, a:a + 512] for nm, a in names]
+        srcs = [lanes(nm, h, 1024 * t)[0] for nm in names]
 
         def call():
             if len(srcs) == 1:
@@ -452,44 +518,42 @@ def rank_program(g, core, T, topo):
                 g.remote_dma_fused([RemoteDMATransfer(dst_ids=[DstId(rid=rid, pnc=pid)], dma_engine_mask=mask, remote_sem=T.sem[s],
                                                       srcs=srcs, dsts=[to], alu_op=1)], local_sem=T.sem.loc)
             return len(en)
-        me = record("G", "send", call, 0.3, 0.3, [(nm, a, a + 512) for nm, a in names], [])
-        record("R", "arrival", len(pairs(src, core)), 0.001, REMOTE, [], [(XP[t + 1], 512 * h, 512 * h + 512)], s, [me])
+        me = record("G", "send", call, 0.3, 0.3, [lanes(nm, h, 1024 * t)[1] for nm in names], [])
+        record("R", "arrival", len(pairs(src, core)), 0.001, REMOTE * (0.5 + PARTS[h][1] / 1024), [], [tor], s, [me])
 
     def outcome(t, h):
-        a, c, bank, X = 512 * h, 32 * h, IB[h], T[XP[t]]
-        top, xr = 2048 + 512 * t, (XP[t], a, a + 512)
-        l, r = nodes(h, 5)
-        b_ = ("bt", a, a + 512)
-        on_s = h == 1 and RB_ON_S[t]
+        (a, n), bank, X, top = PARTS[h], IB[h], T[XP[t]], 2048 + 512 * t
+        (l, r), (x, xr), (bt, btr) = cols("fl", h), lanes(XP[t], h), lanes("bt", h)
+        on_s = h in R_ON_S[t]
+        p6, p7 = T.pb6[:, 0:n], T.pb7[:, 0:n]
         if on_s:
-            gather("S", T.Rb[:, :], ("Rb",), T.Rt[:, 0:top], ("Rt", 0, top), l, r)
-            pe("pb6", [(T.pb6[:, :], T.idB[:, :], T.Rb[:, :]), (T.pb6[:, :], T.idN[:, :], X[:, a:a + 512])], [("Rb",), xr, ("idB",), ("idN",)])
-            act(T.bt[:, a:a + 512], T.pb6[:, :], [("pb6",)], [b_], func=AF.Sign, bias=-0.5)
+            rb, rbr = lanes("Rb", h)
+            gather("S", rb, rbr, T.Rt[:, 0:top], ("Rt", 0, top), l, r)
+            pe("pb6", [(p6, T.idB[:, :], rb), (p6, T.idN[:, :], x)], [rbr, xr, ("idB",), ("idN",)])
+            act(bt, p6, [("pb6",)], [btr], func=AF.Sign, bias=-0.5)
         else:
-            tt(T.bt[:, a:a + 512], T.Rt[:, 0:top].indirect(l), X[:, a:a + 512], A.is_gt, [("Rt", 0, top), r, xr], [b_], ind=GAT)
-        o = T[bank][:, 32:64]
-        pe(bank, [(o, T.id16[:, :], T.hs[:, c:c + 32])], [("id16",), ("hs", c, c + 32)], last=False)
+            tt(bt, T.Rt[:, 0:top].indirect(l), x, A.is_gt, [("Rt", 0, top), r, xr], [btr], ind=GAT)
+        o = T[bank][:, 256:256 + n // 16]
+        (hs, hsr), (e, er) = cols("hs", h), cols("el", h)
+        pe(bank, [(o, T.id16[:, :], hs)], [("id16",), hsr], last=False)
         Q = "Q48" if on_s else "Q97"
-        pe(bank, direct(o, 32, T[Q], T.bt, a), [b_, (Q,)], first=False)
-        ts(T.el[:, c:c + 32], o, 776.0 if on_s else 0.0, A.add, [(bank,)], [("el", c, c + 32)])
-        e, er = T.el[:, c:c + 32], ("el", c, c + 32)
-        m = 1024 * t + a
-        tm, tmr, mk, mkr = T.TM[:, m:m + 512], ("TM", m, m + 512), T.MM[:, m:m + 512], ("MM", m, m + 512)
-        if h == 1 and EB_ON_S[t]:
+        pe(bank, direct(o, n // 16, T[Q], T.bt, a), [btr, (Q,)], first=False)
+        ts(e, o, 776.0 if on_s else 0.0, A.add, [(bank,)], [er])
+        (tm, tmr), (mk, mkr), (v, vr) = (lanes(nm, h, 1024 * t) for nm in ("TM", "MM", "VV"))
+        if h in E_ON_S[t]:
             gather("S", tm, tmr, T.Et[:, :], ("Et",), e, er)
-            for bk, last in (("pb6", True), ("pb7", False)):
-                pe(bk, [(T[bk][:, :], T.idB[:, :], tm), (T[bk][:, :], T.idB[:, :], X[:, a:a + 512])], [tmr, xr, ("idB",)], last=last)
-            act(mk, T.pb6[:, :], [("pb6",)], [mkr], func=AF.Sign, bias=0.5)
-            pe("pb7", [(T.pb7[:, :], T.idS[:, :], mk)], [mkr, ("idS",)], first=False)
-            act(T.VV[:, 512 * t:512 * t + 512], T.pb7[:, :], [("pb7",)], [("VV", 512 * t, 512 * t + 512)], bias=128.0)
-            send(t, h, [("VV", 512 * t)])
+            for bk, p, last in (("pb6", p6, True), ("pb7", p7, False)):
+                pe(bk, [(p, T.idB[:, :], tm), (p, T.idB[:, :], x)], [tmr, xr, ("idB",)], last=last)
+            act(mk, p6, [("pb6",)], [mkr], func=AF.Sign, bias=0.5)
+            pe("pb7", [(p7, T.idS[:, :], mk)], [mkr, ("idS",)], first=False)
+            act(v, p7, [("pb7",)], [vr], bias=128.0)
+            send(t, h, ["VV"])
         else:
-            for u in (0, 256):
-                tt(T.TM[:, m + u:m + u + 256], T.Et[:, :].indirect(T.el[:, c + u // 16:c + u // 16 + 16]), X[:, a + u:a + u + 256], A.add,
-                   [("Et",), er, xr], [("TM", m + u, m + u + 256)], ind=GAT)
-                ts(T.MM[:, m + u:m + u + 256], T.TM[:, m + u:m + u + 256], 0.0, A.is_lt, [("TM", m + u, m + u + 256)], [("MM", m + u, m + u + 256)],
-                   256.0, A.mult)
-            send(t, h, [("TM", m), ("MM", m)])
+            for u, w in ((a, a + n),) if a or n == 256 else ((0, 256), (256, n)):
+                lo, hi = 1024 * t + u, 1024 * t + w
+                tt(T.TM[:, lo:hi], T.Et[:, :].indirect(T.el[:, u // 16:w // 16]), X[:, u:w], A.add, [("Et",), er, xr], [("TM", lo, hi)], ind=GAT)
+                ts(T.MM[:, lo:hi], T.TM[:, lo:hi], 0.0, A.is_lt, [("TM", lo, hi)], [("MM", lo, hi)], 256.0, A.mult)
+            send(t, h, ["TM", "MM"])
 
     def firsts(t):
         top = 2048 + 512 * t
@@ -502,24 +566,25 @@ def rank_program(g, core, T, topo):
         pe("pb4", [(T.pb4[:, 0:256], T.BDs[:, :], T.K5[:, :])], [("K5",), ("BDs",)])
         cp(T.fru[:, :], T.pb4[:, 0:256], [("pb4",)], [("fru",)])
         pe("pb5", [(T.pb5[:, 0:256], T.BDi[:, :], T.K5[:, :])], [("K5",), ("BDi",)], last=False)
+        ts(T.fL[:, :], T.fl[:, 0:16], -float(OFF), A.add, [l0], [("fL",)])
         for c in range(16):
             n = 256 - 16 * c
             e = ("E", 256 * c, 256 * c + n)
-            ts(T.E[:, 256 * c:256 * c + n], T.fru[:, 16 * c:256], T.pb0[:, 128 + c:129 + c], A.is_equal, [("fru",), ("pb0",), ("w16",)],
+            ts(T.E[:, 256 * c:256 * c + n], T.fru[:, 16 * c:256], T.fL[:, c:c + 1], A.is_equal, [("fru",), ("fL",), ("w16",)],
                [e], T.w16[:, c:c + 1], A.mult)
             pe("pb5", [(T.pb5[:, 16 * c:256], T.BD[:, :], T.E[:, 256 * c:256 * c + n])], [e, ("BD",)], False, c == 15)
         tt(T.qB[:, :], T.pb5[:, 0:256], T.thrR[:, :], A.is_ge, [("pb5",), ("thrR",)], [("qB",)])
 
     def lists(t):
         if t < 2:
-            o = T.pb2[:, 80:96]
-            pe("pb2", [(o, T.idB[:, :], T.laneB[:, :])] + direct(o, 16, T.Q64, T.depB, 0), [("depB",), ("Q64",), ("idB",), ("laneB",)])
-            cp(T.depU[:, :], o, [("pb2",)], [("depU",)])
+            o = T[LB][:, 320:336]
+            pe(LB, [(o, T.idB[:, :], T.laneB[:, :])] + direct(o, 16, T.Q64, T.depB, 0), [("depB",), ("Q64",), ("idB",), ("laneB",)])
+            cp(T.depU[:, :], o, [(LB,)], [("depU",)])
             gather("S", T.xf[:, :], ("xf",), T[XP[t]][:, 0:NXP], (XP[t], 0, NXP), T.depU[:, :], ("depU",))
-        o = T.pb2[:, 64:80]
-        pe("pb2", to_list(0, o, 16), [("Fz0",), ("RQ",)], last=False)
-        pe("pb2", direct(o, 16, T.Q512, T.qB, 0), [("qB",), ("Q512",)], first=False)
-        tt(T.fo[:, :], o, T.dumpL[:, :], A.min, [("pb2",), ("dumpL",)], [("fo",)])
+        o = T[LB][:, 300:316]
+        pe(LB, to_list(0, o, 16), [("Fz0",), ("RQ",)], last=False)
+        pe(LB, direct(o, 16, T.Q512, T.qB, 0), [("qB",), ("Q512",)], first=False)
+        tt(T.fo[:, :], o, T.dumpL[:, :], A.min, [(LB,), ("dumpL",)], [("fo",)])
         ts(T.offU[:, :], T.fo[:, :], float(OFF), A.add, [("fo",)], [("offU",)])
 
     def vterms(o, ident, t):
@@ -538,10 +603,10 @@ def rank_program(g, core, T, topo):
             pe("pb4", [(T.pb4[:, 0:256], T.Mb[:, :], T.K5[:, :])], [("K5",), ("Mb",)])
             act(T.old32[:, :], T.pb4[:, 0:256], [("pb4",)], [("old32",)])
             pe("pb4", [(d, T.Mb[:, :], new), (d, T.MbN[:, :], T.K5[:, :])], [newr, ("K5",), ("Mb",), ("MbN",)])
-        o = T.pb1[:, 256:512]
+        o = T.pb0[:, 256:512]
         terms, rd = vterms(o, "idN", t)
-        pe("pb1", [(o, T.idB[:, :], rg)] + terms, rd + [rgr, ("idB",)])
-        act(T.aB[:, :], o, [("pb1",)], [("aB",)], func=AF.Abs)
+        pe("pb0", [(o, T.idB[:, :], rg)] + terms, rd + [rgr, ("idB",)])
+        act(T.aB[:, :], o, [("pb0",)], [("aB",)], func=AF.Abs)
         o = T.pb5[:, 256:512]
         pe("pb5", [(o, T.idM[:, :], T.qB[:, :])], [("qB",), ("idM",)], last=False)
         pe("pb5", [(o, T.BD[:, :], T.aB[:, :])], [("aB",), ("BD",)], first=False)
@@ -564,25 +629,28 @@ def rank_program(g, core, T, topo):
         pe("pb6", [(o, T.idH[:, :], rg)] + terms + [(o, T.idW[:, :], win)], rd + [rgr, winr, ("idW",)])
         ts(T.avI[:, :], o, -512.25, A.add, [("pb6",)], [("avI",)], 0.0, A.max)
         cp(T.Rt[:, n + 1:n + 512:2], T.avI[:, :], [("avI",)], [("Rt", n, n + 512, "odd")])
-        dma("D", T.yr[:, 512 * t:512 * t + 512], T.Rt[:, n:n + 512], 512 * MB, [("Rt", n, n + 512)], [])
+        me = dma("D", T.yr[:, 512 * t:512 * t + 512], T.Rt[:, n:n + 512], 512 * MB, [("Rt", n, n + 512)], [])
+        if t == 2:
+            lead.append(me)
 
+    H = range(len(PARTS))
     for t in range(3):
         if t == 0:
             for k in range(5):
-                for h in range(2):
+                for h in H:
                     paths(0, h, k)
                 pred(k, 1024 if k < 4 else 256)
             env_table()
-        for h in range(2):
+        for h in H:
             hsum(t, h)
         if t > 0:
             for k in range(1, 5):
-                for h in range(2):
+                for h in H:
                     paths(t, h, k)
         if t < 2:
             xg("S", t, 5, 0, 256)
         for k in range(5):
-            for h in range(2):
+            for h in H:
                 step(t, h, k)
         if t == 0:
             new_nodes()
@@ -601,13 +669,16 @@ def rank_program(g, core, T, topo):
         firsts(t)
         outcome(t, 0)
         lists(t)
-        outcome(t, 1)
         splits(t)
+        for h in H[1:]:
+            outcome(t, h)
         new_r(t)
-    dma("D", T.yk0[:, :], T.Ko[0:128:16, 0:3584], 114688, [("Ko",)], [])
-    dma("S", T.yk1[:, :], T.Ko[2:128:16, 0:3584], 114688, [("Ko",)], [])
-    pe("pb3", block(T.pb3[:, 128:192], 64, T.QW, T.XF), [("XF",), ("QW",)])
-    cp(T.yI[:, :], T.pb3[:, 128:192], [("pb3",)], [("yI",)])
+    lead.append(dma("D", T.yk0[:, :], T.Ko[0:128:16, 0:3584], 114688, [("Ko",)], []))
+    lead.append(dma("S", T.yk1[:, :], T.Ko[2:128:16, 0:3584], 114688, [("Ko",)], []))
+    terms = block(T.pb1[:, 384:448], 64, T.QW, T.XF)
+    for j in range(4):
+        pe("pb1", terms[4 * j:4 * j + 4], [("XF", 256 * j, 256 * j + 256), ("QW",)], j == 0, j == 3)
+    cp(T.yI[:, :], T.pb1[:, 384:448], [("pb1",)], [("yI",)])
     ts(T.yJ[:, :], T.yI[:, :], 1023, A.bitwise_and, [("yI",)], [("yJ",)])
     ts(T.ypF[:, :], T.yJ[:, :], 5120.0, A.add, [("yJ",)], [("ypF",)])
     dma("D", T.yp[:, 2048:3072], T.ypF[:, :], 32768, [("ypF",)], [])

@@ -7,15 +7,30 @@ AF = ActivationFunctionType
 PARTS = ((0, 512), (512, 512))
 IB = ("pb2", "pb3")
 LB = "pb2"
-XS = ((384, 384), (448, 448), (448, 448))
+XS = ((384, 384), (416, 416), (416, 416))
 BOTH, ALONE = ((("S", 0, 512), ("V", 512, 1024)),), ((("S", 0, 512), ("S", 512, 1024)),)
 PRED = (BOTH, BOTH, BOTH, BOTH, BOTH)
-R_ON_S = ((), (), ())
+R_ON_S = ((1,), (1,), ())
 E_ON_S = ((), (), ())
 LEAD = 0.0
-XFIRST = 2048
-PASSES = 4
-NOISE, FIN, SLACK = 0.0, 1.0, 0.5
+XFIRST = 4096
+XMID = 4096
+AV_ON_S = (0, 1, 2)
+SUMS_SENT = ()
+SPREAD = 1
+SMALL = 1.0
+BOOST = 6
+BIAS = {}
+WHOLE = 12582912.0
+PASSES = 2
+TRIES, WARM, SEED = 5000, 0.06, 8
+CASES = ((1.0, 1.0, 0.1, 0.3, 0.35, 0.0), (1.0, 0.8, 0.22, 0.28, 0.45, 0.4), (1.4, 1.8, 0.1, 0.3, 0.2, 0.0))
+ORDER = {}
+HOLD = 0.3
+WAIT = 0.0
+RUN = 4
+BITS_FIRST = False
+R_SPLIT = False
 PLAN = []
 BIG = 65536.0
 NXP = 5 * 1024 + 256
@@ -30,24 +45,25 @@ def _sb(dtype, text):
         SCRATCH[n] = ("sbuf", [128, int(c)], dtype)
 
 
-_sb("bfloat16", "xs:4096 Pt:4096 Kt:4096 Zt:3840 Rt:3584 Et:3600 XA:5376 XB:5376 XC:5376 XF:1024 TM:3072 MM:3072 VV:3072 Pg:1024 Kg:1024 "
-    "bt:1024 Rb:1024 K5:256 Rg:768 aB:256 E:4096 qB:256 winB:768 tK:256 xf:256 depB:256 NDlo:128 NEW:768 SC:96 "
-    "ones:256 zer:144 Qa:144 Qb:144 Q01:144 QP:144 QW:144 Q97:144 Q48:144 Q64:144 Q512:144 W1:8 WK:16 RQb:128 BD:128 BDs:128 BDi:128 "
-    "BDf:128 idB:128 idN:128 idH:128 idS:128 idM:128 idW:128 idMn:128 Mb:128 MbN:128 dg:640 pg:512 sfl:256 sfi:256 laneB:16")
-_sb("float16", "RQ:128 id16:128 hs:64 fru:256")
-_sb("float32", "onesF:128 BDF:128 sc:288 fL:16 w16:16 thrR:256 laneL:16 dumpL:16 fo:16 col:32 thF:1 ypF:64 curF:64 curT:64 hF:64 hT:64 "
+_sb("bfloat16", "xs:4096 Pt:4096 Kt:4096 Zt:3840 Rt:3584 Et:3600 XA:5376 XB:5376 XC:5376 QN:144 Pg:1024 Kg:1024 "
+    "bt:1024 K5:256 Rg:3072 aB:256 E:4096 qB:256 winB:768 tK:256 xf:256 depB:256 NDlo:256 NDhi:768 SC:96 "
+    "ones:256 zer:144 Qa:144 Qb:144 Q01:144 QP:144 QW:144 Q97:144 Q256:144 QK0:144 QK1:144 thrR:256 Dhi:128 Dlo:128 Done:128 D2:128 W1:8 WK:16 RQb:128 BD:128 BDs:128 BDi:128 "
+    "BDf:128 idB:128 idN:128 idH:128 idM:128 idW:128 idMn:128 Mb:128 MbN:128 dg:640 pg:512 sfl:256 sfi:256 laneB:16")
+_sb("float16", "TM:3072 MM:3072 CC:2048 RQ:128 id16:128 hs:192 fru:256")
+_sb("float32", "kB:448 sc:288 wS:1 wN:1 ypS:64 onesF:128 BDF:128 w16:16 avF:256 laneL:16 dumpL:16 fo:16 col:32 thF:1 ypF:64 curF:64 curT:64 hF:64 hT:64 "
     "Ct:1024 Cg:1024 Ko:3840 old32:256 tK32:256")
-_sb("int32", "prevI:256 kI:256 kH:256 curI:64 startI:64 wI:1 thI:1 pI:1 pmI:1 pnI:1 ownI:128 own2:128 hI:64 hJ:128 hK:64 yI:64 yJ:64 avI:256")
+_sb("int32", "prevI:256 kI:256 kH:256 curI:64 startI:64 wI:1 thI:1 pI:1 pmI:1 pnI:1 ownI:128 own2:128 hI:64 hJ:128 hK:64 yI:64 yJ:64")
 _sb("uint16", "f0:64 fl:64 sl:384 hl:128 el:64 offU:16 depU:16")
-for _h in range(3):
-    SCRATCH["Fz%d" % _h] = ("sbuf", [128, 36, 4], "float16")
+SCRATCH["Fz"] = ("sbuf", [128, 3 * 36, 4], "float16")
 for _i in range(8):
     SCRATCH["pb%d" % _i] = ("psum", [128, 512], "float32")
 
 NDMA = 64
-SEMAPHORES = ["sV", "sS", "sP", "sG", "loc"] + ["d%d" % i for i in range(NDMA)] + ["a%d%d" % (t, c) for t in range(3) for c in range(3)]
+SEMAPHORES = ["sV", "sS", "sP", "sG", "loc"] + ["d%d" % i for i in range(NDMA)] + ["aw", "ay"] + [s + "%d%d" % (t, c) for s in "ab" for t in range(2) for c in range(4)]
 
-CYC, PEC, GAT, SCA, HAND, DMA0, DMAB, REMOTE = 0.00083, 0.00042, 1.4, 3.0, 0.14, 1.2, 1 / 350e3, 2.6
+CYC, PEC, GAT, SCA, HAND, DMA0, DMAB, REMOTE = 0.00083, 0.00039, 1.5, 3.7, 0.18, 1.5, 2.1e-6, 1.9
+SELF, VFIX, VMIN, SFIX = 0.29, 0, 56, 0.07
+Q_ON_S = True
 WIDTH = {"bfloat16": 2, "float16": 2, "uint16": 2, "float32": 4, "int32": 4}
 
 
@@ -58,13 +74,17 @@ def rank_program(g, core, T, topo):
     dst = T.cores[(rank + 1) % len(T.cores)]
     src = T.cores[(rank - 1) % len(T.cores)]
 
-    def pairs(a, b):
-        return topo.engines(a, b)[::2]
-
     QUEUE = {"V": g.vector, "S": g.scalar, "P": g.tensor, "G": g, "D": g.sync}
     SEM = {"V": "sV", "S": "sS", "P": "sP", "G": "sG"}
     ops = []
     recs = {}
+
+    tags, tag_ = [], [None]
+
+    def tagged(name, fn, *a):
+        tag_[0] = name
+        fn(*a)
+        tag_[0] = None
 
     def norm(r):
         b = r[0]
@@ -74,7 +94,7 @@ def rank_program(g, core, T, topo):
             return (b, r[1], r[2], None)
         return r
 
-    def record(q, kind, calls, busy, done, reads, writes, sem=None, after=()):
+    def record(q, kind, calls, busy, done, reads, writes, sem=None, after=(), picked=0.0):
         me = len(ops)
         pred = {}
         for p in after:
@@ -91,7 +111,8 @@ def rank_program(g, core, T, topo):
                     o = ops[rec[4]]
                     same = o[0] == q and o[1] == "op" and kind == "op"
                     pred[rec[4]] = pred.get(rec[4], False) or not (same and (ps or w))
-        ops.append([q, kind, calls, busy, done, pred, sem])
+        ops.append([q, kind, calls, busy, done, pred, sem, picked])
+        tags.append(tag_[0])
         for rs, w in ((reads, False), (writes, True)):
             for r in rs:
                 b, lo, hi, tag = norm(r)
@@ -104,13 +125,16 @@ def rank_program(g, core, T, topo):
                 recs[b].append([w, lo, hi, tag, me])
         return me
 
-    def op(q, calls, cost, reads, writes):
+    def op(q, calls, cost, reads, writes, ind=0.0):
         if not isinstance(calls, list):
             calls = [calls]
-        return record(q, "op", calls, cost, cost + (0.06 if q == "P" else 0), reads, writes)
+        return record(q, "op", calls, cost, cost + (0.06 if q == "P" else 0), reads, writes, None, sent[:3] if q == "G" else (),
+                      cost - 0.06 if ind > 1 else 0.0)
 
     ndma = [0]
+    sent = []
     lead = []
+    early = []
 
     def dma(q, out, in_, nbytes, reads, writes, after=(), **kw):
         s = "d%d" % ndma[0]
@@ -119,13 +143,17 @@ def rank_program(g, core, T, topo):
 
     def emit():
         n = len(ops)
+        for o in ops:
+            if o[1] == "op" and any(o[5].values()):
+                o[3] += WAIT
+                o[4] += WAIT
         succ = [[] for _ in ops]
         for i, o in enumerate(ops):
             for p in o[5]:
                 succ[p].append(i)
 
         def gap(p, i):
-            return ops[p][4] + HAND if ops[i][5][p] else ops[p][3]
+            return ops[p][4] + (SELF if ops[p][:2] == ops[i][:2] else HAND) if ops[i][5][p] else ops[p][3]
         level = [0.0] * n
         for i in range(n - 1, -1, -1):
             level[i] = max([gap(i, j) + level[j] for j in succ[i]] + [ops[i][4] + (LEAD if i in lead else 0)])
@@ -166,37 +194,113 @@ def rank_program(g, core, T, topo):
                 for j in (ops[i][5] if back else succ[i]):
                     key[i] = max(key[i], key[j] + 1e-6)
             return sorted(range(n), key=lambda i: -key[i])
-        start = best = place(ranked(level, False), False)
-        seed = [1]
-
-        def noise():
-            seed[0] = (seed[0] * 1103515245 + 12345) % 2147483648
-            return (seed[0] / 2147483648 - 0.5) * NOISE
+        lv = list(level)
+        for i in range(n - 1, -1, -1):
+            lv[i] = max([gap(i, j) + lv[j] for j in succ[i]] + [level[i] + (BOOST if i in early else 0)])
+        start = best = place(ranked([lv[i] + BIAS.get(tags[i], 0) for i in range(n)], False), False)
         for _ in range(PASSES):
-            late = place(ranked([start[i] + FIN * ops[i][4] + noise() for i in range(n)], True), True)
-            start = place(ranked([late[i] + noise() for i in range(n)], False), False)
+            late = place(ranked([start[i] + ops[i][4] for i in range(n)], True), True)
+            start = place(ranked(late, False), False)
             if length(start) < length(best):
                 best = start
-            elif length(start) > length(best) + SLACK:
-                start = best
-        start = best
+        cases = []
+        for plain, picked, hand, own, _, far in CASES:
+            more = [(o[3] - o[7]) * (plain - 1) + o[7] * (picked - 1) if o[1] == "op" else far * (o[1] == "arrival") for o in ops]
+            cases.append(([o[3] + m * (o[1] == "op") for o, m in zip(ops, more)],
+                          [[(p, more[p] + (ops[p][4] + (own if ops[p][:2] == o[:2] else hand) if w else ops[p][3]), w) for p, w in o[5].items()]
+                           for o in ops]))
+
+        def once(order, busy, before):
+            at, why, late, free, last, engines = [0.0] * n, [-1] * n, [0.0] * n, {}, {}, 0.0
+            for i in order:
+                q = ops[i][0]
+                t, w = free.get(q, 0.0), last.get(q, -1)
+                for p, d, waits in before[i]:
+                    u = at[p] + d + (late[p] if waits else 0.0)
+                    if u > t:
+                        t, w = u, p
+                at[i], why[i], free[q], last[q] = t, w, t + busy[i], i
+                if ops[i][1] == "dma":
+                    late[i] = max(0.0, engines - t - DMA0)
+                    engines = t + late[i] + ops[i][4]
+            end = max(range(n), key=lambda i: at[i] + late[i] + ops[i][4])
+            return at[end] + late[end] + ops[end][4], at, why, end
+
+        def run(order):
+            runs = [once(order, *c) for c in cases]
+            return sum(r[0] * c[4] for r, c in zip(runs, CASES)), runs[0][1], [r[2] for r in runs], [r[3] for r in runs]
+
+        def polish(at):
+            seed = [SEED]
+
+            def draw():
+                seed[0] = (seed[0] * 1103515245 + 12345) % 2147483648
+                return seed[0] / 2147483648
+            order = sorted(range(n), key=lambda i: (at[i], i))
+            now, at, whys, ends = run(order)
+            least = (now, at)
+            for it in range(TRIES):
+                held, i, why = [], ends[it % len(CASES)], whys[it % len(CASES)]
+                while why[i] >= 0:
+                    if ops[why[i]][0] == ops[i][0] and why[i] not in ops[i][5]:
+                        held.append((why[i], i))
+                    i = why[i]
+                if not held:
+                    continue
+                a, b = held[int(draw() * len(held))]
+                lo, hi = order.index(a), order.index(b)
+                for _ in range(int(draw() * 10) - 6):
+                    lo = max([k for k in range(max(0, lo - 40), lo) if ops[order[k]][0] == ops[a][0]] + [-1]) if lo > 0 else -1
+                    if lo < 0:
+                        break
+                if lo < 0:
+                    continue
+                a, piece = order[lo], order[lo:hi + 1]
+                if draw() < 0.5:
+                    need = set(ops[b][5])
+                    first = {b}
+                    for x in piece[-2::-1]:
+                        if x in need:
+                            first.add(x)
+                            need.update(ops[x][5])
+                    if a in first:
+                        continue
+                else:
+                    second = {a}
+                    for x in piece[1:]:
+                        if not second.isdisjoint(ops[x][5]):
+                            second.add(x)
+                    if b in second:
+                        continue
+                    first = set(piece) - second
+                other = order[:lo] + [x for x in piece if x in first] + [x for x in piece if x not in first] + order[hi + 1:]
+                t, at2, why2, end2 = run(other)
+                if t < now or draw() < math.exp((now - t) / (WARM * (1 - it / TRIES) + 0.005)):
+                    now, at, whys, ends = t, at2, why2, end2
+                    order = sorted(other, key=lambda i: at[i])
+                    if now < least[0]:
+                        least = (now, at)
+            return least[1]
+        if n not in ORDER:
+            ORDER[n] = polish(best)
+        start = best = ORDER[n]
         PLAN[:] = [(length(best), max(level), ops, level, start)]
-        total, seen, mark = {}, {}, {}
+        total, seen, mark, known = {}, {}, {}, {}
         for i in sorted(range(n), key=lambda i: (start[i], i)):
-            q, kind, calls, _, _, pred, sem = ops[i]
+            q, kind, calls, _, _, pred, sem, _ = ops[i]
             if kind == "arrival":
-                mark[i] = (sem, calls)
+                mark[i], known[i] = (sem, calls), {}
                 total[sem] = calls
                 continue
-            need = {}
-            for p in pred:
-                if pred[p]:
-                    s, v = mark[p]
-                    need[s] = max(need.get(s, 0), v)
-            for s in need:
-                if seen.get((q, s), 0) < need[s]:
-                    QUEUE[q].wait_ge(T.sem[s], need[s])
-                    seen[(q, s)] = need[s]
+            mine = seen.setdefault(q, {})
+            for p in sorted((p for p in pred if pred[p]), key=lambda p: -start[p]):
+                s, v = mark[p]
+                if mine.get(s, 0) < v:
+                    QUEUE[q].wait_ge(T.sem[s], v)
+                    mine[s] = v
+                    for s, v in known[p].items():
+                        mine[s] = max(mine.get(s, 0), v)
+            known[i] = dict(mine)
             if kind == "dma":
                 calls().then_inc(T.sem[sem], 16)
                 total[sem] = 16
@@ -210,7 +314,7 @@ def rank_program(g, core, T, topo):
                 total[s] = total.get(s, 0) + len(calls)
                 mark[i] = (s, total[s])
         for s in total:
-            if seen.get(("G", s), 0) < total[s]:
+            if seen["G"].get(s, 0) < total[s]:
                 g.wait_ge(T.sem[s], total[s])
 
     V = g.vector
@@ -223,13 +327,13 @@ def rank_program(g, core, T, topo):
             return 0.05 + n * ind * CYC
         psum = any(r[0].startswith("pb") for r in rd + wr)
         narrow = WIDTH[SCRATCH[rd[0][0]][2]] == 2 and WIDTH[SCRATCH[wr[0][0]][2]] == 2
-        return 0.05 + n * CYC * ((1 if psum else 2) if two else (0.5 if narrow else 1))
+        return VFIX + CYC * max(VMIN, n * ((1 if psum else 2) if two else (0.5 if narrow else 1)))
 
     def cp(out, in_, rd, wr, n=None, ind=0.0):
-        return op("V", lambda: V.tensor_copy(out=out, in_=in_), vcost(n or count(out), rd, wr, False, ind), rd, wr)
+        return op("V", lambda: V.tensor_copy(out=out, in_=in_), vcost(n or count(out), rd, wr, False, ind), rd, wr, ind)
 
     def tt(out, a, b, o, rd, wr, ind=0.0):
-        return op("V", lambda: V.tensor_tensor(out=out, in0=a, in1=b, op=o), vcost(count(b), rd, wr, True, ind), rd, wr)
+        return op("V", lambda: V.tensor_tensor(out=out, in0=a, in1=b, op=o), vcost(count(b), rd, wr, True, ind), rd, wr, ind)
 
     def ts(out, a, s1, o1, rd, wr, s2=None, o2=None):
         c = vcost(count(out), rd, wr)
@@ -242,7 +346,7 @@ def rank_program(g, core, T, topo):
         op("V", lambda: V.memset(T[name][:, lo:hi], v), vcost(hi - lo, [r], [r]), [], [r])
 
     def act(out, in_, rd, wr, func=AF.Copy, ind=1.0, more=0.0, **kw):
-        op("S", lambda: g.scalar.activation(out=out, in_=in_, func=func, **kw), 0.065 + more + count(out) * ind * CYC, rd, wr)
+        op("S", lambda: g.scalar.activation(out=out, in_=in_, func=func, **kw), (0.065 if ind > 1 else SFIX) + more + count(out) * ind * CYC, rd, wr, ind)
 
     def gather(eng, out, outr, win, winr, lst, lstr):
         if eng == "S":
@@ -252,9 +356,9 @@ def rank_program(g, core, T, topo):
 
     def pe(bank, terms, rd, first=True, last=True, wide=1, alone=False):
         n = len(terms)
-        for a in range(0, n, 4):
+        for a in range(0, n, RUN):
             calls, cost = [], 0.0
-            for i in range(a, min(a + 4, n)):
+            for i in range(a, min(a + RUN, n)):
                 o, l, r = terms[i]
                 st, sp = alone or (first and i == 0), alone or (last and i == n - 1)
                 calls.append(lambda o=o, l=l, r=r, st=st, sp=sp: g.tensor.matmul(o, l, r, st, sp))
@@ -299,12 +403,12 @@ def rank_program(g, core, T, topo):
     for a in (0, 1024):
         act(T.Kt[:, a:a + 1024], T.Pt[:, a:a + 1024], [("Pt", a, a + 1024)], [("Kt", a, a + 1024)])
     for h in range(len(PARTS)):
-        cp(T["Fz%d" % h][:, :, :], T.zer[:, :], [("zer",)], [("Fz%d" % h,)])
+        cp(T.Fz[:, 36 * h:36 * h + 36, :], T.zer[:, :], [("zer",)], [("Fz", h, h + 1)])
     for j, v in enumerate((1, 8, -9)):
         op("V", lambda j=j, v=v: V.memset(T.SC[:, j:96:3], v * BIG), 0.07, [], [("SC", 0, 96, "c%d" % j)])
     GR = [-16, 8]
-    sel("W1", "ones", 8, [GR], A.is_ge, 0, 0, 1)
-    sel("W1", "W1", 8, [[16, 8]], A.is_ge, 0, 15, -1)
+    sel("W1", "zer", 8, [GR], A.is_ge, 1, -16, 1)
+    sel("W1", "W1", 8, [GR], A.is_ge, 0, 0, 1)
     for j, (half, below, v) in enumerate(((0, 4, -1 / BIG), (1, 4, -8), (0, 2, 1 / BIG), (1, 2, 9))):
         sel("WK", "WK" if j else "zer", 16, [[1000 - 2000 * half, 2], GR], A.is_ge, v, 1000 * half - below, 1)
     sel("WK", "WK", 16, [[0, 2], GR], A.is_ge, 0, 0, 1)
@@ -319,14 +423,12 @@ def rank_program(g, core, T, topo):
     iota("pI", 0, 1, [[0, 1]], 0, 1)
     iota("sfl", 0, 256, [[1, 256]], 0, 0)
     iota("laneL", 0, 16, [[16, 16]], 0, 0)
-    iota("NDlo", 0, 128, [[2, 128]], 0, 0)
-    for nm, v in (("idB", 1), ("idN", -1), ("idH", 0.5), ("idS", -128), ("idM", -8192), ("idW", 512)):
+    iota("NDlo", 0, 256, [[0, 2], [2, 128]], 0, 0)
+    for nm, v in (("idB", 1), ("idN", -1), ("idH", -0.5), ("idM", -4096), ("idW", 1024)):
         sel(nm, "zer", 128, [[-1, 128]], A.not_equal, v, 0, 1)
     cp(T.id16[:, :], T.idB[:, :], [("idB",)], [("id16",)])
     for h in range(len(PARTS)):
         pe("pb%d" % h, [(T["pb%d" % h][:, 1:96:3], T.idN[:, :], T.ones[:, 0:32])], [("idN",), ("ones",)])
-    sel("Mb", "idB", 128, [[-1, 128]], A.not_equal, 1, -1, 1)
-    sel("MbN", "idN", 128, [[-1, 128]], A.not_equal, -1, -1, 1)
     PL = [GR, [0, 16]]
     sel("BD", "ones", 128, PL, A.is_ge, 0, 0, 1)
     sel("BD", "BD", 128, [[16, 8], [0, 16]], A.is_ge, 0, 15, -1)
@@ -344,6 +446,8 @@ def rank_program(g, core, T, topo):
     tt(T.pg[:, 256:512], T.prevI[:, :], T.pg[:, 0:256], A.subtract, [("prevI",), ("pg", 0, 256)], [("pg", 256, 512)])
     rows = [dma("D", T.Pt[14 + j:128:16, :], T.pg[:, 256 * j:256 * j + 256], 65536, [("pg", 256 * j, 256 * j + 256)],
                 [("Pt", 0, 4096, "r%d" % (14 + j))], [big]) for j in range(2)]
+    if XFIRST < XMID:
+        big = dma("D", T.xs[:, XFIRST:XMID], T.x[:, XFIRST:XMID], (XMID - XFIRST) * MB, [], [("xs", XFIRST, XMID)], rows)
     ts(T.kH[:, :], T.kI[:, :], 0xF00, A.bitwise_and, [("kI",)], [("kH",)])
     cp(T.dg[:, 0:256], T.kH[:, :], [("kH",)], [("dg", 0, 256)])
     tt(T.dg[:, 256:512], T.kI[:, :], T.kH[:, :], A.subtract, [("kI",), ("kH",)], [("dg", 256, 512)])
@@ -352,8 +456,8 @@ def rank_program(g, core, T, topo):
     for i, j in ((0, 0), (1, 2), (2, 1), (3, 3), (4, 4)):
         rows.append(dma("D", T.Kt[i:128:16, 0:2048], T.dg[:, 128 * j:128 * j + 128], 32768, [("dg", 128 * j, 128 * j + 128)],
                         [("Kt", 0, 2048, "r%d" % i)], [big]))
-    if XFIRST < 4096:
-        rows.append(dma("D", T.xs[:, XFIRST:4096], T.x[:, XFIRST:4096], (4096 - XFIRST) * MB, [], [("xs", XFIRST, 4096)], rows))
+    if XMID < 4096:
+        rows.append(dma("D", T.xs[:, XMID:4096], T.x[:, XMID:4096], (4096 - XMID) * MB, [], [("xs", XMID, 4096)], rows))
     dma("D", T.Zt[:, 0:2048], T.z[:, :], 2048 * MB, [], [("Zt", 0, 2048)], rows)
 
     pm, pmr = column("pm")
@@ -362,37 +466,32 @@ def rank_program(g, core, T, topo):
     wc, wcr = column("w")
     cp(wc, T.wI[:, :], [("wI",)], [wcr])
     ts(T.QW[:, :], T.Q01[:, :], wc, A.mult, [("Q01",), wcr], [("QW",)])
-    for nm, v in (("Q97", 97.0), ("Q48", 48.5), ("Q64", 64.0), ("Q512", 512.0)):
-        act(T[nm][:, :], T.Q01[:, :], [("Q01",)], [(nm,)], scale=v)
+    for nm, v in (("Q97", 97), ("Q256", 256)):
+        sel(nm, "zer", 144, [[0, 9], [1, 16]], A.not_equal, v, -15, 0)
+        sel(nm, nm, 144, [[16, 9], [0, 16]], A.is_ge, 0, 15, -1)
+        sel(nm, nm, 144, [[-16, 9], [0, 16]], A.is_ge, 0, 0, 1)
     ts(T.BDi[:, :], T.BDf[:, :], 1e18, A.mult, [("BDf",)], [("BDi",)], 1e18, A.mult)
     ts(T.laneL[:, :], T.laneL[:, :], pm, A.add, [("laneL",), pmr], [("laneL",)])
     cp(T.laneB[:, :], T.laneL[:, :], [("laneL",)], [("laneB",)])
-    ts(T.dumpL[:, :], T.laneL[:, :], 3584.0 - OFF, A.add, [("laneL",)], [("dumpL",)])
+    ts(T.dumpL[:, :], T.laneL[:, :], 3584.0 - OFF - 4096 * Q_ON_S, A.add, [("laneL",)], [("dumpL",)])
     LN = math.log(1.85)
     act(T.w16[:, :], T.laneL[:, :], [("laneL",)], [("w16",)], func=AF.Exp, more=1.3, scale=-LN, bias=128 * LN)
     act(T.thrR[:, :], T.sfl[:, :], [("sfl",), ("w16",)], [("thrR",)], func=AF.Exp, scale=-LN, bias=128 * LN + math.log(2.5))
-    for nm, o, v in (("lt5", A.is_lt, 5.0), ("e0", A.is_equal, 0.0), ("e1", A.is_equal, 1.0), ("e2", A.is_equal, 2.0), ("e3", A.is_equal, 3.0),
-                     ("e4", A.is_equal, 4.0)):
-        c, r = column(nm)
-        ts(c, pm, v, o, [pmr], [r])
-    for nm, a, b in (("hi", "e0", "e2"), ("lo", "e1", "e3"), ("one", "e3", "e4")):
-        c, r = column(nm)
-        tt(c, C[a][0], C[b][0], A.add, [C[a][1], C[b][1]], [r])
-    ts(T.idMn[:, :], T.idN[:, :], C["lt5"][0], A.mult, [("idN",), C["lt5"][1]], [("idMn",)])
-    for j in range(6):
-        c, r = column("n%d" % j)
-        ts(c, C["hi"][0], 2048.0 + 256 * j, A.mult, [C["hi"][1], C["one"][1]], [r], C["one"][0], A.add)
-        act(T.NEW[:, 128 * j:128 * j + 128], T.NDlo[:, :], [("NDlo",), C["lo"][1], r], [("NEW", 128 * j, 128 * j + 128)], func=AF.Identity,
-            scale=C["lo"][0], bias=c)
+    sel("idMn", "idN", 128, [[16, 8], [0, 16]], A.is_ge, 0, 4, -1)
+    for nm, places in (("Dhi", (0, 2)), ("Dlo", (1, 3)), ("Done", (3, 4))):
+        for j, i in enumerate(places):
+            sel(nm, nm if j else "zer", 128, [GR, [999, 16]], A.not_equal, 1, -1000 * i, 1)
+    iota("NDhi", 0, 768, [[256, 6], [0, 128]], 2048, 0)
     fill("thI", 0, 1, 0)
     dma("D", T.thI[0:128:16, :], T.th[:, :], 32, [], [("thI",)])
     cp(T.thF[:, :], T.thI[:, :], [("thI",)], [("thF",)])
     pe("pb5", [(T.pb5[:, 0:1], T.BDF[:, :], T.thF[:, :])], [("BDF",), ("thF",)], wide=4)
     thc, thr = column("th")
-    cp(thc, T.pb5[:, 0:1], [("pb5",)], [thr])
+    ts(thc, T.pb5[:, 0:1], 4096.0 * Q_ON_S, A.add, [("pb5",)], [thr])
     gate = [("XA", 1024, 1040)]
-    iota("Et", 0, 900, [[0, 900]], -256, 0)
-    iota("Ct", 0, 1024, [[0, 1024]], 0, 0)
+    iota("Zt", 2048, 3072, [[0, 1024]], 0, 0)
+    for a in (2048, 2560, 3072):
+        iota("Kt", a, a + 512, [[0, 512]], 1, 0)
     pe_, per = column("pe")
     ts(T.pnI[:, :], T.pI[:, :], 7, A.bitwise_and, [("pI",)], [("pnI",)])
     ts(pe_, T.pnI[:, :], 256.0, A.mult, [("pnI",)], [per], 2048.0, A.add)
@@ -400,12 +499,8 @@ def rank_program(g, core, T, topo):
 
     def env_table():
         dma("D", T.Rt[:, 0:2048], T.rs[:, :], 2048 * MB, gate, [("Rt", 0, 2048)])
-        dma("D", T.Zt[:, 2048:3840], T.z[:, 0:1792], 1792 * MB, gate, [("Zt", 2048, 3840)])
-        dma("D", T.Kt[:, 2048:4096], T.Pt[:, 0:2048], 2048 * MB, gate + [("Pt", 0, 2048)], [("Kt", 2048, 4096)])
-        for a in (900, 1800, 2700):
-            dma("D", T.Et[:, a:a + 900], T.Et[:, 0:900], 900 * MB, [("Et", 0, 900)] + gate, [("Et", a - 4, a + 904)])
-        dma("G", T.Et[:, 0:2048], T.env[:, :], 2048 * MB * 2, [], [("Et", 0, 2048)], accum_op=A.add)
-        dma("G", T.Et[:, 2048:EW], T.env[:, 0:EW - 2048], 1552 * MB * 2, [], [("Et", 2048, EW)], accum_op=A.add)
+        dma("D", T.Et[:, 0:2048], T.env[:, :], 2048 * MB, gate, [("Et", 0, 2048)])
+        dma("D", T.Et[:, 2048:EW], T.env[:, 0:EW - 2048], 1552 * MB, gate, [("Et", 2048, EW)])
 
     def new_nodes():
         for i in range(5):
@@ -423,8 +518,16 @@ def rank_program(g, core, T, topo):
                 dma("D", to(e, a), T[buf][:, 32 * b + 16 * e:32 * b + 16 * e + 16], 8192, [(buf,)],
                     [tor + ("e%d%d" % (e, b),)] if tor else [])
 
-    cp(T.curF[:, :], T.curI[:, :], [("curI",)], [("curF",)])
-    turn(T.curF[:, :], ("curF",), "curT", lambda e, a: T.Ct[16 * e:128:32, a:a + 512], ("Ct", 0, 1024), 0)
+    def late_constants():
+        iota("Ct", 0, 1024, [[0, 1024]], 0, 0)
+        cp(T.curF[:, :], T.curI[:, :], [("curI",)], [("curF",)])
+        turn(T.curF[:, :], ("curF",), "curT", lambda e, a: T.Ct[16 * e:128:32, a:a + 512], ("Ct", 0, 1024), 0)
+        sel("QK0", "Q01", 144, [[16, 9], [0, 16]], A.is_ge, 0, 1, -1)
+        sel("QK1", "Q01", 144, [[16, 9], [0, 16]], A.is_ge, 0, 3, -1)
+        sel("QK1", "QK1", 144, [[-16, 9], [0, 16]], A.is_ge, 0, -2, 1)
+        sel("Mb", "idB", 128, [[-1, 128]], A.not_equal, 1, -1, 1)
+        sel("MbN", "idN", 128, [[-1, 128]], A.not_equal, -1, -1, 1)
+        sel("D2", "zer", 128, [GR, [999, 16]], A.not_equal, 1, -2000, 1)
 
     XP = ["XA", "XB", "XC", "XF"]
 
@@ -437,27 +540,35 @@ def rank_program(g, core, T, topo):
         a, n = PARTS[h]
         return T[name][:, base + a:base + a + n], (name, base + a, base + a + n)
 
+    def current(t, h, u=0, w=None):
+        a, n = PARTS[h]
+        name, base = ("CC", 1024 * t - 1024) if t else ("XA", 0)
+        lo, hi = base + a + u, base + a + (w or n)
+        return T[name][:, lo:hi], (name, lo, hi)
+
     def to_list(h, out, n):
         m = PARTS[h][1] // 4
-        return [(out, T["Fz%d" % h][0:m, 3 - q:35 - q, :], T.RQ[0:m, 32 * q:32 * q + n]) for q in range(4)]
+        return [(out, T.Fz[0:m, 36 * h + 3 - q:36 * h + 35 - q, :], T.RQ[0:m, 32 * q:32 * q + n]) for q in range(4)]
 
     def step(t, h, k):
         l, r = cols("fl" if k else "f0", h)
         (a, n), top, bank = PARTS[h], 2048 + 512 * t, "pb%d" % h
-        pb, F, m = T[bank], "Fz%d" % h, n // 4
-        (kg, kgr), (bt, btr), (x, xr) = lanes("Kg", h), lanes("bt", h), lanes(XP[t], h, 1024 * k)
+        pb, F, m = T[bank], ("Fz", h, h + 1), n // 4
+        (kg, kgr), (bt, btr), (x, xr) = lanes("Kg", h), lanes("bt", h), lanes(XP[t], h, 1024 * k) if k else current(t, h)
         act(kg, T.Kt[:, 0:top].indirect(l), [("Kt", 0, top), r], [kgr], ind=GAT)
         tt(bt, T.Zt[:, 0:top].indirect(l), x, A.is_le, [("Zt", 0, top), r, xr], [btr], ind=GAT)
-        pe(bank, [(pb[0:m, 3 * j + 2:192:12], T.Kg[:, a + j:a + n:4], T.WK[:, :]) for j in range(4)], [kgr, ("WK",)], alone=True)
-        pe(bank, [(pb[0:m, 3 * j:96:12], T.bt[:, a + j:a + n:4], T.W1[:, :]) for j in range(4)], [btr, ("W1",)], alone=True)
+        both = [([(pb[0:m, 3 * j + 2:192:12], T.Kg[:, a + j:a + n:4], T.WK[:, :]) for j in range(4)], [kgr, ("WK",)]),
+                ([(pb[0:m, 3 * j:96:12], T.bt[:, a + j:a + n:4], T.W1[:, :]) for j in range(4)], [btr, ("W1",)])]
+        for terms, rd in both[::-1] if (k > 0 or t == 0) and BITS_FIRST else both:
+            pe(bank, terms, rd, alone=True)
         if h == 0 and t < 2:
             pe("pb4", [(T.pb4[:, 0:256], T.BDf[:, :], T.Kg[:, 0:256])], [("Kg", 0, 256), ("BDf",)], k == 0, k == 4)
         c, scr = 96 * h, ("sc", 96 * h, 96 * h + 96)
-        op("V", lambda: V.tensor_tensor_scan(T.sc[0:m, c:c + 96], T.SC[0:m, :], pb[0:m, 0:96], 0.0, A.max, A.mult), 0.05 + 96 * CYC,
+        op("V", lambda: V.tensor_tensor_scan(T.sc[0:m, c:c + 96], T.SC[0:m, :], pb[0:m, 0:96], 0.0, A.max, A.mult), VFIX + 96 * CYC,
            [("SC",), (bank,)], [scr])
-        tt(T[F][0:m, 3:35:4, :], pb[0:m, 98:192:3], T.sc[0:m, c + 2:c + 96:3], A.add, [(bank,), scr], [(F,)])
+        tt(T.Fz[0:m, 36 * h + 3:36 * h + 35:4, :], pb[0:m, 98:192:3], T.sc[0:m, c + 2:c + 96:3], A.add, [(bank,), scr], [F])
         o = pb[:, 192:192 + n // 16]
-        pe(bank, to_list(h, o, n // 16), [(F,), ("RQ",)])
+        pe(bank, to_list(h, o, n // 16), [F, ("RQ",)])
         l, r = cols("fl", h)
         ts(l, o, float(OFF), A.add, [(bank,)], [r])
 
@@ -489,103 +600,124 @@ def rank_program(g, core, T, topo):
             if a < b:
                 m, lo = (b - a) // 16, 64 * k + 64 + a // 16
                 pe(bank, direct(T[bank][:, 0:m], m, T.QP, T.Pg, a), [("Pg", a, b), ("QP",)])
-                cp(T.sl[:, lo:lo + m], T[bank][:, 0:m], [(bank,)], [("sl", lo, lo + m)])
+                early.append(cp(T.sl[:, lo:lo + m], T[bank][:, 0:m], [(bank,)], [("sl", lo, lo + m)]))
 
     def hsum(t, h):
         (a, n), bank = PARTS[h], IB[h]
         o = T[bank][:, 224:224 + n // 16]
-        pe(bank, direct(o, n // 16, T.QW, T[XP[t]], a), [lanes(XP[t], h)[1], ("QW",)])
+        there = t - 1 in SUMS_SENT
+        if there:
+            for j, nm in enumerate(made[t - 1, h]):
+                pe(bank, direct(o, n // 16, T.QN, T[nm], 1024 * t - 1024 + a), [lanes(nm, h, 1024 * t - 1024)[1], ("QN",)], j == 0,
+                   j == len(made[t - 1, h]) - 1)
+        else:
+            pe(bank, direct(o, n // 16, T.QW, T.CC if t else T.XA, a + (1024 * t - 1024 if t else 0)), [current(t, h)[1], ("QW",)])
+        if t == 1:
+            bk = "pb%d" % (6 + h % 2)
+            pe(bk, [(T[bk][:, 0:n], T.id16[:, :], current(t, h)[0])], [current(t, h)[1], ("id16",)])
+            act(lanes("XB", h)[0], T[bk][:, 0:n], [(bk,)], [lanes("XB", h)[1]])
         hi, hir = cols("hI", h)
         cp(hi, o, [(bank,)], [hir])
-        for want, bits, mid, out, base in ((t > 0, 1023, "hJ", "hl", 64 * t - 64), (True, 2047, "hK", "hs", 0)):
+        pieces = []
+        for want, bits, mid, out, base in ((t > 0, 1023, "hJ", "hl", 64 * t - 64), (True, 2047, "hK", "hs", 64 * t)):
             if want:
-                (u, ur), (w, wr) = cols(mid, h, base), cols(out, h, base)
+                (u, ur), (w, wr) = cols(mid, h), cols(out + "S" * there, h, base)
                 ts(u, hi, bits, A.bitwise_and, [hir], [ur])
                 cp(w, u, [ur], [wr])
+                pieces.append(([(w, wr)], cols(out, h, base)))
+        if there:
+            remote("b%d%d" % (t - 1, h), dst, src, pieces, SMALL)
 
-    def send(t, h, names):
-        en = pairs(core, dst)
-        mask = sum(1 << x for x in en)
-        rid, pid, _ = topo.addr(dst)
-        to, tor = lanes(XP[t + 1], h)
-        s = "a%d%d" % (t, h)
-        srcs = [lanes(nm, h, 1024 * t)[0] for nm in names]
+    def remote(s, to, frm, pieces, time):
+        rid, pid, _ = topo.addr(to)
+        en = topo.engines(core, to)[::SPREAD]
+        m = len(en) // len(pieces)
 
         def call():
-            if len(srcs) == 1:
-                g.remote_dma(out_ap=to, in_ap=srcs[0], remote_sem=T.sem[s], local_sem=T.sem.loc, pid=pid, routing_id=rid, dma_engine_mask=mask)
-            else:
-                g.remote_dma_fused([RemoteDMATransfer(dst_ids=[DstId(rid=rid, pnc=pid)], dma_engine_mask=mask, remote_sem=T.sem[s],
-                                                      srcs=srcs, dsts=[to], alu_op=1)], local_sem=T.sem.loc)
+            g.remote_dma_fused([RemoteDMATransfer(dst_ids=[DstId(rid=rid, pnc=pid)], dma_engine_mask=sum(1 << x for x in en[m * j:m * j + m]),
+                                                  remote_sem=T.sem[s], srcs=[a for a, _ in srcs], dsts=[out[0]], alu_op=int(len(srcs) > 1))
+                                for j, (srcs, out) in enumerate(pieces)], local_sem=T.sem.loc)
             return len(en)
-        me = record("G", "send", call, 0.3, 0.3, [lanes(nm, h, 1024 * t)[1] for nm in names], [])
-        record("R", "arrival", len(pairs(src, core)), 0.001, REMOTE * (0.5 + PARTS[h][1] / 1024), [], [tor], s, [me])
+        me = record("G", "send", call, HOLD, HOLD, [r for srcs, _ in pieces for _, r in srcs], [])
+        sent.append(me)
+        record("R", "arrival", len(topo.engines(frm, core)[::SPREAD]), 0.001, time + 0.3 - HOLD, [], [out[1] for _, out in pieces], s, [me])
+
+    made = {}
+
+    def send(t, h, names):
+        made[t, h] = names
+        if t < 2:
+            remote("a%d%d" % (t, h), dst, src, [([lanes(nm, h, 1024 * t) for nm in names], current(t + 1, h))], REMOTE * (0.5 + PARTS[h][1] / 1024))
+            if t in SUMS_SENT:
+                hsum(t + 1, h)
 
     def outcome(t, h):
-        (a, n), bank, X, top = PARTS[h], IB[h], T[XP[t]], 2048 + 512 * t
-        (l, r), (x, xr), (bt, btr) = cols("fl", h), lanes(XP[t], h), lanes("bt", h)
+        (a, n), bank, top = PARTS[h], IB[h], 2048 + 512 * t
+        (l, r), (x, xr), (bt, btr) = cols("fl", h), current(t, h), lanes("bt", h)
         on_s = h in R_ON_S[t]
-        p6, p7 = T.pb6[:, 0:n], T.pb7[:, 0:n]
         if on_s:
-            rb, rbr = lanes("Rb", h)
+            (rb, rbr), bk = lanes("Rg", h, 1024 * t), "pb%d" % (6 + h % 2)
+            p = T[bk][:, 0:n]
             gather("S", rb, rbr, T.Rt[:, 0:top], ("Rt", 0, top), l, r)
-            pe("pb6", [(p6, T.idB[:, :], rb), (p6, T.idN[:, :], x)], [rbr, xr, ("idB",), ("idN",)])
-            act(bt, p6, [("pb6",)], [btr], func=AF.Sign, bias=-0.5)
-        else:
-            tt(bt, T.Rt[:, 0:top].indirect(l), x, A.is_gt, [("Rt", 0, top), r, xr], [btr], ind=GAT)
-        o = T[bank][:, 256:256 + n // 16]
-        (hs, hsr), (e, er) = cols("hs", h), cols("el", h)
-        pe(bank, [(o, T.id16[:, :], hs)], [("id16",), hsr], last=False)
-        Q = "Q48" if on_s else "Q97"
-        pe(bank, direct(o, n // 16, T[Q], T.bt, a), [btr, (Q,)], first=False)
-        ts(e, o, 776.0 if on_s else 0.0, A.add, [(bank,)], [er])
-        (tm, tmr), (mk, mkr), (v, vr) = (lanes(nm, h, 1024 * t) for nm in ("TM", "MM", "VV"))
-        if h in E_ON_S[t]:
-            gather("S", tm, tmr, T.Et[:, :], ("Et",), e, er)
-            for bk, p, last in (("pb6", p6, True), ("pb7", p7, False)):
-                pe(bk, [(p, T.idB[:, :], tm), (p, T.idB[:, :], x)], [tmr, xr, ("idB",)], last=last)
-            act(mk, p6, [("pb6",)], [mkr], func=AF.Sign, bias=0.5)
-            pe("pb7", [(p7, T.idS[:, :], mk)], [mkr, ("idS",)], first=False)
-            act(v, p7, [("pb7",)], [vr], bias=128.0)
-            send(t, h, ["VV"])
-        else:
-            for u, w in ((a, a + n),) if a or n == 256 else ((0, 256), (256, n)):
-                lo, hi = 1024 * t + u, 1024 * t + w
-                tt(T.TM[:, lo:hi], T.Et[:, :].indirect(T.el[:, u // 16:w // 16]), X[:, u:w], A.add, [("Et",), er, xr], [("TM", lo, hi)], ind=GAT)
-                ts(T.MM[:, lo:hi], T.TM[:, lo:hi], 0.0, A.is_lt, [("TM", lo, hi)], [("MM", lo, hi)], 256.0, A.mult)
-            send(t, h, ["TM", "MM"])
+            pe(bk, [(p, T.idN[:, :], x)], [xr, ("idN",)], last=False)
+            pe(bk, [(p, T.idB[:, :], rb)], [rbr, ("idB",)], first=False)
+            act(bt, p, [(bk,)], [btr], func=AF.Sign, bias=-0.5)
+        pieces = ((0, n),) if a or n == 256 else ((0, 256), (256, n))
+        for u, w in pieces if R_SPLIT and not on_s else ((0, n),):
+            c, d = (a + u) // 16, (a + w) // 16
+            br = ("bt", a + u, a + w)
+            if not on_s:
+                tt(T.bt[:, a + u:a + w], T.Rt[:, 0:top].indirect(T.fl[:, c:d]), current(t, h, u, w)[0], A.is_gt, [("Rt", 0, top), r, xr], [br], ind=GAT)
+            o = T[bank][:, 256 + u // 16:256 + w // 16]
+            pe(bank, [(o, T.id16[:, :], T.hs[:, 64 * t + c:64 * t + d])] * (1 + on_s), [("id16",), ("hs", 64 * t + c, 64 * t + d)], last=False)
+            pe(bank, direct(o, d - c, T.Q97, T.bt, a + u), [br, ("Q97",)], first=False)
+            if on_s:
+                ts(T.el[:, c:d], o, 0.5, A.mult, [(bank,)], [("el", c, d)], 776.0, A.add)
+            else:
+                cp(T.el[:, c:d], o, [(bank,)], [("el", c, d)])
+        for u, w in pieces:
+            er = ("el", (a + u) // 16, (a + w) // 16)
+            lo, hi = 1024 * t + a + u, 1024 * t + a + w
+            tt(T.TM[:, lo:hi], T.Et[:, :].indirect(T.el[:, (a + u) // 16:(a + w) // 16]), current(t, h, u, w)[0], A.add, [("Et",), er, xr],
+               [("TM", lo, hi)], ind=GAT)
+            ts(T.MM[:, lo:hi], T.TM[:, lo:hi], 256.0, A.is_ge, [("TM", lo, hi)], [("MM", lo, hi)], -256.0, A.mult)
+        send(t, h, ["TM", "MM"])
 
     def firsts(t):
         top = 2048 + 512 * t
         l0 = ("fl", 0, 16)
         if t < 2:
-            act(T.depB[:, :], T.pb4[:, 0:256], [("pb4",)], [("depB",)])
+            act(T.depB[:, :], T.pb4[:, 0:256], [("pb4",)], [("depB",)], scale=64.0)
         gather("S", T.K5[:, :], ("K5",), T.Kt[:, 0:top], ("Kt", 0, top), T.fl[:, 0:16], l0)
-        u = 256 * t
-        gather("S", T.Rg[:, u:u + 256], ("Rg", u, u + 256), T.Rt[:, 0:top], ("Rt", 0, top), T.fl[:, 0:16], l0)
+        u = 1024 * t
+        if 0 not in R_ON_S[t]:
+            gather("S", T.Rg[:, u:u + 256], ("Rg", u, u + 256), T.Rt[:, 0:top], ("Rt", 0, top), T.fl[:, 0:16], l0)
         pe("pb4", [(T.pb4[:, 0:256], T.BDs[:, :], T.K5[:, :])], [("K5",), ("BDs",)])
         cp(T.fru[:, :], T.pb4[:, 0:256], [("pb4",)], [("fru",)])
-        pe("pb5", [(T.pb5[:, 0:256], T.BDi[:, :], T.K5[:, :])], [("K5",), ("BDi",)], last=False)
-        ts(T.fL[:, :], T.fl[:, 0:16], -float(OFF), A.add, [l0], [("fL",)])
+        pe("pb5", [(T.pb5[:, 0:256], T.idN[:, :], T.thrR[:, :]), (T.pb5[:, 0:256], T.BDi[:, :], T.K5[:, :])],
+           [("K5",), ("BDi",), ("idN",), ("thrR",)], last=False)
         for c in range(16):
             n = 256 - 16 * c
             e = ("E", 256 * c, 256 * c + n)
-            ts(T.E[:, 256 * c:256 * c + n], T.fru[:, 16 * c:256], T.fL[:, c:c + 1], A.is_equal, [("fru",), ("fL",), ("w16",)],
+            ts(T.E[:, 256 * c:256 * c + n], T.fru[:, 16 * c:256], T.pb0[:, 192 + c:193 + c], A.is_equal, [("fru",), ("pb0",), ("w16",)],
                [e], T.w16[:, c:c + 1], A.mult)
             pe("pb5", [(T.pb5[:, 16 * c:256], T.BD[:, :], T.E[:, 256 * c:256 * c + n])], [e, ("BD",)], False, c == 15)
-        tt(T.qB[:, :], T.pb5[:, 0:256], T.thrR[:, :], A.is_ge, [("pb5",), ("thrR",)], [("qB",)])
+        if Q_ON_S:
+            act(T.qB[:, :], T.pb5[:, 0:256], [("pb5",)], [("qB",)], func=AF.Sign)
+        else:
+            ts(T.qB[:, :], T.pb5[:, 0:256], 0.0, A.is_ge, [("pb5",)], [("qB",)], 2.0, A.mult)
 
     def lists(t):
         if t < 2:
             o = T[LB][:, 320:336]
-            pe(LB, [(o, T.idB[:, :], T.laneB[:, :])] + direct(o, 16, T.Q64, T.depB, 0), [("depB",), ("Q64",), ("idB",), ("laneB",)])
+            pe(LB, [(o, T.idB[:, :], T.laneB[:, :])] + direct(o, 16, T.Q01, T.depB, 0), [("depB",), ("Q01",), ("idB",), ("laneB",)])
             cp(T.depU[:, :], o, [(LB,)], [("depU",)])
             gather("S", T.xf[:, :], ("xf",), T[XP[t]][:, 0:NXP], (XP[t], 0, NXP), T.depU[:, :], ("depU",))
         o = T[LB][:, 300:316]
-        pe(LB, to_list(0, o, 16), [("Fz0",), ("RQ",)], last=False)
-        pe(LB, direct(o, 16, T.Q512, T.qB, 0), [("qB",), ("Q512",)], first=False)
+        pe(LB, to_list(0, o, 16), [("Fz", 0, 1), ("RQ",)], last=False)
+        pe(LB, direct(o, 16, T.Q256, T.qB, 0), [("qB",), ("Q256",)], first=False)
         tt(T.fo[:, :], o, T.dumpL[:, :], A.min, [(LB,), ("dumpL",)], [("fo",)])
-        ts(T.offU[:, :], T.fo[:, :], float(OFF), A.add, [("fo",)], [("offU",)])
+        ts(T.offU[:, :], T.fo[:, :], OFF + 4096.0 * Q_ON_S, A.add, [("fo",)], [("offU",)])
 
     def vterms(o, ident, t):
         m = 1024 * t
@@ -593,20 +725,23 @@ def rank_program(g, core, T, topo):
 
     def splits(t):
         u = 256 * t
-        rg, rgr, win, winr = T.Rg[:, u:u + 256], ("Rg", u, u + 256), T.winB[:, u:u + 256], ("winB", u, u + 256)
-        new, newr = T.NEW[:, u:u + 256], ("NEW", u, u + 256)
+        rg, rgr, win, winr = T.Rg[:, 4 * u:4 * u + 256], ("Rg", 4 * u, 4 * u + 256), T.winB[:, u:u + 256], ("winB", u, u + 256)
         d = T.pb4[:, 256:512]
+        lo, one, old = ("Dlo", "Done", "idMn") if t < 2 else ("Dhi", "D2", "MbN")
+        new = [(d, T.Dhi[:, :], T.NDhi[:, u:u + 256]), (d, T[lo][:, :], T.NDlo[:, :]), (d, T[one][:, :], T.ones[:, :]), (d, T[old][:, :], T.K5[:, :])]
+        newr = [("Dhi",), ("NDhi",), (lo,), ("NDlo",), (one,), ("ones",), (old,), ("K5",)]
         if t < 2:
-            pe("pb4", [(d, T.idB[:, :], new), (d, T.idMn[:, :], T.K5[:, :])], [newr, ("K5",), ("idB",), ("idMn",)])
+            pe("pb4", new, newr)
             cp(T.Zt[:, :].indirect(T.offU[:, :]), T.xf[:, :], [("xf",), ("offU",)], [("Zt",)], n=256, ind=SCA)
         else:
             pe("pb4", [(T.pb4[:, 0:256], T.Mb[:, :], T.K5[:, :])], [("K5",), ("Mb",)])
             act(T.old32[:, :], T.pb4[:, 0:256], [("pb4",)], [("old32",)])
-            pe("pb4", [(d, T.Mb[:, :], new), (d, T.MbN[:, :], T.K5[:, :])], [newr, ("K5",), ("Mb",), ("MbN",)])
-        o = T.pb0[:, 256:512]
+            pe("pb4", new, newr)
+        o = T.pb6[:, 256:512]
         terms, rd = vterms(o, "idN", t)
-        pe("pb0", [(o, T.idB[:, :], rg)] + terms, rd + [rgr, ("idB",)])
-        act(T.aB[:, :], o, [("pb0",)], [("aB",)], func=AF.Abs)
+        pe("pb6", [(o, T.idB[:, :], rg), terms[0]], [rd[0], rd[2], rgr, ("idB",)], last=False)
+        pe("pb6", terms[1:], rd[1:], first=False)
+        act(T.aB[:, :], o, [("pb6",)], [("aB",)], func=AF.Abs)
         o = T.pb5[:, 256:512]
         pe("pb5", [(o, T.idM[:, :], T.qB[:, :])], [("qB",), ("idM",)], last=False)
         pe("pb5", [(o, T.BD[:, :], T.aB[:, :])], [("aB",), ("BD",)], first=False)
@@ -620,15 +755,16 @@ def rank_program(g, core, T, topo):
 
     def new_r(t):
         u, n = 256 * t, 2048 + 512 * t
-        rg, rgr, win, winr = T.Rg[:, u:u + 256], ("Rg", u, u + 256), T.winB[:, u:u + 256], ("winB", u, u + 256)
+        rg, rgr, win, winr = T.Rg[:, 4 * u:4 * u + 256], ("Rg", 4 * u, 4 * u + 256), T.winB[:, u:u + 256], ("winB", u, u + 256)
         o = T.pb7[:, 0:256]
         pe("pb7", [(o, T.idB[:, :], rg), (o, T.idW[:, :], win)], [rgr, winr, ("idB",), ("idW",)])
-        act(T.Rt[:, n:n + 512:2], o, [("pb7",)], [("Rt", n, n + 512, "even")], func=AF.Relu, bias=-512.0)
+        act(T.Rt[:, n:n + 512:2], o, [("pb7",)], [("Rt", n, n + 512, "even")], func=AF.Relu, bias=-1024.0)
         o = T.pb6[:, 0:256]
-        terms, rd = vterms(o, "idH", t)
-        pe("pb6", [(o, T.idH[:, :], rg)] + terms + [(o, T.idW[:, :], win)], rd + [rgr, winr, ("idW",)])
-        ts(T.avI[:, :], o, -512.25, A.add, [("pb6",)], [("avI",)], 0.0, A.max)
-        cp(T.Rt[:, n + 1:n + 512:2], T.avI[:, :], [("avI",)], [("Rt", n, n + 512, "odd")])
+        terms, rd = vterms(o, "idB", t)
+        terms = [(o, T.idH[:, :], T.ones[:, :]), (o, T.idB[:, :], rg)] + terms + [(o, T.idW[:, :], win)]
+        pe("pb6", terms, rd + [rgr, winr, ("idW",), ("idH",), ("ones",)])
+        act(T.avF[:, :], o, [("pb6",)], [("avF",)], scale=0.5, bias=WHOLE - 512)
+        act(T.Rt[:, n + 1:n + 512:2], T.avF[:, :], [("avF",)], [("Rt", n, n + 512, "odd")], func=AF.Relu, bias=-WHOLE)
         me = dma("D", T.yr[:, 512 * t:512 * t + 512], T.Rt[:, n:n + 512], 512 * MB, [("Rt", n, n + 512)], [])
         if t == 2:
             lead.append(me)
@@ -641,45 +777,55 @@ def rank_program(g, core, T, topo):
                     paths(0, h, k)
                 pred(k, 1024 if k < 4 else 256)
             env_table()
+            cp(T.wS[:, :], T.wI[:, :], [("wI",)], [("wS",)])
+            remote("aw", src, dst, [([(T.wS[:, :], ("wS",))], (T.wN[:, :], ("wN",)))], 45.0)
+            ts(T.QN[:, :], T.Q01[:, :], T.wN[:, :], A.mult, [("Q01",), ("wN",)], [("QN",)])
         for h in H:
-            hsum(t, h)
+            if t - 1 not in SUMS_SENT:
+                tagged((t, h), hsum, t, h)
         if t > 0:
             for k in range(1, 5):
                 for h in H:
-                    paths(t, h, k)
+                    tagged((t, h), paths, t, h, k)
         if t < 2:
             xg("S", t, 5, 0, 256)
         for k in range(5):
             for h in H:
-                step(t, h, k)
+                tagged((t, h), step, t, h, k)
         if t == 0:
             new_nodes()
         if t == 1:
+            late_constants()
             for h in range(2):
                 gather("S", T.Cg[:, 512 * h:512 * h + 512], ("Cg", 512 * h, 512 * h + 512), T.Ct[:, :], ("Ct",), T.hl[:, 32 * h:32 * h + 32],
                        ("hl", 32 * h, 32 * h + 32))
             dma("D", T.yp[:, 0:1024], T.Cg[0:128:16, :], 32768, [("Cg",)], [])
         if t == 2:
-            ts(T.hF[:, :], T.hJ[:, 64:128], 4096.0, A.add, [("hJ", 64, 128)], [("hF",)])
+            ts(T.hF[:, :], T.hl[:, 64:128], 4096.0, A.add, [("hl", 64, 128)], [("hF",)])
             turn(T.hF[:, :], ("hF",), "hT", lambda e, a: T.yp[e:8:2, a:a + 512], None, 1024)
-            dma("G", T.Ko[:, :], T.Kt[:, 0:3840], 3840 * 512, [("Kt",)], [("Ko",)])
-            for i in (0, 2):
-                dma("G", T.Ko[i:128:16, 0:3584], T.Kt[i + 1:128:16, 0:3584], 3584 * 64, [("Kt",)], [("Ko", 0, 3840, "r%d" % i)],
-                    accum_op=A.add, max_dma_last_dim=4096)
-        firsts(t)
-        outcome(t, 0)
-        lists(t)
-        splits(t)
+            for i, nm in enumerate(("QK0", "QK1")):
+                bk, kb = "pb%d" % (6 + i), ("kB", 224 * i, 224 * i + 224)
+                pe(bk, block(T[bk][:, 0:224], 224, T[nm], T.Kt), [("Kt", 0, 3584), (nm,)])
+                act(T.kB[:, 224 * i:224 * i + 224], T[bk][:, 0:224], [(bk,)], [kb])
+                dma("D", T.Ko[2 * i:128:16, 0:3584], T.kB[:, 224 * i:224 * i + 224], 114688, [kb], [("Ko", 0, 3840, "r%d" % i)])
+        tagged((t, "s"), firsts, t)
+        tagged((t, "o", 0), outcome, t, 0)
+        tagged((t, "s"), lists, t)
+        tagged((t, "s"), splits, t)
         for h in H[1:]:
-            outcome(t, h)
+            tagged((t, "o", h), outcome, t, h)
         new_r(t)
     lead.append(dma("D", T.yk0[:, :], T.Ko[0:128:16, 0:3584], 114688, [("Ko",)], []))
     lead.append(dma("S", T.yk1[:, :], T.Ko[2:128:16, 0:3584], 114688, [("Ko",)], []))
-    terms = block(T.pb1[:, 384:448], 64, T.QW, T.XF)
-    for j in range(4):
-        pe("pb1", terms[4 * j:4 * j + 4], [("XF", 256 * j, 256 * j + 256), ("QW",)], j == 0, j == 3)
-    cp(T.yI[:, :], T.pb1[:, 384:448], [("pb1",)], [("yI",)])
+    o = T.pb7[:, 384:448]
+    todo = [(nm, r) for r in range(16) for h in H if 0 <= 64 * r - PARTS[h][0] < PARTS[h][1] for nm in made[2, h]]
+    todo.sort(key=lambda x: (x[1] // 4, x[0] != "TM"))
+    for j in range(0, len(todo), 4):
+        pe("pb7", [(o, T.QN[:, 15 - r:143 - r], T[nm][:, 2048 + 64 * r:2112 + 64 * r]) for nm, r in todo[j:j + 4]],
+           [(nm, 2048 + 64 * r, 2112 + 64 * r) for nm, r in todo[j:j + 4]] + [("QN",)], j == 0, j + 4 >= len(todo))
+    cp(T.yI[:, :], o, [("pb7",)], [("yI",)])
     ts(T.yJ[:, :], T.yI[:, :], 1023, A.bitwise_and, [("yI",)], [("yJ",)])
-    ts(T.ypF[:, :], T.yJ[:, :], 5120.0, A.add, [("yJ",)], [("ypF",)])
+    ts(T.ypS[:, :], T.yJ[:, :], 5120.0, A.add, [("yJ",)], [("ypS",)])
+    remote("ay", dst, src, [([(T.ypS[:, :], ("ypS",))], (T.ypF[:, :], ("ypF",)))], SMALL)
     dma("D", T.yp[:, 2048:3072], T.ypF[:, :], 32768, [("ypF",)], [])
     emit()

import math
from concourse.bass import DstId, RemoteDMATransfer
from concourse.mybir import dt, AluOpType, AxisListType, ActivationFunctionType

A = AluOpType
AF = ActivationFunctionType
PARTS = ((0, 512), (512, 512))
IB = ("pb2", "pb3")
LB = "pb2"
XS = ((384, 384), (416, 416), (416, 416))
BOTH, ALONE = ((("S", 0, 512), ("V", 512, 1024)),), ((("S", 0, 512), ("S", 512, 1024)),)
PRED = (BOTH, BOTH, BOTH, BOTH, BOTH)
R_ON_S = ((1,), (1,), ())
E_ON_S = ((), (), ())
LEAD = 0.0
XFIRST = 4096
XMID = 4096
AV_ON_S = (0, 1, 2)
SUMS_SENT = ()
SPREAD = 1
SMALL = 1.0
BOOST = 6
BIAS = {}
WHOLE = 12582912.0
PASSES = 2
TRIES, WARM, SEED = 5000, 0.06, 8
CASES = ((1.0, 1.0, 0.1, 0.3, 0.35, 0.0), (1.0, 0.8, 0.22, 0.28, 0.45, 0.4), (1.4, 1.8, 0.1, 0.3, 0.2, 0.0))
ORDER = {}
HOLD = 0.3
WAIT = 0.0
RUN = 4
BITS_FIRST = False
R_SPLIT = False
PLAN = []
BIG = 65536.0
NXP = 5 * 1024 + 256
OFF = 1792
EW = 3600
SCRATCH = {}


def _sb(dtype, text):
    for w in text.split():
        n, c = w.split(":")
        SCRATCH[n] = ("sbuf", [128, int(c)], dtype)


_sb("bfloat16", "xs:4096 Pt:4096 Kt:4096 Zt:3840 Rt:3584 Et:3600 XA:5376 XB:5376 XC:5376 QN:144 Pg:1024 Kg:1024 "
    "bt:1024 K5:256 Rg:3072 aB:256 E:4096 qB:256 winB:768 tK:256 xf:256 depB:256 NDlo:256 NDhi:768 SC:96 "
    "ones:256 zer:144 Qa:144 Qb:144 Q01:144 QP:144 QW:144 Q97:144 Q256:144 QK0:144 QK1:144 thrR:256 Dhi:128 Dlo:128 Done:128 D2:128 W1:8 WK:16 RQb:128 BD:128 BDs:128 BDi:128 "
    "BDf:128 idB:128 idN:128 idH:128 idM:128 idW:128 idMn:128 Mb:128 MbN:128 dg:640 pg:512 sfl:256 sfi:256 laneB:16")
_sb("float16", "TM:3072 MM:3072 CC:2048 RQ:128 id16:128 hs:192 fru:256")
_sb("float32", "kB:448 sc:288 wS:1 wN:1 ypS:64 onesF:128 BDF:128 w16:16 avF:256 laneL:16 dumpL:16 fo:16 col:32 thF:1 ypF:64 curF:64 curT:64 hF:64 hT:64 "
    "Ct:1024 Cg:1024 Ko:3840 old32:256 tK32:256")
_sb("int32", "prevI:256 kI:256 kH:256 curI:64 startI:64 wI:1 thI:1 pI:1 pmI:1 pnI:1 ownI:128 own2:128 hI:64 hJ:128 hK:64 yI:64 yJ:64")
_sb("uint16", "f0:64 fl:64 sl:384 hl:128 el:64 offU:16 depU:16")
SCRATCH["Fz"] = ("sbuf", [128, 3 * 36, 4], "float16")
for _i in range(8):
    SCRATCH["pb%d" % _i] = ("psum", [128, 512], "float32")

NDMA = 64
SEMAPHORES = ["sV", "sS", "sP", "sG", "loc"] + ["d%d" % i for i in range(NDMA)] + ["aw", "ay"] + [s + "%d%d" % (t, c) for s in "ab" for t in range(2) for c in range(4)]

CYC, PEC, GAT, SCA, HAND, DMA0, DMAB, REMOTE = 0.00083, 0.00039, 1.5, 3.7, 0.18, 1.5, 2.1e-6, 1.9
SELF, VFIX, VMIN, SFIX = 0.29, 0, 56, 0.07
Q_ON_S = True
WIDTH = {"bfloat16": 2, "float16": 2, "uint16": 2, "float32": 4, "int32": 4}


def rank_program(g, core, T, topo):
    rank = T.rank_of(core)
    if rank is None:
        return
    dst = T.cores[(rank + 1) % len(T.cores)]
    src = T.cores[(rank - 1) % len(T.cores)]

    QUEUE = {"V": g.vector, "S": g.scalar, "P": g.tensor, "G": g, "D": g.sync}
    SEM = {"V": "sV", "S": "sS", "P": "sP", "G": "sG"}
    ops = []
    recs = {}

    tags, tag_ = [], [None]

    def tagged(name, fn, *a):
        tag_[0] = name
        fn(*a)
        tag_[0] = None

    def norm(r):
        b = r[0]
        if len(r) == 1 or b.startswith("pb"):
            return (b, 0, 1 << 20, None)
        if len(r) == 3:
            return (b, r[1], r[2], None)
        return r

    def record(q, kind, calls, busy, done, reads, writes, sem=None, after=(), picked=0.0):
        me = len(ops)
        pred = {}
        for p in after:
            pred[p] = False
        for rs, w in ((reads, False), (writes, True)):
            for r in rs:
                b, lo, hi, tag = norm(r)
                ps = b.startswith("pb")
                for rec in recs.get(b, []):
                    if rec[2] <= lo or rec[1] >= hi or (tag is not None and rec[3] is not None and tag != rec[3]):
                        continue
                    if not ps and not w and not rec[0]:
                        continue
                    o = ops[rec[4]]
                    same = o[0] == q and o[1] == "op" and kind == "op"
                    pred[rec[4]] = pred.get(rec[4], False) or not (same and (ps or w))
        ops.append([q, kind, calls, busy, done, pred, sem, picked])
        tags.append(tag_[0])
        for rs, w in ((reads, False), (writes, True)):
            for r in rs:
                b, lo, hi, tag = norm(r)
                lst = recs.setdefault(b, [])
                if b.startswith("pb"):
                    recs[b] = [[True, lo, hi, tag, me]]
                    continue
                if w:
                    recs[b] = [x for x in lst if not (x[1] >= lo and x[2] <= hi and (tag is None or x[3] == tag))]
                recs[b].append([w, lo, hi, tag, me])
        return me

    def op(q, calls, cost, reads, writes, ind=0.0):
        if not isinstance(calls, list):
            calls = [calls]
        return record(q, "op", calls, cost, cost + (0.06 if q == "P" else 0), reads, writes, None, sent[:3] if q == "G" else (),
                      cost - 0.06 if ind > 1 else 0.0)

    ndma = [0]
    sent = []
    lead = []
    early = []

    def dma(q, out, in_, nbytes, reads, writes, after=(), **kw):
        s = "d%d" % ndma[0]
        ndma[0] += 1
        return record(q, "dma", lambda: QUEUE[q].dma_start(out, in_, **kw), 0.06 if q != "G" else 1.0, DMA0 + 0.2 + nbytes * DMAB, reads, writes, s, after)

    def emit():
        n = len(ops)
        for o in ops:
            if o[1] == "op" and any(o[5].values()):
                o[3] += WAIT
                o[4] += WAIT
        succ = [[] for _ in ops]
        for i, o in enumerate(ops):
            for p in o[5]:
                succ[p].append(i)

        def gap(p, i):
            return ops[p][4] + (SELF if ops[p][:2] == ops[i][:2] else HAND) if ops[i][5][p] else ops[p][3]
        level = [0.0] * n
        for i in range(n - 1, -1, -1):
            level[i] = max([gap(i, j) + level[j] for j in succ[i]] + [ops[i][4] + (LEAD if i in lead else 0)])

        def place(order, back):
            at, taken = [0.0] * n, {}
            for i in order:
                if back:
                    t = max([at[j] + gap(i, j) for j in succ[i]] + [ops[i][4]])
                else:
                    t = max([at[p] + gap(p, i) for p in ops[i][5]] + [0.0])
                uses = [(ops[i][0], 0.0, ops[i][3])]
                if ops[i][1] == "dma":
                    uses.append(("engines", DMA0, ops[i][4]))
                if back:
                    uses = [(q, -hi, -lo) for q, lo, hi in uses]
                moved = True
                while moved:
                    moved = False
                    for q, lo, hi in uses:
                        for a, b in taken.setdefault(q, []):
                            if a >= t + hi:
                                break
                            if t + lo < b - 1e-9 and t + hi > a + 1e-9:
                                t, moved = b - lo, True
                for q, lo, hi in uses:
                    taken[q].append((t + lo, t + hi))
                    taken[q].sort()
                at[i] = t
            return at

        def length(at):
            return max(at[i] + ops[i][4] for i in range(n))

        def ranked(key, back):
            key = list(key)
            for i in (range(n) if back else range(n - 1, -1, -1)):
                for j in (ops[i][5] if back else succ[i]):
                    key[i] = max(key[i], key[j] + 1e-6)
            return sorted(range(n), key=lambda i: -key[i])
        lv = list(level)
        for i in range(n - 1, -1, -1):
            lv[i] = max([gap(i, j) + lv[j] for j in succ[i]] + [level[i] + (BOOST if i in early else 0)])
        start = best = place(ranked([lv[i] + BIAS.get(tags[i], 0) for i in range(n)], False), False)
        for _ in range(PASSES):
            late = place(ranked([start[i] + ops[i][4] for i in range(n)], True), True)
            start = place(ranked(late, False), False)
            if length(start) < length(best):
                best = start
        cases = []
        for plain, picked, hand, own, _, far in CASES:
            more = [(o[3] - o[7]) * (plain - 1) + o[7] * (picked - 1) if o[1] == "op" else far * (o[1] == "arrival") for o in ops]
            cases.append(([o[3] + m * (o[1] == "op") for o, m in zip(ops, more)],
                          [[(p, more[p] + (ops[p][4] + (own if ops[p][:2] == o[:2] else hand) if w else ops[p][3]), w) for p, w in o[5].items()]
                           for o in ops]))

        def once(order, busy, before):
            at, why, late, free, last, engines = [0.0] * n, [-1] * n, [0.0] * n, {}, {}, 0.0
            for i in order:
                q = ops[i][0]
                t, w = free.get(q, 0.0), last.get(q, -1)
                for p, d, waits in before[i]:
                    u = at[p] + d + (late[p] if waits else 0.0)
                    if u > t:
                        t, w = u, p
                at[i], why[i], free[q], last[q] = t, w, t + busy[i], i
                if ops[i][1] == "dma":
                    late[i] = max(0.0, engines - t - DMA0)
                    engines = t + late[i] + ops[i][4]
            end = max(range(n), key=lambda i: at[i] + late[i] + ops[i][4])
            return at[end] + late[end] + ops[end][4], at, why, end

        def run(order):
            runs = [once(order, *c) for c in cases]
            return sum(r[0] * c[4] for r, c in zip(runs, CASES)), runs[0][1], [r[2] for r in runs], [r[3] for r in runs]

        def polish(at):
            seed = [SEED]

            def draw():
                seed[0] = (seed[0] * 1103515245 + 12345) % 2147483648
                return seed[0] / 2147483648
            order = sorted(range(n), key=lambda i: (at[i], i))
            now, at, whys, ends = run(order)
            least = (now, at)
            for it in range(TRIES):
                held, i, why = [], ends[it % len(CASES)], whys[it % len(CASES)]
                while why[i] >= 0:
                    if ops[why[i]][0] == ops[i][0] and why[i] not in ops[i][5]:
                        held.append((why[i], i))
                    i = why[i]
                if not held:
                    continue
                a, b = held[int(draw() * len(held))]
                lo, hi = order.index(a), order.index(b)
                for _ in range(int(draw() * 10) - 6):
                    lo = max([k for k in range(max(0, lo - 40), lo) if ops[order[k]][0] == ops[a][0]] + [-1]) if lo > 0 else -1
                    if lo < 0:
                        break
                if lo < 0:
                    continue
                a, piece = order[lo], order[lo:hi + 1]
                if draw() < 0.5:
                    need = set(ops[b][5])
                    first = {b}
                    for x in piece[-2::-1]:
                        if x in need:
                            first.add(x)
                            need.update(ops[x][5])
                    if a in first:
                        continue
                else:
                    second = {a}
                    for x in piece[1:]:
                        if not second.isdisjoint(ops[x][5]):
                            second.add(x)
                    if b in second:
                        continue
                    first = set(piece) - second
                other = order[:lo] + [x for x in piece if x in first] + [x for x in piece if x not in first] + order[hi + 1:]
                t, at2, why2, end2 = run(other)
                if t < now or draw() < math.exp((now - t) / (WARM * (1 - it / TRIES) + 0.005)):
                    now, at, whys, ends = t, at2, why2, end2
                    order = sorted(other, key=lambda i: at[i])
                    if now < least[0]:
                        least = (now, at)
            return least[1]
        if n not in ORDER:
            ORDER[n] = polish(best)
        start = best = ORDER[n]
        PLAN[:] = [(length(best), max(level), ops, level, start)]
        total, seen, mark, known = {}, {}, {}, {}
        for i in sorted(range(n), key=lambda i: (start[i], i)):
            q, kind, calls, _, _, pred, sem, _ = ops[i]
            if kind == "arrival":
                mark[i], known[i] = (sem, calls), {}
                total[sem] = calls
                continue
            mine = seen.setdefault(q, {})
            for p in sorted((p for p in pred if pred[p]), key=lambda p: -start[p]):
                s, v = mark[p]
                if mine.get(s, 0) < v:
                    QUEUE[q].wait_ge(T.sem[s], v)
                    mine[s] = v
                    for s, v in known[p].items():
                        mine[s] = max(mine.get(s, 0), v)
            known[i] = dict(mine)
            if kind == "dma":
                calls().then_inc(T.sem[sem], 16)
                total[sem] = 16
                mark[i] = (sem, 16)
            elif kind == "send":
                total["loc"] = total.get("loc", 0) + calls()
            else:
                s = SEM[q]
                for c in calls:
                    c().then_inc(T.sem[s], 1)
                total[s] = total.get(s, 0) + len(calls)
                mark[i] = (s, total[s])
        for s in total:
            if seen["G"].get(s, 0) < total[s]:
                g.wait_ge(T.sem[s], total[s])

    V = g.vector

    def count(ap):
        return math.prod(ap.shape[1:])

    def vcost(n, rd, wr, two=False, ind=0.0):
        if ind:
            return 0.05 + n * ind * CYC
        psum = any(r[0].startswith("pb") for r in rd + wr)
        narrow = WIDTH[SCRATCH[rd[0][0]][2]] == 2 and WIDTH[SCRATCH[wr[0][0]][2]] == 2
        return VFIX + CYC * max(VMIN, n * ((1 if psum else 2) if two else (0.5 if narrow else 1)))

    def cp(out, in_, rd, wr, n=None, ind=0.0):
        return op("V", lambda: V.tensor_copy(out=out, in_=in_), vcost(n or count(out), rd, wr, False, ind), rd, wr, ind)

    def tt(out, a, b, o, rd, wr, ind=0.0):
        return op("V", lambda: V.tensor_tensor(out=out, in0=a, in1=b, op=o), vcost(count(b), rd, wr, True, ind), rd, wr, ind)

    def ts(out, a, s1, o1, rd, wr, s2=None, o2=None):
        c = vcost(count(out), rd, wr)
        if o2 is None:
            return op("V", lambda: V.tensor_scalar(out=out, in0=a, scalar1=s1, scalar2=None, op0=o1), c, rd, wr)
        return op("V", lambda: V.tensor_scalar(out=out, in0=a, scalar1=s1, scalar2=s2, op0=o1, op1=o2), c, rd, wr)

    def fill(name, lo, hi, v):
        r = (name, lo, hi)
        op("V", lambda: V.memset(T[name][:, lo:hi], v), vcost(hi - lo, [r], [r]), [], [r])

    def act(out, in_, rd, wr, func=AF.Copy, ind=1.0, more=0.0, **kw):
        op("S", lambda: g.scalar.activation(out=out, in_=in_, func=func, **kw), (0.065 if ind > 1 else SFIX) + more + count(out) * ind * CYC, rd, wr, ind)

    def gather(eng, out, outr, win, winr, lst, lstr):
        if eng == "S":
            act(out, win.indirect(lst), [winr, lstr], [outr], ind=GAT)
        else:
            cp(out, win.indirect(lst), [winr, lstr], [outr], ind=GAT)

    def pe(bank, terms, rd, first=True, last=True, wide=1, alone=False):
        n = len(terms)
        for a in range(0, n, RUN):
            calls, cost = [], 0.0
            for i in range(a, min(a + RUN, n)):
                o, l, r = terms[i]
                st, sp = alone or (first and i == 0), alone or (last and i == n - 1)
                calls.append(lambda o=o, l=l, r=r, st=st, sp=sp: g.tensor.matmul(o, l, r, st, sp))
                cost += wide * max(64, count(r)) * PEC
            op("P", calls, cost, rd, [(bank,)])

    def direct(out, n, Q, data, base):
        return [(out, Q[:, 15 - r:143 - r], data[:, base + r:base + 16 * n:16]) for r in range(16)]

    def block(out, n, Q, data):
        return [(out, Q[:, 15 - r:143 - r], data[:, n * r:n * r + n]) for r in range(16)]

    def iota(name, lo, hi, pattern, base, cm):
        ap = T[name][:, lo:hi]
        kw = {} if SCRATCH[name][2] == "int32" else {"allow_small_or_imprecise_dtypes": True}
        op("G", lambda: g.iota(ap, pattern, base, cm, **kw), 0.13 + 2 * (hi - lo) * CYC, [], [(name, lo, hi)])

    def sel(name, src_, n, pattern, cmp, v, base, cm):
        op("G", lambda: g.affine_select(T[name][:, 0:n], T[src_][:, 0:n], pattern, cmp, float(v), base, cm), 0.17 + 2 * n * CYC,
           [(src_, 0, n)], [(name, 0, n)])

    C = {}

    def column(nm):
        i = len(C)
        C[nm] = (T.col[:, i:i + 1], ("col", i, i + 1))
        return C[nm]

    MB = 128 * 2
    small = [dma("D", T.prevI[:, :], T.prev[:, :], 131072, [], [("prevI",)]),
             dma("S", T.kI[:, 0:128], T.kid0[:, :], 65536, [], [("kI", 0, 128)]),
             dma("D", T.kI[:, 128:256], T.kid1[:, :], 65536, [], [("kI", 128, 256)]),
             dma("S", T.curI[:, :], T.cur[:, :], 32768, [], [("curI",)]),
             dma("D", T.startI[:, :], T.start[:, :], 32768, [], [("startI",)])]
    big = dma("D", T.xs[:, 0:XFIRST], T.x[:, 0:XFIRST], XFIRST * MB, [], [("xs", 0, XFIRST)], small)
    dma("S", T.wI[:, :], T.w[:, :], 512, [], [("wI",)], small)

    fill("ones", 0, 256, 1.0)
    fill("zer", 0, 144, 0.0)
    for a in range(0, 4096, 1024):
        fill("Pt", a, a + 1024, 1.0)
    for a in (0, 1024):
        act(T.Kt[:, a:a + 1024], T.Pt[:, a:a + 1024], [("Pt", a, a + 1024)], [("Kt", a, a + 1024)])
    for h in range(len(PARTS)):
        cp(T.Fz[:, 36 * h:36 * h + 36, :], T.zer[:, :], [("zer",)], [("Fz", h, h + 1)])
    for j, v in enumerate((1, 8, -9)):
        op("V", lambda j=j, v=v: V.memset(T.SC[:, j:96:3], v * BIG), 0.07, [], [("SC", 0, 96, "c%d" % j)])
    GR = [-16, 8]
    sel("W1", "zer", 8, [GR], A.is_ge, 1, -16, 1)
    sel("W1", "W1", 8, [GR], A.is_ge, 0, 0, 1)
    for j, (half, below, v) in enumerate(((0, 4, -1 / BIG), (1, 4, -8), (0, 2, 1 / BIG), (1, 2, 9))):
        sel("WK", "WK" if j else "zer", 16, [[1000 - 2000 * half, 2], GR], A.is_ge, v, 1000 * half - below, 1)
    sel("WK", "WK", 16, [[0, 2], GR], A.is_ge, 0, 0, 1)
    sel("WK", "WK", 16, [[1000, 2], GR], A.not_equal, -OFF, -1013, 1)
    sel("Qa", "ones", 144, [[0, 9], [1, 16]], A.is_equal, 0, -15, 0)
    sel("Qb", "Qa", 144, [[16, 9], [0, 16]], A.is_ge, 0, 15, -1)
    sel("QP", "Qb", 144, [[-16, 9], [0, 16]], A.is_ge, 0, -14, 1)
    sel("Q01", "Qb", 144, [[-16, 9], [0, 16]], A.is_ge, 0, 0, 1)
    sel("RQb", "ones", 128, [[-1, 4], [-4, 32]], A.is_equal, 0, 0, 1)
    cp(T.RQ[:, :], T.RQb[:, :], [("RQb",)], [("RQ",)])
    iota("ownI", 0, 128, [[1, 128]], 0, 128)
    iota("pI", 0, 1, [[0, 1]], 0, 1)
    iota("sfl", 0, 256, [[1, 256]], 0, 0)
    iota("laneL", 0, 16, [[16, 16]], 0, 0)
    iota("NDlo", 0, 256, [[0, 2], [2, 128]], 0, 0)
    for nm, v in (("idB", 1), ("idN", -1), ("idH", -0.5), ("idM", -4096), ("idW", 1024)):
        sel(nm, "zer", 128, [[-1, 128]], A.not_equal, v, 0, 1)
    cp(T.id16[:, :], T.idB[:, :], [("idB",)], [("id16",)])
    for h in range(len(PARTS)):
        pe("pb%d" % h, [(T["pb%d" % h][:, 1:96:3], T.idN[:, :], T.ones[:, 0:32])], [("idN",), ("ones",)])
    PL = [GR, [0, 16]]
    sel("BD", "ones", 128, PL, A.is_ge, 0, 0, 1)
    sel("BD", "BD", 128, [[16, 8], [0, 16]], A.is_ge, 0, 15, -1)
    sel("BDf", "zer", 128, PL, A.not_equal, 1, -4, 1)
    sel("BDs", "zer", 128, PL, A.not_equal, 1, 0, 1)
    sel("BDs", "BDs", 128, PL, A.not_equal, 1, -1, 1)
    sel("BDs", "BDs", 128, PL, A.not_equal, -OFF, -13, 1)
    fill("onesF", 0, 128, 1.0)
    sel("BDF", "onesF", 128, PL, A.is_ge, 0, 0, 1)
    sel("BDF", "BDF", 128, [[16, 8], [0, 16]], A.is_ge, 0, 15, -1)

    cp(T.f0[:, :], T.startI[:, :], [("startI",)], [("f0",)])
    cp(T.sl[:, 0:64], T.curI[:, :], [("curI",)], [("sl", 0, 64)])
    cp(T.pg[:, 0:256], T.prevI[:, :], [("prevI",)], [("pg", 0, 256)])
    tt(T.pg[:, 256:512], T.prevI[:, :], T.pg[:, 0:256], A.subtract, [("prevI",), ("pg", 0, 256)], [("pg", 256, 512)])
    rows = [dma("D", T.Pt[14 + j:128:16, :], T.pg[:, 256 * j:256 * j + 256], 65536, [("pg", 256 * j, 256 * j + 256)],
                [("Pt", 0, 4096, "r%d" % (14 + j))], [big]) for j in range(2)]
    if XFIRST < XMID:
        big = dma("D", T.xs[:, XFIRST:XMID], T.x[:, XFIRST:XMID], (XMID - XFIRST) * MB, [], [("xs", XFIRST, XMID)], rows)
    ts(T.kH[:, :], T.kI[:, :], 0xF00, A.bitwise_and, [("kI",)], [("kH",)])
    cp(T.dg[:, 0:256], T.kH[:, :], [("kH",)], [("dg", 0, 256)])
    tt(T.dg[:, 256:512], T.kI[:, :], T.kH[:, :], A.subtract, [("kI",), ("kH",)], [("dg", 256, 512)])
    ts(T.own2[:, :], T.ownI[:, :], 2047, A.bitwise_and, [("ownI",)], [("own2",)])
    tt(T.dg[:, 512:640], T.kI[:, 0:128], T.own2[:, :], A.not_equal, [("kI", 0, 128), ("own2",)], [("dg", 512, 640)])
    for i, j in ((0, 0), (1, 2), (2, 1), (3, 3), (4, 4)):
        rows.append(dma("D", T.Kt[i:128:16, 0:2048], T.dg[:, 128 * j:128 * j + 128], 32768, [("dg", 128 * j, 128 * j + 128)],
                        [("Kt", 0, 2048, "r%d" % i)], [big]))
    if XMID < 4096:
        rows.append(dma("D", T.xs[:, XMID:4096], T.x[:, XMID:4096], (4096 - XMID) * MB, [], [("xs", XMID, 4096)], rows))
    dma("D", T.Zt[:, 0:2048], T.z[:, :], 2048 * MB, [], [("Zt", 0, 2048)], rows)

    pm, pmr = column("pm")
    ts(T.pmI[:, :], T.pI[:, :], 15, A.bitwise_and, [("pI",)], [("pmI",)])
    cp(pm, T.pmI[:, :], [("pmI",)], [pmr])
    wc, wcr = column("w")
    cp(wc, T.wI[:, :], [("wI",)], [wcr])
    ts(T.QW[:, :], T.Q01[:, :], wc, A.mult, [("Q01",), wcr], [("QW",)])
    for nm, v in (("Q97", 97), ("Q256", 256)):
        sel(nm, "zer", 144, [[0, 9], [1, 16]], A.not_equal, v, -15, 0)
        sel(nm, nm, 144, [[16, 9], [0, 16]], A.is_ge, 0, 15, -1)
        sel(nm, nm, 144, [[-16, 9], [0, 16]], A.is_ge, 0, 0, 1)
    ts(T.BDi[:, :], T.BDf[:, :], 1e18, A.mult, [("BDf",)], [("BDi",)], 1e18, A.mult)
    ts(T.laneL[:, :], T.laneL[:, :], pm, A.add, [("laneL",), pmr], [("laneL",)])
    cp(T.laneB[:, :], T.laneL[:, :], [("laneL",)], [("laneB",)])
    ts(T.dumpL[:, :], T.laneL[:, :], 3584.0 - OFF - 4096 * Q_ON_S, A.add, [("laneL",)], [("dumpL",)])
    LN = math.log(1.85)
    act(T.w16[:, :], T.laneL[:, :], [("laneL",)], [("w16",)], func=AF.Exp, more=1.3, scale=-LN, bias=128 * LN)
    act(T.thrR[:, :], T.sfl[:, :], [("sfl",), ("w16",)], [("thrR",)], func=AF.Exp, scale=-LN, bias=128 * LN + math.log(2.5))
    sel("idMn", "idN", 128, [[16, 8], [0, 16]], A.is_ge, 0, 4, -1)
    for nm, places in (("Dhi", (0, 2)), ("Dlo", (1, 3)), ("Done", (3, 4))):
        for j, i in enumerate(places):
            sel(nm, nm if j else "zer", 128, [GR, [999, 16]], A.not_equal, 1, -1000 * i, 1)
    iota("NDhi", 0, 768, [[256, 6], [0, 128]], 2048, 0)
    fill("thI", 0, 1, 0)
    dma("D", T.thI[0:128:16, :], T.th[:, :], 32, [], [("thI",)])
    cp(T.thF[:, :], T.thI[:, :], [("thI",)], [("thF",)])
    pe("pb5", [(T.pb5[:, 0:1], T.BDF[:, :], T.thF[:, :])], [("BDF",), ("thF",)], wide=4)
    thc, thr = column("th")
    ts(thc, T.pb5[:, 0:1], 4096.0 * Q_ON_S, A.add, [("pb5",)], [thr])
    gate = [("XA", 1024, 1040)]
    iota("Zt", 2048, 3072, [[0, 1024]], 0, 0)
    for a in (2048, 2560, 3072):
        iota("Kt", a, a + 512, [[0, 512]], 1, 0)
    pe_, per = column("pe")
    ts(T.pnI[:, :], T.pI[:, :], 7, A.bitwise_and, [("pI",)], [("pnI",)])
    ts(pe_, T.pnI[:, :], 256.0, A.mult, [("pnI",)], [per], 2048.0, A.add)
    act(T.sfi[:, :], T.sfl[:, :], [("sfl",), per], [("sfi",)], func=AF.Identity, scale=0.0, bias=pe_)

    def env_table():
        dma("D", T.Rt[:, 0:2048], T.rs[:, :], 2048 * MB, gate, [("Rt", 0, 2048)])
        dma("D", T.Et[:, 0:2048], T.env[:, :], 2048 * MB, gate, [("Et", 0, 2048)])
        dma("D", T.Et[:, 2048:EW], T.env[:, 0:EW - 2048], 1552 * MB, gate, [("Et", 2048, EW)])

    def new_nodes():
        for i in range(5):
            if i < 4:
                nm = ("sfi", "sfl")[i % 2]
                dma("D", T.Kt[i:128:16, 2048:4096], T[nm][0:64, :], 32768, [(nm,)], [("Kt", 2048, 4096, "r%d" % i)])
            else:
                dma("D", T.Kt[i:128:16, 2048:4096], T.zer[:, 0:128], 32768, [("zer",)], [("Kt", 2048, 4096, "r%d" % i)])

    def turn(lst, lstr, buf, to, tor, col):
        op("V", lambda: V.transpose(T[buf][:, :], lst), 0.05 + 64 * CYC, [lstr], [(buf,)])
        for e in range(2):
            for b in range(2):
                a = col + 512 * b
                dma("D", to(e, a), T[buf][:, 32 * b + 16 * e:32 * b + 16 * e + 16], 8192, [(buf,)],
                    [tor + ("e%d%d" % (e, b),)] if tor else [])

    def late_constants():
        iota("Ct", 0, 1024, [[0, 1024]], 0, 0)
        cp(T.curF[:, :], T.curI[:, :], [("curI",)], [("curF",)])
        turn(T.curF[:, :], ("curF",), "curT", lambda e, a: T.Ct[16 * e:128:32, a:a + 512], ("Ct", 0, 1024), 0)
        sel("QK0", "Q01", 144, [[16, 9], [0, 16]], A.is_ge, 0, 1, -1)
        sel("QK1", "Q01", 144, [[16, 9], [0, 16]], A.is_ge, 0, 3, -1)
        sel("QK1", "QK1", 144, [[-16, 9], [0, 16]], A.is_ge, 0, -2, 1)
        sel("Mb", "idB", 128, [[-1, 128]], A.not_equal, 1, -1, 1)
        sel("MbN", "idN", 128, [[-1, 128]], A.not_equal, -1, -1, 1)
        sel("D2", "zer", 128, [GR, [999, 16]], A.not_equal, 1, -2000, 1)

    XP = ["XA", "XB", "XC", "XF"]

    def cols(name, h, base=0):
        a, n = PARTS[h]
        lo, hi = base + a // 16, base + (a + n) // 16
        return T[name][:, lo:hi], (name, lo, hi)

    def lanes(name, h, base=0):
        a, n = PARTS[h]
        return T[name][:, base + a:base + a + n], (name, base + a, base + a + n)

    def current(t, h, u=0, w=None):
        a, n = PARTS[h]
        name, base = ("CC", 1024 * t - 1024) if t else ("XA", 0)
        lo, hi = base + a + u, base + a + (w or n)
        return T[name][:, lo:hi], (name, lo, hi)

    def to_list(h, out, n):
        m = PARTS[h][1] // 4
        return [(out, T.Fz[0:m, 36 * h + 3 - q:36 * h + 35 - q, :], T.RQ[0:m, 32 * q:32 * q + n]) for q in range(4)]

    def step(t, h, k):
        l, r = cols("fl" if k else "f0", h)
        (a, n), top, bank = PARTS[h], 2048 + 512 * t, "pb%d" % h
        pb, F, m = T[bank], ("Fz", h, h + 1), n // 4
        (kg, kgr), (bt, btr), (x, xr) = lanes("Kg", h), lanes("bt", h), lanes(XP[t], h, 1024 * k) if k else current(t, h)
        act(kg, T.Kt[:, 0:top].indirect(l), [("Kt", 0, top), r], [kgr], ind=GAT)
        tt(bt, T.Zt[:, 0:top].indirect(l), x, A.is_le, [("Zt", 0, top), r, xr], [btr], ind=GAT)
        both = [([(pb[0:m, 3 * j + 2:192:12], T.Kg[:, a + j:a + n:4], T.WK[:, :]) for j in range(4)], [kgr, ("WK",)]),
                ([(pb[0:m, 3 * j:96:12], T.bt[:, a + j:a + n:4], T.W1[:, :]) for j in range(4)], [btr, ("W1",)])]
        for terms, rd in both[::-1] if (k > 0 or t == 0) and BITS_FIRST else both:
            pe(bank, terms, rd, alone=True)
        if h == 0 and t < 2:
            pe("pb4", [(T.pb4[:, 0:256], T.BDf[:, :], T.Kg[:, 0:256])], [("Kg", 0, 256), ("BDf",)], k == 0, k == 4)
        c, scr = 96 * h, ("sc", 96 * h, 96 * h + 96)
        op("V", lambda: V.tensor_tensor_scan(T.sc[0:m, c:c + 96], T.SC[0:m, :], pb[0:m, 0:96], 0.0, A.max, A.mult), VFIX + 96 * CYC,
           [("SC",), (bank,)], [scr])
        tt(T.Fz[0:m, 36 * h + 3:36 * h + 35:4, :], pb[0:m, 98:192:3], T.sc[0:m, c + 2:c + 96:3], A.add, [(bank,), scr], [F])
        o = pb[:, 192:192 + n // 16]
        pe(bank, to_list(h, o, n // 16), [F, ("RQ",)])
        l, r = cols("fl", h)
        ts(l, o, float(OFF), A.add, [(bank,)], [r])

    def xg(eng, t, k, a, b):
        if a >= b:
            return
        o = 1024 * k
        out, outr = T[XP[t]][:, o + a:o + b], (XP[t], o + a, o + b)
        if t == 0:
            lo, hi = 64 * k + a // 16, 64 * k + b // 16
            gather(eng, out, outr, T.xs[:, :], ("xs",), T.sl[:, lo:hi], ("sl", lo, hi))
        else:
            w, lo, hi = 1024 * (k - 1), 64 * (t - 1) + a // 16, 64 * (t - 1) + b // 16
            gather(eng, out, outr, T[XP[t - 1]][:, w:w + 1024], (XP[t - 1], w, w + 1024), T.hl[:, lo:hi], ("hl", lo, hi))

    def paths(t, h, k):
        a, n = PARTS[h]
        xg("S", t, k, a, a + XS[t][h])
        xg("V", t, k, a + XS[t][h], a + n)

    def pred(k, n):
        for j, who in enumerate(PRED[k]):
            for eng, a, b in who:
                if a < min(b, n):
                    b = min(b, n)
                    lo, hi = 64 * k + a // 16, 64 * k + b // 16
                    gather(eng, T.Pg[:, a:b], ("Pg", a, b), T.Pt[:, :], ("Pt",), T.sl[:, lo:hi], ("sl", lo, hi))
            a, b, bank = who[0][1], min(who[-1][2], n), "pb%d" % (7 - j)
            if a < b:
                m, lo = (b - a) // 16, 64 * k + 64 + a // 16
                pe(bank, direct(T[bank][:, 0:m], m, T.QP, T.Pg, a), [("Pg", a, b), ("QP",)])
                early.append(cp(T.sl[:, lo:lo + m], T[bank][:, 0:m], [(bank,)], [("sl", lo, lo + m)]))

    def hsum(t, h):
        (a, n), bank = PARTS[h], IB[h]
        o = T[bank][:, 224:224 + n // 16]
        there = t - 1 in SUMS_SENT
        if there:
            for j, nm in enumerate(made[t - 1, h]):
                pe(bank, direct(o, n // 16, T.QN, T[nm], 1024 * t - 1024 + a), [lanes(nm, h, 1024 * t - 1024)[1], ("QN",)], j == 0,
                   j == len(made[t - 1, h]) - 1)
        else:
            pe(bank, direct(o, n // 16, T.QW, T.CC if t else T.XA, a + (1024 * t - 1024 if t else 0)), [current(t, h)[1], ("QW",)])
        if t == 1:
            bk = "pb%d" % (6 + h % 2)
            pe(bk, [(T[bk][:, 0:n], T.id16[:, :], current(t, h)[0])], [current(t, h)[1], ("id16",)])
            act(lanes("XB", h)[0], T[bk][:, 0:n], [(bk,)], [lanes("XB", h)[1]])
        hi, hir = cols("hI", h)
        cp(hi, o, [(bank,)], [hir])
        pieces = []
        for want, bits, mid, out, base in ((t > 0, 1023, "hJ", "hl", 64 * t - 64), (True, 2047, "hK", "hs", 64 * t)):
            if want:
                (u, ur), (w, wr) = cols(mid, h), cols(out + "S" * there, h, base)
                ts(u, hi, bits, A.bitwise_and, [hir], [ur])
                cp(w, u, [ur], [wr])
                pieces.append(([(w, wr)], cols(out, h, base)))
        if there:
            remote("b%d%d" % (t - 1, h), dst, src, pieces, SMALL)

    def remote(s, to, frm, pieces, time):
        rid, pid, _ = topo.addr(to)
        en = topo.engines(core, to)[::SPREAD]
        m = len(en) // len(pieces)

        def call():
            g.remote_dma_fused([RemoteDMATransfer(dst_ids=[DstId(rid=rid, pnc=pid)], dma_engine_mask=sum(1 << x for x in en[m * j:m * j + m]),
                                                  remote_sem=T.sem[s], srcs=[a for a, _ in srcs], dsts=[out[0]], alu_op=int(len(srcs) > 1))
                                for j, (srcs, out) in enumerate(pieces)], local_sem=T.sem.loc)
            return len(en)
        me = record("G", "send", call, HOLD, HOLD, [r for srcs, _ in pieces for _, r in srcs], [])
        sent.append(me)
        record("R", "arrival", len(topo.engines(frm, core)[::SPREAD]), 0.001, time + 0.3 - HOLD, [], [out[1] for _, out in pieces], s, [me])

    made = {}

    def send(t, h, names):
        made[t, h] = names
        if t < 2:
            remote("a%d%d" % (t, h), dst, src, [([lanes(nm, h, 1024 * t) for nm in names], current(t + 1, h))], REMOTE * (0.5 + PARTS[h][1] / 1024))
            if t in SUMS_SENT:
                hsum(t + 1, h)

    def outcome(t, h):
        (a, n), bank, top = PARTS[h], IB[h], 2048 + 512 * t
        (l, r), (x, xr), (bt, btr) = cols("fl", h), current(t, h), lanes("bt", h)
        on_s = h in R_ON_S[t]
        if on_s:
            (rb, rbr), bk = lanes("Rg", h, 1024 * t), "pb%d" % (6 + h % 2)
            p = T[bk][:, 0:n]
            gather("S", rb, rbr, T.Rt[:, 0:top], ("Rt", 0, top), l, r)
            pe(bk, [(p, T.idN[:, :], x)], [xr, ("idN",)], last=False)
            pe(bk, [(p, T.idB[:, :], rb)], [rbr, ("idB",)], first=False)
            act(bt, p, [(bk,)], [btr], func=AF.Sign, bias=-0.5)
        pieces = ((0, n),) if a or n == 256 else ((0, 256), (256, n))
        for u, w in pieces if R_SPLIT and not on_s else ((0, n),):
            c, d = (a + u) // 16, (a + w) // 16
            br = ("bt", a + u, a + w)
            if not on_s:
                tt(T.bt[:, a + u:a + w], T.Rt[:, 0:top].indirect(T.fl[:, c:d]), current(t, h, u, w)[0], A.is_gt, [("Rt", 0, top), r, xr], [br], ind=GAT)
            o = T[bank][:, 256 + u // 16:256 + w // 16]
            pe(bank, [(o, T.id16[:, :], T.hs[:, 64 * t + c:64 * t + d])] * (1 + on_s), [("id16",), ("hs", 64 * t + c, 64 * t + d)], last=False)
            pe(bank, direct(o, d - c, T.Q97, T.bt, a + u), [br, ("Q97",)], first=False)
            if on_s:
                ts(T.el[:, c:d], o, 0.5, A.mult, [(bank,)], [("el", c, d)], 776.0, A.add)
            else:
                cp(T.el[:, c:d], o, [(bank,)], [("el", c, d)])
        for u, w in pieces:
            er = ("el", (a + u) // 16, (a + w) // 16)
            lo, hi = 1024 * t + a + u, 1024 * t + a + w
            tt(T.TM[:, lo:hi], T.Et[:, :].indirect(T.el[:, (a + u) // 16:(a + w) // 16]), current(t, h, u, w)[0], A.add, [("Et",), er, xr],
               [("TM", lo, hi)], ind=GAT)
            ts(T.MM[:, lo:hi], T.TM[:, lo:hi], 256.0, A.is_ge, [("TM", lo, hi)], [("MM", lo, hi)], -256.0, A.mult)
        send(t, h, ["TM", "MM"])

    def firsts(t):
        top = 2048 + 512 * t
        l0 = ("fl", 0, 16)
        if t < 2:
            act(T.depB[:, :], T.pb4[:, 0:256], [("pb4",)], [("depB",)], scale=64.0)
        gather("S", T.K5[:, :], ("K5",), T.Kt[:, 0:top], ("Kt", 0, top), T.fl[:, 0:16], l0)
        u = 1024 * t
        if 0 not in R_ON_S[t]:
            gather("S", T.Rg[:, u:u + 256], ("Rg", u, u + 256), T.Rt[:, 0:top], ("Rt", 0, top), T.fl[:, 0:16], l0)
        pe("pb4", [(T.pb4[:, 0:256], T.BDs[:, :], T.K5[:, :])], [("K5",), ("BDs",)])
        cp(T.fru[:, :], T.pb4[:, 0:256], [("pb4",)], [("fru",)])
        pe("pb5", [(T.pb5[:, 0:256], T.idN[:, :], T.thrR[:, :]), (T.pb5[:, 0:256], T.BDi[:, :], T.K5[:, :])],
           [("K5",), ("BDi",), ("idN",), ("thrR",)], last=False)
        for c in range(16):
            n = 256 - 16 * c
            e = ("E", 256 * c, 256 * c + n)
            ts(T.E[:, 256 * c:256 * c + n], T.fru[:, 16 * c:256], T.pb0[:, 192 + c:193 + c], A.is_equal, [("fru",), ("pb0",), ("w16",)],
               [e], T.w16[:, c:c + 1], A.mult)
            pe("pb5", [(T.pb5[:, 16 * c:256], T.BD[:, :], T.E[:, 256 * c:256 * c + n])], [e, ("BD",)], False, c == 15)
        if Q_ON_S:
            act(T.qB[:, :], T.pb5[:, 0:256], [("pb5",)], [("qB",)], func=AF.Sign)
        else:
            ts(T.qB[:, :], T.pb5[:, 0:256], 0.0, A.is_ge, [("pb5",)], [("qB",)], 2.0, A.mult)

    def lists(t):
        if t < 2:
            o = T[LB][:, 320:336]
            pe(LB, [(o, T.idB[:, :], T.laneB[:, :])] + direct(o, 16, T.Q01, T.depB, 0), [("depB",), ("Q01",), ("idB",), ("laneB",)])
            cp(T.depU[:, :], o, [(LB,)], [("depU",)])
            gather("S", T.xf[:, :], ("xf",), T[XP[t]][:, 0:NXP], (XP[t], 0, NXP), T.depU[:, :], ("depU",))
        o = T[LB][:, 300:316]
        pe(LB, to_list(0, o, 16), [("Fz", 0, 1), ("RQ",)], last=False)
        pe(LB, direct(o, 16, T.Q256, T.qB, 0), [("qB",), ("Q256",)], first=False)
        tt(T.fo[:, :], o, T.dumpL[:, :], A.min, [(LB,), ("dumpL",)], [("fo",)])
        ts(T.offU[:, :], T.fo[:, :], OFF + 4096.0 * Q_ON_S, A.add, [("fo",)], [("offU",)])

    def vterms(o, ident, t):
        m = 1024 * t
        return [(o, T[ident][:, :], T.TM[:, m:m + 256]), (o, T[ident][:, :], T.MM[:, m:m + 256])], [("TM", m, m + 256), ("MM", m, m + 256), (ident,)]

    def splits(t):
        u = 256 * t
        rg, rgr, win, winr = T.Rg[:, 4 * u:4 * u + 256], ("Rg", 4 * u, 4 * u + 256), T.winB[:, u:u + 256], ("winB", u, u + 256)
        d = T.pb4[:, 256:512]
        lo, one, old = ("Dlo", "Done", "idMn") if t < 2 else ("Dhi", "D2", "MbN")
        new = [(d, T.Dhi[:, :], T.NDhi[:, u:u + 256]), (d, T[lo][:, :], T.NDlo[:, :]), (d, T[one][:, :], T.ones[:, :]), (d, T[old][:, :], T.K5[:, :])]
        newr = [("Dhi",), ("NDhi",), (lo,), ("NDlo",), (one,), ("ones",), (old,), ("K5",)]
        if t < 2:
            pe("pb4", new, newr)
            cp(T.Zt[:, :].indirect(T.offU[:, :]), T.xf[:, :], [("xf",), ("offU",)], [("Zt",)], n=256, ind=SCA)
        else:
            pe("pb4", [(T.pb4[:, 0:256], T.Mb[:, :], T.K5[:, :])], [("K5",), ("Mb",)])
            act(T.old32[:, :], T.pb4[:, 0:256], [("pb4",)], [("old32",)])
            pe("pb4", new, newr)
        o = T.pb6[:, 256:512]
        terms, rd = vterms(o, "idN", t)
        pe("pb6", [(o, T.idB[:, :], rg), terms[0]], [rd[0], rd[2], rgr, ("idB",)], last=False)
        pe("pb6", terms[1:], rd[1:], first=False)
        act(T.aB[:, :], o, [("pb6",)], [("aB",)], func=AF.Abs)
        o = T.pb5[:, 256:512]
        pe("pb5", [(o, T.idM[:, :], T.qB[:, :])], [("qB",), ("idM",)], last=False)
        pe("pb5", [(o, T.BD[:, :], T.aB[:, :])], [("aB",), ("BD",)], first=False)
        ts(win, o, thc, A.is_ge, [("pb5",), thr], [winr])
        if t < 2:
            tt(T.tK[:, :], d, win, A.mult, [("pb4",), winr], [("tK",)])
            tt(T.Kt[:, :].indirect(T.offU[:, :]), T.K5[:, :], T.tK[:, :], A.add, [("K5",), ("tK",), ("offU",)], [("Kt",)], ind=SCA)
        else:
            tt(T.tK32[:, :], d, win, A.mult, [("pb4",), winr], [("tK32",)])
            tt(T.Ko[:, :].indirect(T.offU[:, :]), T.old32[:, :], T.tK32[:, :], A.add, [("old32",), ("tK32",), ("offU",)], [("Ko",)], ind=SCA)

    def new_r(t):
        u, n = 256 * t, 2048 + 512 * t
        rg, rgr, win, winr = T.Rg[:, 4 * u:4 * u + 256], ("Rg", 4 * u, 4 * u + 256), T.winB[:, u:u + 256], ("winB", u, u + 256)
        o = T.pb7[:, 0:256]
        pe("pb7", [(o, T.idB[:, :], rg), (o, T.idW[:, :], win)], [rgr, winr, ("idB",), ("idW",)])
        act(T.Rt[:, n:n + 512:2], o, [("pb7",)], [("Rt", n, n + 512, "even")], func=AF.Relu, bias=-1024.0)
        o = T.pb6[:, 0:256]
        terms, rd = vterms(o, "idB", t)
        terms = [(o, T.idH[:, :], T.ones[:, :]), (o, T.idB[:, :], rg)] + terms + [(o, T.idW[:, :], win)]
        pe("pb6", terms, rd + [rgr, winr, ("idW",), ("idH",), ("ones",)])
        act(T.avF[:, :], o, [("pb6",)], [("avF",)], scale=0.5, bias=WHOLE - 512)
        act(T.Rt[:, n + 1:n + 512:2], T.avF[:, :], [("avF",)], [("Rt", n, n + 512, "odd")], func=AF.Relu, bias=-WHOLE)
        me = dma("D", T.yr[:, 512 * t:512 * t + 512], T.Rt[:, n:n + 512], 512 * MB, [("Rt", n, n + 512)], [])
        if t == 2:
            lead.append(me)

    H = range(len(PARTS))
    for t in range(3):
        if t == 0:
            for k in range(5):
                for h in H:
                    paths(0, h, k)
                pred(k, 1024 if k < 4 else 256)
            env_table()
            cp(T.wS[:, :], T.wI[:, :], [("wI",)], [("wS",)])
            remote("aw", src, dst, [([(T.wS[:, :], ("wS",))], (T.wN[:, :], ("wN",)))], 45.0)
            ts(T.QN[:, :], T.Q01[:, :], T.wN[:, :], A.mult, [("Q01",), ("wN",)], [("QN",)])
        for h in H:
            if t - 1 not in SUMS_SENT:
                tagged((t, h), hsum, t, h)
        if t > 0:
            for k in range(1, 5):
                for h in H:
                    tagged((t, h), paths, t, h, k)
        if t < 2:
            xg("S", t, 5, 0, 256)
        for k in range(5):
            for h in H:
                tagged((t, h), step, t, h, k)
        if t == 0:
            new_nodes()
        if t == 1:
            late_constants()
            for h in range(2):
                gather("S", T.Cg[:, 512 * h:512 * h + 512], ("Cg", 512 * h, 512 * h + 512), T.Ct[:, :], ("Ct",), T.hl[:, 32 * h:32 * h + 32],
                       ("hl", 32 * h, 32 * h + 32))
            dma("D", T.yp[:, 0:1024], T.Cg[0:128:16, :], 32768, [("Cg",)], [])
        if t == 2:
            ts(T.hF[:, :], T.hl[:, 64:128], 4096.0, A.add, [("hl", 64, 128)], [("hF",)])
            turn(T.hF[:, :], ("hF",), "hT", lambda e, a: T.yp[e:8:2, a:a + 512], None, 1024)
            for i, nm in enumerate(("QK0", "QK1")):
                bk, kb = "pb%d" % (6 + i), ("kB", 224 * i, 224 * i + 224)
                pe(bk, block(T[bk][:, 0:224], 224, T[nm], T.Kt), [("Kt", 0, 3584), (nm,)])
                act(T.kB[:, 224 * i:224 * i + 224], T[bk][:, 0:224], [(bk,)], [kb])
                dma("D", T.Ko[2 * i:128:16, 0:3584], T.kB[:, 224 * i:224 * i + 224], 114688, [kb], [("Ko", 0, 3840, "r%d" % i)])
        tagged((t, "s"), firsts, t)
        tagged((t, "o", 0), outcome, t, 0)
        tagged((t, "s"), lists, t)
        tagged((t, "s"), splits, t)
        for h in H[1:]:
            tagged((t, "o", h), outcome, t, h)
        new_r(t)
    lead.append(dma("D", T.yk0[:, :], T.Ko[0:128:16, 0:3584], 114688, [("Ko",)], []))
    lead.append(dma("S", T.yk1[:, :], T.Ko[2:128:16, 0:3584], 114688, [("Ko",)], []))
    o = T.pb7[:, 384:448]
    todo = [(nm, r) for r in range(16) for h in H if 0 <= 64 * r - PARTS[h][0] < PARTS[h][1] for nm in made[2, h]]
    todo.sort(key=lambda x: (x[1] // 4, x[0] != "TM"))
    for j in range(0, len(todo), 4):
        pe("pb7", [(o, T.QN[:, 15 - r:143 - r], T[nm][:, 2048 + 64 * r:2112 + 64 * r]) for nm, r in todo[j:j + 4]],
           [(nm, 2048 + 64 * r, 2112 + 64 * r) for nm, r in todo[j:j + 4]] + [("QN",)], j == 0, j + 4 >= len(todo))
    cp(T.yI[:, :], o, [("pb7",)], [("yI",)])
    ts(T.yJ[:, :], T.yI[:, :], 1023, A.bitwise_and, [("yI",)], [("yJ",)])
    ts(T.ypS[:, :], T.yJ[:, :], 5120.0, A.add, [("yJ",)], [("ypS",)])
    remote("ay", dst, src, [([(T.ypS[:, :], ("ypS",))], (T.ypF[:, :], ("ypF",)))], SMALL)
    dma("D", T.yp[:, 2048:3072], T.ypF[:, :], 32768, [("ypF",)], [])
    emit()
